import numpy as np
import ml_dtypes


def mxq(x, axis, fmt="e4m3"):
    dtype, down = {"e4m3": (ml_dtypes.float8_e4m3fn, 7), "e5m2": (ml_dtypes.float8_e5m2, 14)}[fmt]
    v = np.moveaxis(np.asarray(x, np.float32).astype(ml_dtypes.bfloat16).astype(np.float64), axis, -1)
    blocks = v.reshape(v.shape[:-1] + (-1, 32))
    amax = np.abs(blocks).max(-1, keepdims=True)
    byte = np.maximum(np.where(amax > 0, np.frexp(amax)[1] - 1 + 127, 0) - down, 1)
    scale = np.exp2(byte - 127.0)
    codes = (blocks / scale).astype(np.float32).astype(dtype).astype(np.float64)
    return np.moveaxis((codes * scale).reshape(v.shape), -1, axis)


WIDE = False


def mx_kscale(k):
    if not WIDE:
        return np.ones(k)
    levels = np.array([10, -10, 5, -5, 0])
    if k % 512:
        return np.exp2(np.random.permutation(np.resize(levels, k // 32))).repeat(32)
    a = np.empty((k // 512, 16))
    for p in range(k // 512):
        a[p, :8] = np.random.permutation(np.resize(levels, 8))
        for g in range(8):
            far = levels[np.abs(levels - a[p, g]) >= 10]
            a[p, g + 8] = far[np.random.randint(len(far))]
    return np.exp2(a.ravel()).repeat(32)


def f64(x):
    return np.asarray(x).astype(np.float64)


def striped(idx):
    return np.tile(idx.reshape(-1, 16).T, (8, 1)).astype(np.uint16)


def unstriped(offs):
    return offs[:16].T.reshape(-1).astype(np.int64)


E2M1 = np.array([0.0, 0.5, 1.0, 1.5, 2.0, 3.0, 4.0, 6.0, -0.0, -0.5, -1.0, -1.5, -2.0, -3.0, -4.0, -6.0])


def pack_weight(w, fmt):
    k, n = w.shape
    w = f64(np.asarray(w, np.float32).astype(ml_dtypes.bfloat16)).reshape(k // 32, 32, n)
    amax = np.abs(w).max(1)
    if fmt == "e4m3":
        byte = np.frexp(amax)[1] - 1 + 127 - 7
    else:
        mant, ex = np.frexp(amax / 6.0)
        byte = np.where(mant > 0.5, ex, ex - 1) + 127
    byte = np.clip(np.where(amax > 0, byte, 1), 1, 254)
    scaled = (w * np.exp2(127.0 - byte)[:, None, :]).reshape(k, n).astype(np.float32)
    by_word = np.ascontiguousarray(scaled.reshape(k // 512, 128, 4, n).transpose(0, 1, 3, 2))
    if fmt == "e4m3":
        words = by_word.astype(ml_dtypes.float8_e4m3fn).view(np.uint8)
    else:
        c = by_word.astype(ml_dtypes.float4_e2m1fn).view(np.uint8) & 0xF
        words = (c[..., 0::2] | (c[..., 1::2] << 4)).reshape(k // 512, 128, 2 * n)
    return np.ascontiguousarray(words), np.ascontiguousarray(byte.astype(np.uint8).reshape(k // 512, 16, n))


def unpack_weight(words, scales, fmt):
    g, _, n = scales.shape
    words = np.ascontiguousarray(words).reshape(g, 128, n, -1)
    if fmt == "e4m3":
        vals = words.view(ml_dtypes.float8_e4m3fn).astype(np.float64)
    else:
        nib = np.empty((g, 128, n, 4), np.uint8)
        nib[..., 0::2] = words & 0xF
        nib[..., 1::2] = words >> 4
        vals = E2M1[nib]
    vals = vals * np.repeat(np.exp2(scales.astype(np.float64) - 127.0), 8, axis=1)[..., None]
    return vals.transpose(0, 1, 3, 2).reshape(g * 512, n)


def gelu(v):
    return 0.5 * v * (1.0 + np.tanh(np.sqrt(2.0 / np.pi) * (v + 0.044715 * v**3)))


K, H, T, S, P = 1024, 1024, 2048, 1024, 512

def setup_inputs():
    n = np.random.standard_normal
    s = mx_kscale(K)[:, None]
    u = mx_kscale(H)[:, None]
    tab_words, tab_scales = pack_weight(n((K, T)) * s, "e4m3")
    w1_words, w1_scales = pack_weight(n((K, H)) / np.sqrt(K) / s, "e2m1")
    return {
        "tab_words": tab_words, "tab_scales": tab_scales,
        "offs": striped(np.random.permutation(T)[:S]),
        "pos1": striped(np.random.permutation(S)[:P]),
        "pos2": striped(np.random.permutation(S)[:P]),
        "w1_words": w1_words, "w1_scales": w1_scales,
        "gain": (np.exp(0.3 * n(H)) * u[:, 0]).astype(np.float32),
        "w2": (n((H, H)) / np.sqrt(H) / u).astype(np.float32),
        "step": np.exp(0.3 * n(H)).astype(np.float32),
    }

def reference(tab_words, tab_scales, offs, pos1, pos2, w1_words, w1_scales, gain, w2, step):
    v = unpack_weight(tab_words, tab_scales, "e4m3")[:, unstriped(offs)]
    w1 = unpack_weight(w1_words, w1_scales, "e2m1")
    h = w1.T @ v
    x = np.tanh(h[:, unstriped(pos1)]) * f64(gain)[:, None]
    x = mxq(x, 0, "e4m3")
    y = mxq(f64(w2), 0, "e4m3").T @ x
    d = h[:, unstriped(pos2)]
    rate = np.tanh(d + y)
    return d + f64(step)[:, None] * rate

@@ -1,0 +1,262 @@
+from contextlib import ExitStack
+
+import concourse.mybir as mybir
+from concourse.masks import make_identity
+
+F32 = mybir.dt.float32
+BF16 = mybir.dt.bfloat16
+I32 = mybir.dt.int32
+U32 = mybir.dt.uint32
+U16 = mybir.dt.uint16
+U8 = mybir.dt.uint8
+FP8X4 = mybir.dt.float8_e4m3fn_x4
+FP4X4 = mybir.dt.float4_e2m1fn_x4
+ACT = mybir.ActivationFunctionType
+ALU = mybir.AluOpType
+
+K, H, T, S, M = 1024, 1024, 2048, 1024, 512
+P = 128
+SLOTS = 4
+PASSES = 2
+BANK = 512
+SC_ROW = 24
+VEC_ROW = 120
+LATE = 5
+FLOPS = 2 * K * H * S + 2 * H * H * M
+
+
+def tile_list_creek_half_step_kernel(
+    tc, tab_words, tab_scales, offs, pos1, pos2, w1_words, w1_scales, gain, w2, step, out
+):
+    nc = tc.nc
+    with ExitStack() as ctx:
+        lists = ctx.enter_context(tc.tile_pool(name="lists", bufs=1))
+        keep = ctx.enter_context(tc.tile_pool(name="keep", bufs=1))
+        ring = ctx.enter_context(tc.tile_pool(name="ring", bufs=3))
+        psum = ctx.enter_context(tc.psum_pool(name="psum", bufs=8))
+
+        offs_sb = lists.tile([P, S // 16], U16, name="offs_sb")
+        pos1_sb = lists.tile([P, M // 16], U16, name="pos1_sb")
+        pos2_sb = lists.tile([P, M // 16], U16, name="pos2_sb")
+
+        tab_sc = keep.tile([P, T], U8, name="tab_sc", tag="slot0")
+        tab_w = [keep.tile([P, T], U32, name="tab_w%d" % a, tag="slot%d" % (1 + a)) for a in range(PASSES)]
+        w1_raw = keep.tile([P, PASSES * H // 2], I32, name="w1_raw", tag="slot3")
+        w1_sc_raw = keep.tile([P, PASSES * H], U8, name="w1_sc_raw", align_bytes=64)
+        v_sc_raw = keep.tile([P, S], U8, name="v_sc_raw", align_bytes=64)
+        v_sc = keep.tile([P, PASSES * S], U8, name="v_sc", align_bytes=64)
+        vec = keep.tile([P, 2 * P], F32, name="vec")
+        ident = keep.tile([P, P], F32, name="ident")
+
+        for q in range(4):
+            nc.vector.memset(tab_sc[32 * q : 32 * q + SC_ROW, :].bitcast(I32), 0)
+        nc.vector.memset(w1_sc_raw[:].bitcast(I32), 0)
+        nc.vector.memset(v_sc[96:P, :].bitcast(I32), 0)
+        nc.gpsimd.memset(vec[0:VEC_ROW, :], 0.0)
+        make_identity(nc, ident[:])
+
+        nc.sync.dma_start(offs_sb[:], offs)
+        tab_sc_i32 = tab_scales.bitcast(I32)
+        for q in range(4):
+            nc.sync.dma_start(
+                out=tab_sc[32 * q + SC_ROW : 32 * (q + 1), :].bitcast(I32), in_=tab_sc_i32[:, 4 * q : 4 * q + 4, :]
+            )
+
+        def load_table_words(a):
+            nc.sync.dma_start(
+                out=tab_w[a][:].bitcast(I32), in_=tab_words[a].rearrange("p t i -> p (t i)").bitcast(I32)
+            )
+
+        load_table_words(0)
+        for row, vector in ((VEC_ROW, gain), (VEC_ROW + SLOTS, step)):
+            nc.sync.dma_start(
+                out=vec[row : row + SLOTS, :].rearrange("t (c j) -> t c j", j=8),
+                in_=vector.rearrange("(c t j) -> t c j", t=SLOTS, j=8),
+            )
+        nc.sync.dma_start(pos1_sb[:], pos1)
+        nc.sync.dma_start(pos2_sb[:], pos2)
+        load_table_words(1)
+        nc.sync.dma_start(
+            out=w1_raw[:].rearrange("p (a c) -> p a c", a=PASSES),
+            in_=w1_words.bitcast(I32).rearrange("a p c -> p a c"),
+        )
+        w1_sc_i32 = w1_scales.bitcast(I32)
+        for q in range(4):
+            nc.sync.dma_start(
+                out=w1_sc_raw[32 * q : 32 * q + 4, :].bitcast(I32).rearrange("r (a c) -> r a c", a=PASSES),
+                in_=w1_sc_i32[:, 4 * q : 4 * q + 4, :].rearrange("a r c -> r a c"),
+            )
+
+        w2_raw = {}
+
+        def load_w2(a, b, slot):
+            raw = keep.tile([P, SLOTS, BANK], F32, name="w2_raw%d%d" % (a, b), tag=slot)
+            rows = w2[BANK * a : BANK * (a + 1), BANK * b : BANK * (b + 1)].rearrange(
+                "(g t j) n -> t g j n", t=SLOTS, j=8
+            )
+            for t in range(SLOTS):
+                nc.sync.dma_start(out=raw[:, t, :], in_=rows[t])
+            w2_raw[a, b] = raw
+
+        nc.vector.tensor_copy(v_sc_raw[:], tab_sc[:].indirect(offs_sb[:]))
+        for a in range(PASSES):
+            first = SC_ROW + 4 * a
+            nc.scalar.dma_start(
+                out=v_sc[0 : P - first, S * a : S * (a + 1)].bitcast(I32), in_=v_sc_raw[first:P, :].bitcast(I32)
+            )
+        load_w2(0, 0, "slot0")
+        v_w = {}
+        half_cols = BANK // 16
+
+        def gather_words(a, c):
+            v_w[a, c] = keep.tile([P, BANK], U32, name="v_w%d%d" % (a, c), align_bytes=64)
+            nc.vector.tensor_copy(
+                v_w[a, c][:], tab_w[a][:].indirect(offs_sb[:, half_cols * c : half_cols * (c + 1)])
+            )
+
+        gather_words(0, 0)
+        gather_words(0, 1)
+        load_w2(0, 1, "slot1")
+        gather_words(1, 0)
+
+        w1_c = keep.tile([P, PASSES * H * 2], U8, name="w1_c", align_bytes=64)
+        nc.vector.tensor_copy(
+            out=w1_c[:].bitcast(I32).rearrange("p (s t g w) -> p s t g w", t=SLOTS, g=16, w=4),
+            in_=w1_raw[:].rearrange("p (s g t w) -> p s t g w", t=SLOTS, g=16, w=4),
+        )
+        w1_sc = keep.tile([P, PASSES * H], U8, name="w1_sc", align_bytes=64)
+        nc.vector.tensor_copy(
+            out=w1_sc[:].bitcast(I32).rearrange("p (s t g w) -> p s t g w", t=SLOTS, g=16, w=2),
+            in_=w1_sc_raw[:].bitcast(I32).rearrange("p (s g t w) -> p s t g w", t=SLOTS, g=16, w=2),
+        )
+        load_w2(1, 0, "slot3")
+        gather_words(1, 1)
+        load_w2(1, 1, "slot2")
+
+        vec_ps = psum.tile([P, PASSES, P], F32, name="vec_ps", tag="bank")
+        for b in range(PASSES):
+            nc.tensor.transpose(vec_ps[:, b, :], vec[:, P * b : P * (b + 1)], ident[:])
+        vec_t = keep.tile([P, PASSES, 2 * SLOTS], F32, name="vec_t")
+        nc.scalar.activation(vec_t[:], vec_ps[:, :, VEC_ROW:P], ACT.Copy)
+
+        w2_c = [keep.tile([P, H], U32, name="w2_c%d" % a, align_bytes=64) for a in range(PASSES)]
+        w2_sc = [keep.tile([P, H], U8, name="w2_sc%d" % a, align_bytes=64) for a in range(PASSES)]
+        w2_bf = {}
+
+        def cast_w2(a, b, u):
+            if u == 0:
+                w2_bf[a, b] = keep.tile([P, SLOTS * BANK], BF16, name="w2_bf%d%d" % (a, b), align_bytes=64)
+            dst = w2_bf[a, b][:, BANK * u : BANK * (u + 1)].rearrange("p (g h i t) -> p g h t i", h=2, i=4, t=SLOTS)
+            src = w2_raw[a, b][:].rearrange("p t (g u h i) -> p u g h t i", u=SLOTS, h=2, i=4)[:, u]
+            nc.scalar.copy(out=dst, in_=src)
+
+        def quantize_w2(a, b):
+            nc.vector.quantize_mx(
+                out=w2_c[a][:, BANK * b : BANK * (b + 1)].bitcast(FP8X4),
+                scales=w2_sc[a][:, BANK * b : BANK * (b + 1)],
+                in_=w2_bf[a, b][:],
+            )
+
+        h = []
+        picked = [keep.tile([P, SLOTS, M], F32, name="picked%d" % b) for b in range(PASSES)]
+        x_c = [keep.tile([P, M], U32, name="x_c%d" % b, align_bytes=64) for b in range(PASSES)]
+        x_sc = [keep.tile([P, M], U8, name="x_sc%d" % b, align_bytes=64) for b in range(PASSES)]
+
+        def stage1(i):
+            rows = keep.tile([P, S], F32, name="h%d" % i)
+            for c in range(2):
+                acc = psum.tile([P, BANK], F32, name="acc", tag="bank")
+                for a in range(PASSES):
+                    col = H * a + P * i
+                    nc.tensor.matmul_mx(
+                        out=acc[:],
+                        lhsT=w1_c[:, 2 * col : 2 * (col + P)].bitcast(FP4X4),
+                        lhsT_scale=w1_sc[:, col : col + P],
+                        rhs=v_w[a, c][:].bitcast(FP8X4),
+                        rhs_scale=v_sc[:, S * a + BANK * c : S * a + BANK * (c + 1)],
+                        start=(a == 0),
+                        stop=(a == PASSES - 1),
+                    )
+                nc.scalar.copy(out=rows[:, BANK * c : BANK * (c + 1)], in_=acc[:])
+            h.append(rows)
+
+        HALF = M // 2
+
+        def make_x(b, c):
+            cols = slice(HALF * c, HALF * (c + 1))
+            bounded = ring.tile([P, HALF * SLOTS], F32, name="bounded")
+            nc.scalar.activation(
+                bounded[:].rearrange("p (c i t) -> p c t i", i=4, t=SLOTS),
+                picked[b][:, :, cols].rearrange("p t (c i) -> p c t i", i=4),
+                ACT.Tanh,
+            )
+            x_bf = ring.tile([P, HALF * SLOTS], BF16, name="x_bf", align_bytes=64)
+            nc.vector.tensor_tensor(
+                x_bf[:].rearrange("p (m t) -> p m t", t=SLOTS),
+                bounded[:].rearrange("p (m t) -> p m t", t=SLOTS),
+                vec_t[:, b, 0:SLOTS].unsqueeze(1).to_broadcast([P, HALF, SLOTS]),
+                ALU.mult,
+            )
+            return x_bf
+
+        def quantize_x(b, c, x_bf):
+            cols = slice(HALF * c, HALF * (c + 1))
+            nc.vector.quantize_mx(out=x_c[b][:, cols].bitcast(FP8X4), scales=x_sc[b][:, cols], in_=x_bf[:])
+
+        units = [(a, b, u) for a in range(PASSES) for b in range(PASSES) for u in range(SLOTS)]
+        for i in range(PASSES * SLOTS):
+            b, t = divmod(i, SLOTS)
+            stage1(i)
+            nc.vector.tensor_copy(picked[b][:, t, :], h[i][:].indirect(pos1_sb[:]))
+            for a, bb, u in units[2 * i : 2 * i + 2]:
+                cast_w2(a, bb, u)
+                if u == SLOTS - 1:
+                    quantize_w2(a, bb)
+            if t == SLOTS - 1:
+                halves = [make_x(b, c) for c in range(2)]
+                for c in range(2):
+                    quantize_x(b, c, halves[c])
+
+        down = []
+        late = keep.tile([P, PASSES * SLOTS - LATE, M], F32, name="late", tag="slot2")
+        for i in range(PASSES * SLOTS):
+            if i < LATE:
+                d = keep.tile([P, M], F32, name="down%d" % i)[:]
+            else:
+                d = late[:, i - LATE, :]
+            nc.vector.tensor_copy(d, h[i][:].indirect(pos2_sb[:]))
+            down.append(d)
+
+        y = [psum.tile([P, M], F32, name="y%d" % i, tag="bank") for i in range(PASSES * SLOTS)]
+        for a in range(PASSES):
+            for i in range(PASSES * SLOTS):
+                nc.tensor.matmul_mx(
+                    out=y[i][:],
+                    lhsT=w2_c[a][:, P * i : P * (i + 1)].bitcast(FP8X4),
+                    lhsT_scale=w2_sc[a][:, P * i : P * (i + 1)],
+                    rhs=x_c[a][:].bitcast(FP8X4),
+                    rhs_scale=x_sc[a][:],
+                    start=(a == 0),
+                    stop=(a == PASSES - 1),
+                )
+
+        out_rows = out.rearrange("(b g t j) m -> b t g j m", b=PASSES, t=SLOTS, j=8)
+        rates = []
+
+        def finish(i):
+            b, t = divmod(i, SLOTS)
+            res = keep.tile([P, M], F32, name="res%d" % i)
+            nc.vector.scalar_tensor_tensor(
+                res[:], rates[i][:], vec_t[:, b, SLOTS + t : SLOTS + t + 1], down[i], ALU.mult, ALU.add
+            )
+            nc.sync.dma_start(out=out_rows[b, t], in_=res[:])
+
+        for i in range(PASSES * SLOTS):
+            moved = ring.tile([P, M], F32, name="moved")
+            nc.vector.tensor_tensor(moved[:], y[i][:], down[i], ALU.add)
+            rate = ring.tile([P, M], F32, name="rate")
+            nc.scalar.activation(rate[:], moved[:], ACT.Tanh)
+            rates.append(rate)
+            if i > 0:
+                finish(i - 1)
+        finish(PASSES * SLOTS - 1)

@@ -19,9 +19,12 @@ P = 128
 SLOTS = 4
 PASSES = 2
 BANK = 512
-SC_ROW = 24
+SC_ROW = 96
+W1_WORDS = PASSES * H // 2
+W1_SCALES = PASSES * H // 4
 VEC_ROW = 120
 LATE = 5
+ON_GPSIMD = (0, 2, 4)
 FLOPS = 2 * K * H * S + 2 * H * H * M
 
 
@@ -39,28 +42,30 @@ def tile_list_creek_half_step_kernel(
         pos1_sb = lists.tile([P, M // 16], U16, name="pos1_sb")
         pos2_sb = lists.tile([P, M // 16], U16, name="pos2_sb")
 
-        tab_sc = keep.tile([P, T], U8, name="tab_sc", tag="slot0")
-        tab_w = [keep.tile([P, T], U32, name="tab_w%d" % a, tag="slot%d" % (1 + a)) for a in range(PASSES)]
-        w1_raw = keep.tile([P, PASSES * H // 2], I32, name="w1_raw", tag="slot3")
-        w1_sc_raw = keep.tile([P, PASSES * H], U8, name="w1_sc_raw", align_bytes=64)
-        v_sc_raw = keep.tile([P, S], U8, name="v_sc_raw", align_bytes=64)
+        tab_sc = keep.tile([P, T], U8, name="tab_sc", tag="slot0", align_bytes=64)
+        tab_w = [keep.tile([P, T], U32, name="tab_w%d" % a, tag="slot%d" % (1 + a), align_bytes=64) for a in range(PASSES)]
+        w1_sc_raw = keep.tile([P, W1_SCALES], I32, name="w1_sc_raw")
+        v_sc_raw = keep.tile([P, S], U8, name="v_sc_raw")
         v_sc = keep.tile([P, PASSES * S], U8, name="v_sc", align_bytes=64)
         vec = keep.tile([P, 2 * P], F32, name="vec")
         ident = keep.tile([P, P], F32, name="ident")
 
+        nc.vector.memset(tab_sc[0:SC_ROW, :].bitcast(I32), 0)
+        nc.vector.memset(w1_sc_raw[:], 0)
+        nc.vector.memset(v_sc[:].bitcast(I32), 0)
+        w1_sc_i32 = w1_scales.bitcast(I32)
         for q in range(4):
-            nc.vector.memset(tab_sc[32 * q : 32 * q + SC_ROW, :].bitcast(I32), 0)
-        nc.vector.memset(w1_sc_raw[:].bitcast(I32), 0)
-        nc.vector.memset(v_sc[96:P, :].bitcast(I32), 0)
+            nc.scalar.dma_start(
+                out=w1_sc_raw[32 * q : 32 * q + 4, :].rearrange("r (a c) -> r a c", a=PASSES),
+                in_=w1_sc_i32[:, 4 * q : 4 * q + 4, :].rearrange("a r c -> r a c"),
+            )
         nc.gpsimd.memset(vec[0:VEC_ROW, :], 0.0)
         make_identity(nc, ident[:])
 
         nc.sync.dma_start(offs_sb[:], offs)
-        tab_sc_i32 = tab_scales.bitcast(I32)
-        for q in range(4):
-            nc.sync.dma_start(
-                out=tab_sc[32 * q + SC_ROW : 32 * (q + 1), :].bitcast(I32), in_=tab_sc_i32[:, 4 * q : 4 * q + 4, :]
-            )
+        nc.sync.dma_start(
+            out=tab_sc[SC_ROW:P, :].bitcast(I32), in_=tab_scales.bitcast(I32).rearrange("a q c -> q a c")
+        )
 
         def load_table_words(a):
             nc.sync.dma_start(
@@ -76,21 +81,10 @@ def tile_list_creek_half_step_kernel(
         nc.sync.dma_start(pos1_sb[:], pos1)
         nc.sync.dma_start(pos2_sb[:], pos2)
         load_table_words(1)
-        nc.sync.dma_start(
-            out=w1_raw[:].rearrange("p (a c) -> p a c", a=PASSES),
-            in_=w1_words.bitcast(I32).rearrange("a p c -> p a c"),
-        )
-        w1_sc_i32 = w1_scales.bitcast(I32)
-        for q in range(4):
-            nc.sync.dma_start(
-                out=w1_sc_raw[32 * q : 32 * q + 4, :].bitcast(I32).rearrange("r (a c) -> r a c", a=PASSES),
-                in_=w1_sc_i32[:, 4 * q : 4 * q + 4, :].rearrange("a r c -> r a c"),
-            )
 
         w2_raw = {}
 
-        def load_w2(a, b, slot):
-            raw = keep.tile([P, SLOTS, BANK], F32, name="w2_raw%d%d" % (a, b), tag=slot)
+        def load_w2(a, b, raw):
             rows = w2[BANK * a : BANK * (a + 1), BANK * b : BANK * (b + 1)].rearrange(
                 "(g t j) n -> t g j n", t=SLOTS, j=8
             )
@@ -99,39 +93,46 @@ def tile_list_creek_half_step_kernel(
             w2_raw[a, b] = raw
 
         nc.vector.tensor_copy(v_sc_raw[:], tab_sc[:].indirect(offs_sb[:]))
-        for a in range(PASSES):
-            first = SC_ROW + 4 * a
+        for q in range(4):
+            first = SC_ROW + 8 * q
             nc.scalar.dma_start(
-                out=v_sc[0 : P - first, S * a : S * (a + 1)].bitcast(I32), in_=v_sc_raw[first:P, :].bitcast(I32)
+                out=v_sc[32 * q : 32 * q + 4, :].bitcast(I32).rearrange("r (a c) -> r a c", a=PASSES),
+                in_=v_sc_raw[first : first + 8, :].bitcast(I32),
             )
-        load_w2(0, 0, "slot0")
+        w1_raw = keep.tile([P, W1_WORDS], I32, name="w1_raw", tag="slot0", align_bytes=64)
+        nc.sync.dma_start(
+            out=w1_raw[:].rearrange("p (a c) -> p a c", a=PASSES),
+            in_=w1_words.bitcast(I32).rearrange("a p c -> p a c"),
+        )
         v_w = {}
         half_cols = BANK // 16
 
         def gather_words(a, c):
-            v_w[a, c] = keep.tile([P, BANK], U32, name="v_w%d%d" % (a, c), align_bytes=64)
+            tag = "slot0" if (a, c) == (1, 1) else "v_w%d%d" % (a, c)
+            v_w[a, c] = keep.tile([P, BANK], U32, name="v_w%d%d" % (a, c), tag=tag, align_bytes=64)
             nc.vector.tensor_copy(
                 v_w[a, c][:], tab_w[a][:].indirect(offs_sb[:, half_cols * c : half_cols * (c + 1)])
             )
 
         gather_words(0, 0)
         gather_words(0, 1)
-        load_w2(0, 1, "slot1")
+        w2_in = keep.tile([P, PASSES * PASSES, SLOTS, BANK], F32, name="w2_in", tag="slot1", align_bytes=64)
+        for a in range(PASSES):
+            for b in range(PASSES):
+                load_w2(a, b, w2_in[:, PASSES * a + b])
         gather_words(1, 0)
 
+        w1_sc = keep.tile([P, PASSES * H], U8, name="w1_sc", align_bytes=64)
+        nc.vector.tensor_copy(
+            out=w1_sc[:].bitcast(I32).rearrange("p (s t g w) -> p s t g w", t=SLOTS, g=16, w=2),
+            in_=w1_sc_raw[:].rearrange("p (s g t w) -> p s t g w", t=SLOTS, g=16, w=2),
+        )
         w1_c = keep.tile([P, PASSES * H * 2], U8, name="w1_c", align_bytes=64)
         nc.vector.tensor_copy(
             out=w1_c[:].bitcast(I32).rearrange("p (s t g w) -> p s t g w", t=SLOTS, g=16, w=4),
             in_=w1_raw[:].rearrange("p (s g t w) -> p s t g w", t=SLOTS, g=16, w=4),
         )
-        w1_sc = keep.tile([P, PASSES * H], U8, name="w1_sc", align_bytes=64)
-        nc.vector.tensor_copy(
-            out=w1_sc[:].bitcast(I32).rearrange("p (s t g w) -> p s t g w", t=SLOTS, g=16, w=2),
-            in_=w1_sc_raw[:].bitcast(I32).rearrange("p (s g t w) -> p s t g w", t=SLOTS, g=16, w=2),
-        )
-        load_w2(1, 0, "slot3")
         gather_words(1, 1)
-        load_w2(1, 1, "slot2")
 
         vec_ps = psum.tile([P, PASSES, P], F32, name="vec_ps", tag="bank")
         for b in range(PASSES):
@@ -145,10 +146,14 @@ def tile_list_creek_half_step_kernel(
 
         def cast_w2(a, b, u):
             if u == 0:
-                w2_bf[a, b] = keep.tile([P, SLOTS * BANK], BF16, name="w2_bf%d%d" % (a, b), align_bytes=64)
+                tag = "slot2" if (a, b) == (0, 0) else "w2_bf%d%d" % (a, b)
+                w2_bf[a, b] = keep.tile([P, SLOTS * BANK], BF16, name="w2_bf%d%d" % (a, b), tag=tag, align_bytes=64)
             dst = w2_bf[a, b][:, BANK * u : BANK * (u + 1)].rearrange("p (g h i t) -> p g h t i", h=2, i=4, t=SLOTS)
-            src = w2_raw[a, b][:].rearrange("p t (g u h i) -> p u g h t i", u=SLOTS, h=2, i=4)[:, u]
-            nc.scalar.copy(out=dst, in_=src)
+            src = w2_raw[a, b].rearrange("p t (g u h i) -> p u g h t i", u=SLOTS, h=2, i=4)[:, u]
+            if (a, b) == (0, 0):
+                nc.vector.tensor_copy(out=dst, in_=src)
+            else:
+                nc.scalar.copy(out=dst, in_=src)
 
         def quantize_w2(a, b):
             nc.vector.quantize_mx(
@@ -190,7 +195,7 @@ def tile_list_creek_half_step_kernel(
                 picked[b][:, :, cols].rearrange("p t (c i) -> p c t i", i=4),
                 ACT.Tanh,
             )
-            x_bf = ring.tile([P, HALF * SLOTS], BF16, name="x_bf", align_bytes=64)
+            x_bf = keep.tile([P, HALF * SLOTS], BF16, name="x_bf%d%d" % (b, c), align_bytes=64)
             nc.vector.tensor_tensor(
                 x_bf[:].rearrange("p (m t) -> p m t", t=SLOTS),
                 bounded[:].rearrange("p (m t) -> p m t", t=SLOTS),
@@ -204,11 +209,15 @@ def tile_list_creek_half_step_kernel(
             nc.vector.quantize_mx(out=x_c[b][:, cols].bitcast(FP8X4), scales=x_sc[b][:, cols], in_=x_bf[:])
 
         units = [(a, b, u) for a in range(PASSES) for b in range(PASSES) for u in range(SLOTS)]
+        for u in range(SLOTS):
+            cast_w2(0, 0, u)
+        quantize_w2(0, 0)
+        share = [4, 6, 8, 10, 10, 12, 14, 14, 16]
         for i in range(PASSES * SLOTS):
             b, t = divmod(i, SLOTS)
             stage1(i)
             nc.vector.tensor_copy(picked[b][:, t, :], h[i][:].indirect(pos1_sb[:]))
-            for a, bb, u in units[2 * i : 2 * i + 2]:
+            for a, bb, u in units[share[i] : share[i + 1]]:
                 cast_w2(a, bb, u)
                 if u == SLOTS - 1:
                     quantize_w2(a, bb)
@@ -218,12 +227,14 @@ def tile_list_creek_half_step_kernel(
                     quantize_x(b, c, halves[c])
 
         down = []
-        late = keep.tile([P, PASSES * SLOTS - LATE, M], F32, name="late", tag="slot2")
+        late = keep.tile([P, PASSES * SLOTS - 1 - LATE, M], F32, name="late", tag="slot1", align_bytes=64)
         for i in range(PASSES * SLOTS):
             if i < LATE:
                 d = keep.tile([P, M], F32, name="down%d" % i)[:]
-            else:
+            elif i < PASSES * SLOTS - 1:
                 d = late[:, i - LATE, :]
+            else:
+                d = keep.tile([P, M], F32, name="down_last", tag="x_bf11", align_bytes=64)[:]
             nc.vector.tensor_copy(d, h[i][:].indirect(pos2_sb[:]))
             down.append(d)
 
@@ -241,22 +252,31 @@ def tile_list_creek_half_step_kernel(
                 )
 
         out_rows = out.rearrange("(b g t j) m -> b t g j m", b=PASSES, t=SLOTS, j=8)
+        last = PASSES * SLOTS - 1
+        pieces = [(i, slice(0, M)) for i in range(last)] + [(last, slice(0, HALF)), (last, slice(HALF, M))]
         rates = []
 
-        def finish(i):
+        def finish(n):
+            i, cols = pieces[n]
             b, t = divmod(i, SLOTS)
-            res = keep.tile([P, M], F32, name="res%d" % i)
-            nc.vector.scalar_tensor_tensor(
-                res[:], rates[i][:], vec_t[:, b, SLOTS + t : SLOTS + t + 1], down[i], ALU.mult, ALU.add
-            )
-            nc.sync.dma_start(out=out_rows[b, t], in_=res[:])
+            width = cols.stop - cols.start
+            step_col = vec_t[:, b, SLOTS + t : SLOTS + t + 1]
+            res = keep.tile([P, width], F32, name="res%d" % n)
+            if i in ON_GPSIMD:
+                scaled = ring.tile([P, width], F32, name="scaled")
+                nc.scalar.activation(scaled[:], rates[n][:], ACT.Copy, scale=step_col)
+                nc.gpsimd.tensor_tensor(res[:], scaled[:], down[i][:, cols], ALU.add)
+            else:
+                nc.vector.scalar_tensor_tensor(res[:], rates[n][:], step_col, down[i][:, cols], ALU.mult, ALU.add)
+            nc.sync.dma_start(out=out_rows[b, t][:, :, cols], in_=res[:])
 
-        for i in range(PASSES * SLOTS):
-            moved = ring.tile([P, M], F32, name="moved")
-            nc.vector.tensor_tensor(moved[:], y[i][:], down[i], ALU.add)
-            rate = ring.tile([P, M], F32, name="rate")
+        for n, (i, cols) in enumerate(pieces):
+            width = cols.stop - cols.start
+            moved = ring.tile([P, width], F32, name="moved")
+            nc.vector.tensor_tensor(moved[:], y[i][:, cols], down[i][:, cols], ALU.add)
+            rate = ring.tile([P, width], F32, name="rate")
             nc.scalar.activation(rate[:], moved[:], ACT.Tanh)
             rates.append(rate)
-            if i > 0:
-                finish(i - 1)
-        finish(PASSES * SLOTS - 1)
+            if n > 0:
+                finish(n - 1)
+        finish(len(pieces) - 1)

@@ -1,7 +1,6 @@
 from contextlib import ExitStack
 
 import concourse.mybir as mybir
-from concourse.masks import make_identity
 
 F32 = mybir.dt.float32
 BF16 = mybir.dt.bfloat16
@@ -22,7 +21,6 @@ BANK = 512
 SC_ROW = 96
 W1_WORDS = PASSES * H // 2
 W1_SCALES = PASSES * H // 4
-VEC_ROW = 120
 LATE = 5
 ON_GPSIMD = (0, 2, 4)
 FLOPS = 2 * K * H * S + 2 * H * H * M
@@ -42,13 +40,13 @@ def tile_list_creek_half_step_kernel(
         pos1_sb = lists.tile([P, M // 16], U16, name="pos1_sb")
         pos2_sb = lists.tile([P, M // 16], U16, name="pos2_sb")
 
-        tab_sc = keep.tile([P, T], U8, name="tab_sc", tag="slot0", align_bytes=64)
+        tab_sc = keep.tile([P, T], U8, name="tab_sc")
         tab_w = [keep.tile([P, T], U32, name="tab_w%d" % a, tag="slot%d" % (1 + a), align_bytes=64) for a in range(PASSES)]
         w1_sc_raw = keep.tile([P, W1_SCALES], I32, name="w1_sc_raw")
         v_sc_raw = keep.tile([P, S], U8, name="v_sc_raw")
         v_sc = keep.tile([P, PASSES * S], U8, name="v_sc", align_bytes=64)
-        vec = keep.tile([P, 2 * P], F32, name="vec")
-        ident = keep.tile([P, P], F32, name="ident")
+        gain_sb = keep.tile([P, PASSES, SLOTS], F32, name="gain_sb")
+        step_sb = keep.tile([P, PASSES, SLOTS], F32, name="step_sb")
 
         nc.vector.memset(tab_sc[0:SC_ROW, :].bitcast(I32), 0)
         nc.vector.memset(w1_sc_raw[:], 0)
@@ -59,8 +57,6 @@ def tile_list_creek_half_step_kernel(
                 out=w1_sc_raw[32 * q : 32 * q + 4, :].rearrange("r (a c) -> r a c", a=PASSES),
                 in_=w1_sc_i32[:, 4 * q : 4 * q + 4, :].rearrange("a r c -> r a c"),
             )
-        nc.gpsimd.memset(vec[0:VEC_ROW, :], 0.0)
-        make_identity(nc, ident[:])
 
         nc.sync.dma_start(offs_sb[:], offs)
         nc.sync.dma_start(
@@ -73,23 +69,22 @@ def tile_list_creek_half_step_kernel(
             )
 
         load_table_words(0)
-        for row, vector in ((VEC_ROW, gain), (VEC_ROW + SLOTS, step)):
-            nc.sync.dma_start(
-                out=vec[row : row + SLOTS, :].rearrange("t (c j) -> t c j", j=8),
-                in_=vector.rearrange("(c t j) -> t c j", t=SLOTS, j=8),
-            )
+        for tile, vector in ((gain_sb, gain), (step_sb, step)):
+            nc.sync.dma_start(out=tile[:], in_=vector.rearrange("(b p t) -> p b t", b=PASSES, t=SLOTS))
         nc.sync.dma_start(pos1_sb[:], pos1)
         nc.sync.dma_start(pos2_sb[:], pos2)
         load_table_words(1)
+        w1_raw = keep.tile([P, W1_WORDS], I32, name="w1_raw", tag="slot0", align_bytes=64)
+        nc.sync.dma_start(
+            out=w1_raw[:].rearrange("p (a c) -> p a c", a=PASSES),
+            in_=w1_words.bitcast(I32).rearrange("a p c -> p a c"),
+        )
 
         w2_raw = {}
 
         def load_w2(a, b, raw):
-            rows = w2[BANK * a : BANK * (a + 1), BANK * b : BANK * (b + 1)].rearrange(
-                "(g t j) n -> t g j n", t=SLOTS, j=8
-            )
-            for t in range(SLOTS):
-                nc.sync.dma_start(out=raw[:, t, :], in_=rows[t])
+            rows = w2[BANK * a : BANK * (a + 1), BANK * b : BANK * (b + 1)]
+            nc.sync.dma_start(out=raw, in_=rows.rearrange("(p t) n -> p t n", t=SLOTS))
             w2_raw[a, b] = raw
 
         nc.vector.tensor_copy(v_sc_raw[:], tab_sc[:].indirect(offs_sb[:]))
@@ -99,11 +94,6 @@ def tile_list_creek_half_step_kernel(
                 out=v_sc[32 * q : 32 * q + 4, :].bitcast(I32).rearrange("r (a c) -> r a c", a=PASSES),
                 in_=v_sc_raw[first : first + 8, :].bitcast(I32),
             )
-        w1_raw = keep.tile([P, W1_WORDS], I32, name="w1_raw", tag="slot0", align_bytes=64)
-        nc.sync.dma_start(
-            out=w1_raw[:].rearrange("p (a c) -> p a c", a=PASSES),
-            in_=w1_words.bitcast(I32).rearrange("a p c -> p a c"),
-        )
         v_w = {}
         half_cols = BANK // 16
 
@@ -124,21 +114,15 @@ def tile_list_creek_half_step_kernel(
 
         w1_sc = keep.tile([P, PASSES * H], U8, name="w1_sc", align_bytes=64)
         nc.vector.tensor_copy(
-            out=w1_sc[:].bitcast(I32).rearrange("p (s t g w) -> p s t g w", t=SLOTS, g=16, w=2),
-            in_=w1_sc_raw[:].rearrange("p (s g t w) -> p s t g w", t=SLOTS, g=16, w=2),
+            out=w1_sc[:].rearrange("p (s t m) -> p s t m", t=SLOTS, m=P),
+            in_=w1_sc_raw[:].bitcast(U8).rearrange("p (s m t) -> p s t m", t=SLOTS, m=P),
         )
         w1_c = keep.tile([P, PASSES * H * 2], U8, name="w1_c", align_bytes=64)
         nc.vector.tensor_copy(
-            out=w1_c[:].bitcast(I32).rearrange("p (s t g w) -> p s t g w", t=SLOTS, g=16, w=4),
-            in_=w1_raw[:].rearrange("p (s g t w) -> p s t g w", t=SLOTS, g=16, w=4),
+            out=w1_c[:].bitcast(U16).rearrange("p (s t m) -> p s t m", t=SLOTS, m=P),
+            in_=w1_raw[:].bitcast(U16).rearrange("p (s m t) -> p s t m", t=SLOTS, m=P),
         )
         gather_words(1, 1)
-
-        vec_ps = psum.tile([P, PASSES, P], F32, name="vec_ps", tag="bank")
-        for b in range(PASSES):
-            nc.tensor.transpose(vec_ps[:, b, :], vec[:, P * b : P * (b + 1)], ident[:])
-        vec_t = keep.tile([P, PASSES, 2 * SLOTS], F32, name="vec_t")
-        nc.scalar.activation(vec_t[:], vec_ps[:, :, VEC_ROW:P], ACT.Copy)
 
         w2_c = [keep.tile([P, H], U32, name="w2_c%d" % a, align_bytes=64) for a in range(PASSES)]
         w2_sc = [keep.tile([P, H], U8, name="w2_sc%d" % a, align_bytes=64) for a in range(PASSES)]
@@ -148,8 +132,9 @@ def tile_list_creek_half_step_kernel(
             if u == 0:
                 tag = "slot2" if (a, b) == (0, 0) else "w2_bf%d%d" % (a, b)
                 w2_bf[a, b] = keep.tile([P, SLOTS * BANK], BF16, name="w2_bf%d%d" % (a, b), tag=tag, align_bytes=64)
-            dst = w2_bf[a, b][:, BANK * u : BANK * (u + 1)].rearrange("p (g h i t) -> p g h t i", h=2, i=4, t=SLOTS)
-            src = w2_raw[a, b].rearrange("p t (g u h i) -> p u g h t i", u=SLOTS, h=2, i=4)[:, u]
+            part = slice(32 * u, 32 * (u + 1))
+            dst = w2_bf[a, b][:].rearrange("p (s m t) -> p m t s", s=SLOTS, t=SLOTS)[:, part]
+            src = w2_raw[a, b].rearrange("p t (m s) -> p m t s", s=SLOTS)[:, part]
             if (a, b) == (0, 0):
                 nc.vector.tensor_copy(out=dst, in_=src)
             else:
@@ -182,7 +167,7 @@ def tile_list_creek_half_step_kernel(
                         start=(a == 0),
                         stop=(a == PASSES - 1),
                     )
-                nc.scalar.copy(out=rows[:, BANK * c : BANK * (c + 1)], in_=acc[:])
+                nc.scalar.activation(rows[:, BANK * c : BANK * (c + 1)], acc[:], ACT.Copy)
             h.append(rows)
 
         HALF = M // 2
@@ -199,7 +184,7 @@ def tile_list_creek_half_step_kernel(
             nc.vector.tensor_tensor(
                 x_bf[:].rearrange("p (m t) -> p m t", t=SLOTS),
                 bounded[:].rearrange("p (m t) -> p m t", t=SLOTS),
-                vec_t[:, b, 0:SLOTS].unsqueeze(1).to_broadcast([P, HALF, SLOTS]),
+                gain_sb[:, b, :].unsqueeze(1).to_broadcast([P, HALF, SLOTS]),
                 ALU.mult,
             )
             return x_bf
@@ -251,7 +236,7 @@ def tile_list_creek_half_step_kernel(
                     stop=(a == PASSES - 1),
                 )
 
-        out_rows = out.rearrange("(b g t j) m -> b t g j m", b=PASSES, t=SLOTS, j=8)
+        out_rows = out.rearrange("(b p t) m -> b t p m", b=PASSES, t=SLOTS)
         last = PASSES * SLOTS - 1
         pieces = [(i, slice(0, M)) for i in range(last)] + [(last, slice(0, HALF)), (last, slice(HALF, M))]
         rates = []
@@ -260,7 +245,7 @@ def tile_list_creek_half_step_kernel(
             i, cols = pieces[n]
             b, t = divmod(i, SLOTS)
             width = cols.stop - cols.start
-            step_col = vec_t[:, b, SLOTS + t : SLOTS + t + 1]
+            step_col = step_sb[:, b, t : t + 1]
             res = keep.tile([P, width], F32, name="res%d" % n)
             if i in ON_GPSIMD:
                 scaled = ring.tile([P, width], F32, name="scaled")
@@ -268,7 +253,7 @@ def tile_list_creek_half_step_kernel(
                 nc.gpsimd.tensor_tensor(res[:], scaled[:], down[i][:, cols], ALU.add)
             else:
                 nc.vector.scalar_tensor_tensor(res[:], rates[n][:], step_col, down[i][:, cols], ALU.mult, ALU.add)
-            nc.sync.dma_start(out=out_rows[b, t][:, :, cols], in_=res[:])
+            nc.sync.dma_start(out=out_rows[b, t][:, cols], in_=res[:])
 
         for n, (i, cols) in enumerate(pieces):
             width = cols.stop - cols.start

@@ -14,16 +14,24 @@ ACT = mybir.ActivationFunctionType
 ALU = mybir.AluOpType
 
 K, H, T, S, M = 1024, 1024, 2048, 1024, 512
+FLOPS = 2 * K * H * S + 2 * H * H * M
+
 P = 128
 SLOTS = 4
 PASSES = 2
+TILES = PASSES * SLOTS
 BANK = 512
+QUADRANTS = 4
+PER_COLUMN = 16
+HALF = M // 2
 SC_ROW = 96
 W1_WORDS = PASSES * H // 2
 W1_SCALES = PASSES * H // 4
+CAST_COLS = P // SLOTS
+
+CAST_BEHIND = (0, 1, 2, 4, 5, 7)
 LATE = 5
 ON_GPSIMD = (0, 2, 4)
-FLOPS = 2 * K * H * S + 2 * H * H * M
 
 
 def tile_list_creek_half_step_kernel(
@@ -36,23 +44,26 @@ def tile_list_creek_half_step_kernel(
         ring = ctx.enter_context(tc.tile_pool(name="ring", bufs=3))
         psum = ctx.enter_context(tc.psum_pool(name="psum", bufs=8))
 
-        offs_sb = lists.tile([P, S // 16], U16, name="offs_sb")
-        pos1_sb = lists.tile([P, M // 16], U16, name="pos1_sb")
-        pos2_sb = lists.tile([P, M // 16], U16, name="pos2_sb")
+        offs_sb = lists.tile([P, S // PER_COLUMN], U16, name="offs_sb")
+        pos1_sb = lists.tile([P, M // PER_COLUMN], U16, name="pos1_sb")
+        pos2_sb = lists.tile([P, M // PER_COLUMN], U16, name="pos2_sb")
 
         tab_sc = keep.tile([P, T], U8, name="tab_sc")
-        tab_w = [keep.tile([P, T], U32, name="tab_w%d" % a, tag="slot%d" % (1 + a), align_bytes=64) for a in range(PASSES)]
-        w1_sc_raw = keep.tile([P, W1_SCALES], I32, name="w1_sc_raw")
+        tab_w = [
+            keep.tile([P, T], U32, name="tab_w%d" % a, tag="slot%d" % (1 + a), align_bytes=64) for a in range(PASSES)
+        ]
+        w1_sc_raw = keep.tile([P, W1_SCALES], I32, name="w1_sc_raw", align_bytes=64)
         v_sc_raw = keep.tile([P, S], U8, name="v_sc_raw")
         v_sc = keep.tile([P, PASSES * S], U8, name="v_sc", align_bytes=64)
         gain_sb = keep.tile([P, PASSES, SLOTS], F32, name="gain_sb")
         step_sb = keep.tile([P, PASSES, SLOTS], F32, name="step_sb")
 
-        nc.vector.memset(tab_sc[0:SC_ROW, :].bitcast(I32), 0)
         nc.vector.memset(w1_sc_raw[:], 0)
+        nc.vector.memset(tab_sc[0:SC_ROW, :].bitcast(I32), 0)
         nc.vector.memset(v_sc[:].bitcast(I32), 0)
+
         w1_sc_i32 = w1_scales.bitcast(I32)
-        for q in range(4):
+        for q in range(QUADRANTS):
             nc.scalar.dma_start(
                 out=w1_sc_raw[32 * q : 32 * q + 4, :].rearrange("r (a c) -> r a c", a=PASSES),
                 in_=w1_sc_i32[:, 4 * q : 4 * q + 4, :].rearrange("a r c -> r a c"),
@@ -73,88 +84,79 @@ def tile_list_creek_half_step_kernel(
             nc.sync.dma_start(out=tile[:], in_=vector.rearrange("(b p t) -> p b t", b=PASSES, t=SLOTS))
         nc.sync.dma_start(pos1_sb[:], pos1)
         nc.sync.dma_start(pos2_sb[:], pos2)
-        load_table_words(1)
         w1_raw = keep.tile([P, W1_WORDS], I32, name="w1_raw", tag="slot0", align_bytes=64)
         nc.sync.dma_start(
             out=w1_raw[:].rearrange("p (a c) -> p a c", a=PASSES),
             in_=w1_words.bitcast(I32).rearrange("a p c -> p a c"),
         )
-
-        w2_raw = {}
-
-        def load_w2(a, b, raw):
-            rows = w2[BANK * a : BANK * (a + 1), BANK * b : BANK * (b + 1)]
-            nc.sync.dma_start(out=raw, in_=rows.rearrange("(p t) n -> p t n", t=SLOTS))
-            w2_raw[a, b] = raw
+        load_table_words(1)
 
         nc.vector.tensor_copy(v_sc_raw[:], tab_sc[:].indirect(offs_sb[:]))
-        for q in range(4):
-            first = SC_ROW + 8 * q
+        for q in range(QUADRANTS):
+            first = SC_ROW + 4 * PASSES * q
             nc.scalar.dma_start(
                 out=v_sc[32 * q : 32 * q + 4, :].bitcast(I32).rearrange("r (a c) -> r a c", a=PASSES),
-                in_=v_sc_raw[first : first + 8, :].bitcast(I32),
+                in_=v_sc_raw[first : first + 4 * PASSES, :].bitcast(I32),
             )
-        v_w = {}
-        half_cols = BANK // 16
 
-        def gather_words(a, c):
-            tag = "slot0" if (a, c) == (1, 1) else "v_w%d%d" % (a, c)
+        v_w = {}
+        list_cols = BANK // PER_COLUMN
+
+        def gather_words(a, c, tag):
             v_w[a, c] = keep.tile([P, BANK], U32, name="v_w%d%d" % (a, c), tag=tag, align_bytes=64)
             nc.vector.tensor_copy(
-                v_w[a, c][:], tab_w[a][:].indirect(offs_sb[:, half_cols * c : half_cols * (c + 1)])
+                v_w[a, c][:], tab_w[a][:].indirect(offs_sb[:, list_cols * c : list_cols * (c + 1)])
             )
 
-        gather_words(0, 0)
-        gather_words(0, 1)
+        gather_words(0, 0, "v_w00")
+        gather_words(0, 1, "v_w01")
+
         w2_in = keep.tile([P, PASSES * PASSES, SLOTS, BANK], F32, name="w2_in", tag="slot1", align_bytes=64)
         for a in range(PASSES):
             for b in range(PASSES):
-                load_w2(a, b, w2_in[:, PASSES * a + b])
-        gather_words(1, 0)
+                rows = w2[BANK * a : BANK * (a + 1), BANK * b : BANK * (b + 1)]
+                nc.sync.dma_start(out=w2_in[:, PASSES * a + b], in_=rows.rearrange("(p t) n -> p t n", t=SLOTS))
 
-        w1_sc = keep.tile([P, PASSES * H], U8, name="w1_sc", align_bytes=64)
-        nc.vector.tensor_copy(
-            out=w1_sc[:].rearrange("p (s t m) -> p s t m", t=SLOTS, m=P),
-            in_=w1_sc_raw[:].bitcast(U8).rearrange("p (s m t) -> p s t m", t=SLOTS, m=P),
-        )
         w1_c = keep.tile([P, PASSES * H * 2], U8, name="w1_c", align_bytes=64)
         nc.vector.tensor_copy(
             out=w1_c[:].bitcast(U16).rearrange("p (s t m) -> p s t m", t=SLOTS, m=P),
             in_=w1_raw[:].bitcast(U16).rearrange("p (s m t) -> p s t m", t=SLOTS, m=P),
         )
-        gather_words(1, 1)
+        gather_words(1, 0, "slot0")
+        w1_sc = keep.tile([P, PASSES * H], U8, name="w1_sc", align_bytes=64)
+        nc.vector.tensor_copy(
+            out=w1_sc[:].rearrange("p (s t m) -> p s t m", t=SLOTS, m=P),
+            in_=w1_sc_raw[:].bitcast(U8).rearrange("p (s m t) -> p s t m", t=SLOTS, m=P),
+        )
+        gather_words(1, 1, "w1_sc_raw")
 
         w2_c = [keep.tile([P, H], U32, name="w2_c%d" % a, align_bytes=64) for a in range(PASSES)]
         w2_sc = [keep.tile([P, H], U8, name="w2_sc%d" % a, align_bytes=64) for a in range(PASSES)]
         w2_bf = {}
 
-        def cast_w2(a, b, u):
+        def cast_w2(copy, a, b, u, tag):
             if u == 0:
-                tag = "slot2" if (a, b) == (0, 0) else "w2_bf%d%d" % (a, b)
                 w2_bf[a, b] = keep.tile([P, SLOTS * BANK], BF16, name="w2_bf%d%d" % (a, b), tag=tag, align_bytes=64)
-            part = slice(32 * u, 32 * (u + 1))
-            dst = w2_bf[a, b][:].rearrange("p (s m t) -> p m t s", s=SLOTS, t=SLOTS)[:, part]
-            src = w2_raw[a, b].rearrange("p t (m s) -> p m t s", s=SLOTS)[:, part]
-            if (a, b) == (0, 0):
-                nc.vector.tensor_copy(out=dst, in_=src)
-            else:
-                nc.scalar.copy(out=dst, in_=src)
-
-        def quantize_w2(a, b):
-            nc.vector.quantize_mx(
-                out=w2_c[a][:, BANK * b : BANK * (b + 1)].bitcast(FP8X4),
-                scales=w2_sc[a][:, BANK * b : BANK * (b + 1)],
-                in_=w2_bf[a, b][:],
+            part = slice(CAST_COLS * u, CAST_COLS * (u + 1))
+            copy(
+                out=w2_bf[a, b][:].rearrange("p (s m t) -> p m t s", s=SLOTS, t=SLOTS)[:, part],
+                in_=w2_in[:, PASSES * a + b].rearrange("p t (m s) -> p m t s", s=SLOTS)[:, part],
             )
+            if u == SLOTS - 1:
+                nc.vector.quantize_mx(
+                    out=w2_c[a][:, BANK * b : BANK * (b + 1)].bitcast(FP8X4),
+                    scales=w2_sc[a][:, BANK * b : BANK * (b + 1)],
+                    in_=w2_bf[a, b][:],
+                )
 
         h = []
         picked = [keep.tile([P, SLOTS, M], F32, name="picked%d" % b) for b in range(PASSES)]
         x_c = [keep.tile([P, M], U32, name="x_c%d" % b, align_bytes=64) for b in range(PASSES)]
         x_sc = [keep.tile([P, M], U8, name="x_sc%d" % b, align_bytes=64) for b in range(PASSES)]
 
-        def stage1(i):
-            rows = keep.tile([P, S], F32, name="h%d" % i)
-            for c in range(2):
+        def first_product(i):
+            h_tile = keep.tile([P, S], F32, name="h%d" % i)
+            for c in range(S // BANK):
                 acc = psum.tile([P, BANK], F32, name="acc", tag="bank")
                 for a in range(PASSES):
                     col = H * a + P * i
@@ -167,17 +169,14 @@ def tile_list_creek_half_step_kernel(
                         start=(a == 0),
                         stop=(a == PASSES - 1),
                     )
-                nc.scalar.activation(rows[:, BANK * c : BANK * (c + 1)], acc[:], ACT.Copy)
-            h.append(rows)
-
-        HALF = M // 2
+                nc.scalar.activation(h_tile[:, BANK * c : BANK * (c + 1)], acc[:], ACT.Copy)
+            h.append(h_tile)
 
         def make_x(b, c):
-            cols = slice(HALF * c, HALF * (c + 1))
             bounded = ring.tile([P, HALF * SLOTS], F32, name="bounded")
             nc.scalar.activation(
-                bounded[:].rearrange("p (c i t) -> p c t i", i=4, t=SLOTS),
-                picked[b][:, :, cols].rearrange("p t (c i) -> p c t i", i=4),
+                bounded[:].rearrange("p (g i t) -> p g t i", i=4, t=SLOTS),
+                picked[b][:, :, HALF * c : HALF * (c + 1)].rearrange("p t (g i) -> p g t i", i=4),
                 ACT.Tanh,
             )
             x_bf = keep.tile([P, HALF * SLOTS], BF16, name="x_bf%d%d" % (b, c), align_bytes=64)
@@ -189,43 +188,40 @@ def tile_list_creek_half_step_kernel(
             )
             return x_bf
 
-        def quantize_x(b, c, x_bf):
-            cols = slice(HALF * c, HALF * (c + 1))
-            nc.vector.quantize_mx(out=x_c[b][:, cols].bitcast(FP8X4), scales=x_sc[b][:, cols], in_=x_bf[:])
-
-        units = [(a, b, u) for a in range(PASSES) for b in range(PASSES) for u in range(SLOTS)]
         for u in range(SLOTS):
-            cast_w2(0, 0, u)
-        quantize_w2(0, 0)
-        share = [4, 6, 8, 10, 10, 12, 14, 14, 16]
-        for i in range(PASSES * SLOTS):
+            cast_w2(nc.vector.tensor_copy, 0, 0, u, "slot2")
+        scalar_casts = [(a, b, u) for a in range(PASSES) for b in range(PASSES) for u in range(SLOTS)][SLOTS:]
+
+        for i in range(TILES):
             b, t = divmod(i, SLOTS)
-            stage1(i)
+            first_product(i)
             nc.vector.tensor_copy(picked[b][:, t, :], h[i][:].indirect(pos1_sb[:]))
-            for a, bb, u in units[share[i] : share[i + 1]]:
-                cast_w2(a, bb, u)
-                if u == SLOTS - 1:
-                    quantize_w2(a, bb)
+            if i in CAST_BEHIND:
+                done = 2 * CAST_BEHIND.index(i)
+                for unit_a, unit_b, u in scalar_casts[done : done + 2]:
+                    cast_w2(nc.scalar.copy, unit_a, unit_b, u, "w2_bf%d%d" % (unit_a, unit_b))
             if t == SLOTS - 1:
-                halves = [make_x(b, c) for c in range(2)]
-                for c in range(2):
-                    quantize_x(b, c, halves[c])
+                halves = [make_x(b, c) for c in range(M // HALF)]
+                for c, x_bf in enumerate(halves):
+                    cols = slice(HALF * c, HALF * (c + 1))
+                    nc.vector.quantize_mx(out=x_c[b][:, cols].bitcast(FP8X4), scales=x_sc[b][:, cols], in_=x_bf[:])
 
+        last = TILES - 1
         down = []
-        late = keep.tile([P, PASSES * SLOTS - 1 - LATE, M], F32, name="late", tag="slot1", align_bytes=64)
-        for i in range(PASSES * SLOTS):
+        late = keep.tile([P, last - LATE, M], F32, name="late", tag="slot1", align_bytes=64)
+        for i in range(TILES):
             if i < LATE:
-                d = keep.tile([P, M], F32, name="down%d" % i)[:]
-            elif i < PASSES * SLOTS - 1:
-                d = late[:, i - LATE, :]
+                skip = keep.tile([P, M], F32, name="down%d" % i)[:]
+            elif i < last:
+                skip = late[:, i - LATE, :]
             else:
-                d = keep.tile([P, M], F32, name="down_last", tag="x_bf11", align_bytes=64)[:]
-            nc.vector.tensor_copy(d, h[i][:].indirect(pos2_sb[:]))
-            down.append(d)
+                skip = keep.tile([P, M], F32, name="down_last", tag="x_bf11", align_bytes=64)[:]
+            nc.vector.tensor_copy(skip, h[i][:].indirect(pos2_sb[:]))
+            down.append(skip)
 
-        y = [psum.tile([P, M], F32, name="y%d" % i, tag="bank") for i in range(PASSES * SLOTS)]
+        y = [psum.tile([P, M], F32, name="y%d" % i, tag="bank") for i in range(TILES)]
         for a in range(PASSES):
-            for i in range(PASSES * SLOTS):
+            for i in range(TILES):
                 nc.tensor.matmul_mx(
                     out=y[i][:],
                     lhsT=w2_c[a][:, P * i : P * (i + 1)].bitcast(FP8X4),
@@ -237,7 +233,6 @@ def tile_list_creek_half_step_kernel(
                 )
 
         out_rows = out.rearrange("(b p t) m -> b t p m", b=PASSES, t=SLOTS)
-        last = PASSES * SLOTS - 1
         pieces = [(i, slice(0, M)) for i in range(last)] + [(last, slice(0, HALF)), (last, slice(HALF, M))]
         rates = []
 

@@ -29,9 +29,9 @@ W1_WORDS = PASSES * H // 2
 W1_SCALES = PASSES * H // 4
 CAST_COLS = P // SLOTS
 
-CAST_BEHIND = (0, 1, 2, 4, 5, 7)
-LATE = 5
-ON_GPSIMD = (0, 2, 4)
+
+ON_GPSIMD = (0, 1, 2, 3, 4)
+GAIN_ON_GPSIMD = (True, True, True, True)
 
 
 def tile_list_creek_half_step_kernel(
@@ -49,11 +49,9 @@ def tile_list_creek_half_step_kernel(
         pos2_sb = lists.tile([P, M // PER_COLUMN], U16, name="pos2_sb")
 
         tab_sc = keep.tile([P, T], U8, name="tab_sc")
-        tab_w = [
-            keep.tile([P, T], U32, name="tab_w%d" % a, tag="slot%d" % (1 + a), align_bytes=64) for a in range(PASSES)
-        ]
+        tab_w = [keep.tile([P, T], U32, name="tab_w%d" % a, align_bytes=64) for a in range(PASSES)]
         w1_sc_raw = keep.tile([P, W1_SCALES], I32, name="w1_sc_raw", align_bytes=64)
-        v_sc_raw = keep.tile([P, S], U8, name="v_sc_raw")
+        v_sc_raw = keep.tile([P, S], U8, name="v_sc_raw", align_bytes=64)
         v_sc = keep.tile([P, PASSES * S], U8, name="v_sc", align_bytes=64)
         gain_sb = keep.tile([P, PASSES, SLOTS], F32, name="gain_sb")
         step_sb = keep.tile([P, PASSES, SLOTS], F32, name="step_sb")
@@ -80,16 +78,11 @@ def tile_list_creek_half_step_kernel(
             )
 
         load_table_words(0)
-        for tile, vector in ((gain_sb, gain), (step_sb, step)):
-            nc.sync.dma_start(out=tile[:], in_=vector.rearrange("(b p t) -> p b t", b=PASSES, t=SLOTS))
-        nc.sync.dma_start(pos1_sb[:], pos1)
-        nc.sync.dma_start(pos2_sb[:], pos2)
-        w1_raw = keep.tile([P, W1_WORDS], I32, name="w1_raw", tag="slot0", align_bytes=64)
-        nc.sync.dma_start(
-            out=w1_raw[:].rearrange("p (a c) -> p a c", a=PASSES),
-            in_=w1_words.bitcast(I32).rearrange("a p c -> p a c"),
-        )
+        w1_raw = [keep.tile([P, H // 2], I32, name="w1_raw%d" % a, align_bytes=64) for a in range(PASSES)]
+        for a in range(PASSES):
+            nc.sync.dma_start(out=w1_raw[a][:], in_=w1_words[a].bitcast(I32))
         load_table_words(1)
+        nc.sync.dma_start(pos1_sb[:], pos1)
 
         nc.vector.tensor_copy(v_sc_raw[:], tab_sc[:].indirect(offs_sb[:]))
         for q in range(QUADRANTS):
@@ -109,26 +102,28 @@ def tile_list_creek_half_step_kernel(
             )
 
         gather_words(0, 0, "v_w00")
-        gather_words(0, 1, "v_w01")
-
-        w2_in = keep.tile([P, PASSES * PASSES, SLOTS, BANK], F32, name="w2_in", tag="slot1", align_bytes=64)
-        for a in range(PASSES):
-            for b in range(PASSES):
-                rows = w2[BANK * a : BANK * (a + 1), BANK * b : BANK * (b + 1)]
-                nc.sync.dma_start(out=w2_in[:, PASSES * a + b], in_=rows.rearrange("(p t) n -> p t n", t=SLOTS))
-
         w1_c = keep.tile([P, PASSES * H * 2], U8, name="w1_c", align_bytes=64)
-        nc.vector.tensor_copy(
-            out=w1_c[:].bitcast(U16).rearrange("p (s t m) -> p s t m", t=SLOTS, m=P),
-            in_=w1_raw[:].bitcast(U16).rearrange("p (s m t) -> p s t m", t=SLOTS, m=P),
-        )
-        gather_words(1, 0, "slot0")
+        for a in range(PASSES):
+            nc.vector.tensor_copy(
+                out=w1_c[:, 2 * H * a : 2 * H * (a + 1)].bitcast(U16).rearrange("p (s t m) -> p s t m", t=SLOTS, m=P),
+                in_=w1_raw[a][:].bitcast(U16).rearrange("p (s m t) -> p s t m", t=SLOTS, m=P),
+            )
         w1_sc = keep.tile([P, PASSES * H], U8, name="w1_sc", align_bytes=64)
         nc.vector.tensor_copy(
             out=w1_sc[:].rearrange("p (s t m) -> p s t m", t=SLOTS, m=P),
             in_=w1_sc_raw[:].bitcast(U8).rearrange("p (s m t) -> p s t m", t=SLOTS, m=P),
         )
-        gather_words(1, 1, "w1_sc_raw")
+        gather_words(1, 0, "w1_sc_raw")
+        gather_words(1, 1, "v_w11")
+        gather_words(0, 1, "tab_w1")
+
+        units = [(a, b) for b in range(PASSES) for a in range(PASSES)]
+        w2_in = {}
+        for (a, b), tag in zip(units[:3], ("w1_raw0", "w1_raw1", "v_sc_raw")):
+            w2_in[a, b] = keep.tile([P, SLOTS, BANK], F32, name="w2_in%d%d" % (a, b), tag=tag, align_bytes=64)
+        for n, (a, b) in enumerate(units[:3]):
+            rows = w2[BANK * a : BANK * (a + 1), BANK * b : BANK * (b + 1)]
+            nc.sync.dma_start(out=w2_in[a, b][:], in_=rows.rearrange("(p t) n -> p t n", t=SLOTS))
 
         w2_c = [keep.tile([P, H], U32, name="w2_c%d" % a, align_bytes=64) for a in range(PASSES)]
         w2_sc = [keep.tile([P, H], U8, name="w2_sc%d" % a, align_bytes=64) for a in range(PASSES)]
@@ -140,98 +135,127 @@ def tile_list_creek_half_step_kernel(
             part = slice(CAST_COLS * u, CAST_COLS * (u + 1))
             copy(
                 out=w2_bf[a, b][:].rearrange("p (s m t) -> p m t s", s=SLOTS, t=SLOTS)[:, part],
-                in_=w2_in[:, PASSES * a + b].rearrange("p t (m s) -> p m t s", s=SLOTS)[:, part],
+                in_=w2_in[a, b][:].rearrange("p t (m s) -> p m t s", s=SLOTS)[:, part],
             )
-            if u == SLOTS - 1:
-                nc.vector.quantize_mx(
-                    out=w2_c[a][:, BANK * b : BANK * (b + 1)].bitcast(FP8X4),
-                    scales=w2_sc[a][:, BANK * b : BANK * (b + 1)],
-                    in_=w2_bf[a, b][:],
-                )
 
-        h = []
+        def quantise_w2(a, b):
+            nc.vector.quantize_mx(
+                out=w2_c[a][:, BANK * b : BANK * (b + 1)].bitcast(FP8X4),
+                scales=w2_sc[a][:, BANK * b : BANK * (b + 1)],
+                in_=w2_bf[a, b][:],
+            )
+
+        h = [keep.tile([P, S], F32, name="h%d" % i) for i in range(TILES)]
         picked = [keep.tile([P, SLOTS, M], F32, name="picked%d" % b) for b in range(PASSES)]
         x_c = [keep.tile([P, M], U32, name="x_c%d" % b, align_bytes=64) for b in range(PASSES)]
         x_sc = [keep.tile([P, M], U8, name="x_sc%d" % b, align_bytes=64) for b in range(PASSES)]
 
-        def first_product(i):
-            h_tile = keep.tile([P, S], F32, name="h%d" % i)
-            for c in range(S // BANK):
-                acc = psum.tile([P, BANK], F32, name="acc", tag="bank")
-                for a in range(PASSES):
-                    col = H * a + P * i
-                    nc.tensor.matmul_mx(
-                        out=acc[:],
-                        lhsT=w1_c[:, 2 * col : 2 * (col + P)].bitcast(FP4X4),
-                        lhsT_scale=w1_sc[:, col : col + P],
-                        rhs=v_w[a, c][:].bitcast(FP8X4),
-                        rhs_scale=v_sc[:, S * a + BANK * c : S * a + BANK * (c + 1)],
-                        start=(a == 0),
-                        stop=(a == PASSES - 1),
-                    )
-                nc.scalar.activation(h_tile[:, BANK * c : BANK * (c + 1)], acc[:], ACT.Copy)
-            h.append(h_tile)
+        def first_product(i, c):
+            acc = psum.tile([P, BANK], F32, name="acc", tag="bank")
+            for a in range(PASSES):
+                col = H * a + P * i
+                nc.tensor.matmul_mx(
+                    out=acc[:],
+                    lhsT=w1_c[:, 2 * col : 2 * (col + P)].bitcast(FP4X4),
+                    lhsT_scale=w1_sc[:, col : col + P],
+                    rhs=v_w[a, c][:].bitcast(FP8X4),
+                    rhs_scale=v_sc[:, S * a + BANK * c : S * a + BANK * (c + 1)],
+                    start=(a == 0),
+                    stop=(a == PASSES - 1),
+                )
+            nc.scalar.activation(h[i][:, BANK * c : BANK * (c + 1)], acc[:], ACT.Copy)
+
+        def pick_upstream(i):
+            b, t = divmod(i, SLOTS)
+            nc.vector.tensor_copy(picked[b][:, t, :], h[i][:].indirect(pos1_sb[:]))
+
+        x_bf = {}
 
         def make_x(b, c):
-            bounded = ring.tile([P, HALF * SLOTS], F32, name="bounded")
+            bounded = keep.tile([P, HALF * SLOTS], F32, name="bounded%d%d" % (b, c))
             nc.scalar.activation(
                 bounded[:].rearrange("p (g i t) -> p g t i", i=4, t=SLOTS),
                 picked[b][:, :, HALF * c : HALF * (c + 1)].rearrange("p t (g i) -> p g t i", i=4),
                 ACT.Tanh,
             )
-            x_bf = keep.tile([P, HALF * SLOTS], BF16, name="x_bf%d%d" % (b, c), align_bytes=64)
-            nc.vector.tensor_tensor(
-                x_bf[:].rearrange("p (m t) -> p m t", t=SLOTS),
+            x_bf[b, c] = keep.tile([P, HALF * SLOTS], BF16, name="x_bf%d%d" % (b, c), align_bytes=64)
+            engine = nc.gpsimd if GAIN_ON_GPSIMD[2 * b + c] else nc.vector
+            engine.tensor_tensor(
+                x_bf[b, c][:].rearrange("p (m t) -> p m t", t=SLOTS),
                 bounded[:].rearrange("p (m t) -> p m t", t=SLOTS),
                 gain_sb[:, b, :].unsqueeze(1).to_broadcast([P, HALF, SLOTS]),
                 ALU.mult,
             )
-            return x_bf
 
+        def quantise_x(b, c):
+            cols = slice(HALF * c, HALF * (c + 1))
+            nc.vector.quantize_mx(out=x_c[b][:, cols].bitcast(FP8X4), scales=x_sc[b][:, cols], in_=x_bf[b, c][:])
+
+        nc.sync.dma_start(out=gain_sb[:], in_=gain.rearrange("(b p t) -> p b t", b=PASSES, t=SLOTS))
+        a, b = units[3]
+        rows = w2[BANK * a : BANK * (a + 1), BANK * b : BANK * (b + 1)]
+        w2_in[a, b] = keep.tile([P, SLOTS, BANK], F32, name="w2_in_last", tag="tab_w0", align_bytes=64)
+        nc.sync.dma_start(out=w2_in[a, b][:], in_=rows.rearrange("(p t) n -> p t n", t=SLOTS))
+        nc.sync.dma_start(pos2_sb[:], pos2)
+        nc.sync.dma_start(out=step_sb[:], in_=step.rearrange("(b p t) -> p b t", b=PASSES, t=SLOTS))
+
+        for c in range(2):
+            for i in range(SLOTS):
+                first_product(i, c)
         for u in range(SLOTS):
-            cast_w2(nc.vector.tensor_copy, 0, 0, u, "slot2")
-        scalar_casts = [(a, b, u) for a in range(PASSES) for b in range(PASSES) for u in range(SLOTS)][SLOTS:]
+            cast_w2(nc.vector.tensor_copy, 0, 0, u, "w2_bf00")
+        for i in range(SLOTS):
+            pick_upstream(i)
+        quantise_w2(0, 0)
+        for i in range(SLOTS, TILES):
+            if i == TILES - 1:
+                make_x(0, 0)
+            for c in range(2):
+                first_product(i, c)
+            pick_upstream(i)
+        make_x(0, 1)
+        for c in range(2):
+            make_x(1, c)
+        for a, b in units[1:]:
+            for u in range(SLOTS):
+                cast_w2(nc.scalar.copy, a, b, u, "w2_bf%d%d" % (a, b))
 
-        for i in range(TILES):
-            b, t = divmod(i, SLOTS)
-            first_product(i)
-            nc.vector.tensor_copy(picked[b][:, t, :], h[i][:].indirect(pos1_sb[:]))
-            if i in CAST_BEHIND:
-                done = 2 * CAST_BEHIND.index(i)
-                for unit_a, unit_b, u in scalar_casts[done : done + 2]:
-                    cast_w2(nc.scalar.copy, unit_a, unit_b, u, "w2_bf%d%d" % (unit_a, unit_b))
-            if t == SLOTS - 1:
-                halves = [make_x(b, c) for c in range(M // HALF)]
-                for c, x_bf in enumerate(halves):
-                    cols = slice(HALF * c, HALF * (c + 1))
-                    nc.vector.quantize_mx(out=x_c[b][:, cols].bitcast(FP8X4), scales=x_sc[b][:, cols], in_=x_bf[:])
+        down = {}
 
-        last = TILES - 1
-        down = []
-        late = keep.tile([P, last - LATE, M], F32, name="late", tag="slot1", align_bytes=64)
-        for i in range(TILES):
-            if i < LATE:
-                skip = keep.tile([P, M], F32, name="down%d" % i)[:]
-            elif i < last:
-                skip = late[:, i - LATE, :]
-            else:
-                skip = keep.tile([P, M], F32, name="down_last", tag="x_bf11", align_bytes=64)[:]
+        def pick_downstream(i, skip):
             nc.vector.tensor_copy(skip, h[i][:].indirect(pos2_sb[:]))
-            down.append(skip)
+            down[i] = skip
+
+        early = keep.tile([P, SLOTS, M], F32, name="early", tag="picked0")
+        pick_downstream(0, early[:, 0, :])
+        pick_downstream(1, early[:, 1, :])
+        quantise_x(0, 0)
+        pick_downstream(2, early[:, 2, :])
+        quantise_x(0, 1)
+        pick_downstream(3, early[:, 3, :])
+        quantise_w2(1, 0)
+        quantise_x(1, 0)
+        pick_downstream(4, keep.tile([P, M], F32, name="down4", tag="x_bf01", align_bytes=64)[:])
+        quantise_x(1, 1)
+        pick_downstream(5, keep.tile([P, M], F32, name="down5", tag="x_bf11", align_bytes=64)[:])
+        quantise_w2(0, 1)
+        quantise_w2(1, 1)
 
         y = [psum.tile([P, M], F32, name="y%d" % i, tag="bank") for i in range(TILES)]
-        for a in range(PASSES):
-            for i in range(TILES):
-                nc.tensor.matmul_mx(
-                    out=y[i][:],
-                    lhsT=w2_c[a][:, P * i : P * (i + 1)].bitcast(FP8X4),
-                    lhsT_scale=w2_sc[a][:, P * i : P * (i + 1)],
-                    rhs=x_c[a][:].bitcast(FP8X4),
-                    rhs_scale=x_sc[a][:],
-                    start=(a == 0),
-                    stop=(a == PASSES - 1),
-                )
+        for b in range(PASSES):
+            for a in range(PASSES):
+                for i in range(SLOTS * b, SLOTS * (b + 1)):
+                    nc.tensor.matmul_mx(
+                        out=y[i][:],
+                        lhsT=w2_c[a][:, P * i : P * (i + 1)].bitcast(FP8X4),
+                        lhsT_scale=w2_sc[a][:, P * i : P * (i + 1)],
+                        rhs=x_c[a][:].bitcast(FP8X4),
+                        rhs_scale=x_sc[a][:],
+                        start=(a == 0),
+                        stop=(a == PASSES - 1),
+                    )
 
+        last = TILES - 1
         out_rows = out.rearrange("(b p t) m -> b t p m", b=PASSES, t=SLOTS)
         pieces = [(i, slice(0, M)) for i in range(last)] + [(last, slice(0, HALF)), (last, slice(HALF, M))]
         rates = []
@@ -252,11 +276,14 @@ def tile_list_creek_half_step_kernel(
 
         for n, (i, cols) in enumerate(pieces):
             width = cols.stop - cols.start
-            moved = ring.tile([P, width], F32, name="moved")
+            moved = keep.tile([P, width], F32, name="moved%d" % n)
             nc.vector.tensor_tensor(moved[:], y[i][:, cols], down[i][:, cols], ALU.add)
             rate = ring.tile([P, width], F32, name="rate")
             nc.scalar.activation(rate[:], moved[:], ACT.Tanh)
             rates.append(rate)
+            if n in (1, 3):
+                j = 6 + n // 2
+                pick_downstream(j, keep.tile([P, M], F32, name="down%d" % j, tag="moved%d" % (n - 1))[:])
             if n > 0:
                 finish(n - 1)
         finish(len(pieces) - 1)

@@ -30,8 +30,7 @@ W1_SCALES = PASSES * H // 4
 CAST_COLS = P // SLOTS
 
 
-ON_GPSIMD = (0, 1, 2, 3, 4)
-GAIN_ON_GPSIMD = (True, True, True, True)
+ON_GPSIMD = (0, 1, 2)
 
 
 def tile_list_creek_half_step_kernel(
@@ -48,49 +47,62 @@ def tile_list_creek_half_step_kernel(
         pos1_sb = lists.tile([P, M // PER_COLUMN], U16, name="pos1_sb")
         pos2_sb = lists.tile([P, M // PER_COLUMN], U16, name="pos2_sb")
 
-        tab_sc = keep.tile([P, T], U8, name="tab_sc")
-        tab_w = [keep.tile([P, T], U32, name="tab_w%d" % a, align_bytes=64) for a in range(PASSES)]
-        w1_sc_raw = keep.tile([P, W1_SCALES], I32, name="w1_sc_raw", align_bytes=64)
+        tab_sc = keep.tile([P, T], U8, name="tab_sc", align_bytes=64)
+        w1_sc_raw = keep.tile([P, H], U8, name="w1_sc_raw", align_bytes=64)
+        w1_sc_ord = keep.tile([P, H], U8, name="w1_sc_ord", align_bytes=64)
+        w1_sc = keep.tile([P, PASSES * H], U8, name="w1_sc", align_bytes=64)
         v_sc_raw = keep.tile([P, S], U8, name="v_sc_raw", align_bytes=64)
         v_sc = keep.tile([P, PASSES * S], U8, name="v_sc", align_bytes=64)
-        gain_sb = keep.tile([P, PASSES, SLOTS], F32, name="gain_sb")
-        step_sb = keep.tile([P, PASSES, SLOTS], F32, name="step_sb")
 
-        nc.vector.memset(w1_sc_raw[:], 0)
+        nc.vector.memset(w1_sc_raw[0:SC_ROW, :].bitcast(I32), 0)
         nc.vector.memset(tab_sc[0:SC_ROW, :].bitcast(I32), 0)
+        nc.vector.memset(w1_sc[:].bitcast(I32), 0)
         nc.vector.memset(v_sc[:].bitcast(I32), 0)
 
-        w1_sc_i32 = w1_scales.bitcast(I32)
-        for q in range(QUADRANTS):
-            nc.scalar.dma_start(
-                out=w1_sc_raw[32 * q : 32 * q + 4, :].rearrange("r (a c) -> r a c", a=PASSES),
-                in_=w1_sc_i32[:, 4 * q : 4 * q + 4, :].rearrange("a r c -> r a c"),
-            )
+        def load_scale_rows(queue, tile, scales):
+            queue.dma_start(out=tile[SC_ROW:P, :].bitcast(I32), in_=scales.bitcast(I32).rearrange("a q c -> q a c"))
 
-        nc.sync.dma_start(offs_sb[:], offs)
-        nc.sync.dma_start(
-            out=tab_sc[SC_ROW:P, :].bitcast(I32), in_=tab_scales.bitcast(I32).rearrange("a q c -> q a c")
-        )
+        def move_scale_rows(queue, plane, rows):
+            for q in range(QUADRANTS):
+                first = SC_ROW + 4 * PASSES * q
+                queue.dma_start(
+                    out=plane[32 * q : 32 * q + 4, :].bitcast(I32).rearrange("r (a c) -> r a c", a=PASSES),
+                    in_=rows[first : first + 4 * PASSES, :].bitcast(I32),
+                )
 
-        def load_table_words(a):
-            nc.sync.dma_start(
+        tab_w = []
+
+        def load_table_words(queue, a, tag):
+            tab_w.append(keep.tile([P, T], U32, name="tab_w%d" % a, tag=tag, align_bytes=64))
+            queue.dma_start(
                 out=tab_w[a][:].bitcast(I32), in_=tab_words[a].rearrange("p t i -> p (t i)").bitcast(I32)
             )
 
-        load_table_words(0)
-        w1_raw = [keep.tile([P, H // 2], I32, name="w1_raw%d" % a, align_bytes=64) for a in range(PASSES)]
-        for a in range(PASSES):
-            nc.sync.dma_start(out=w1_raw[a][:], in_=w1_words[a].bitcast(I32))
-        load_table_words(1)
+        load_scale_rows(nc.scalar, w1_sc_raw, w1_scales)
+        nc.sync.dma_start(offs_sb[:], offs)
+        load_scale_rows(nc.sync, tab_sc, tab_scales)
         nc.sync.dma_start(pos1_sb[:], pos1)
+        nc.sync.dma_start(pos2_sb[:], pos2)
+        load_table_words(nc.sync, 0, "tab_w0")
+        w1_raw = keep.tile([P, W1_WORDS], I32, name="w1_raw", align_bytes=64)
+        nc.sync.dma_start(
+            out=w1_raw[:].rearrange("p (a c) -> p a c", a=PASSES),
+            in_=w1_words.bitcast(I32).rearrange("a p c -> p a c"),
+        )
+
+        nc.vector.tensor_copy(
+            out=w1_sc_ord[:].rearrange("p (b t m) -> p b t m", t=SLOTS, m=P),
+            in_=w1_sc_raw[:].rearrange("p (b m t) -> p b t m", t=SLOTS, m=P),
+        )
+        move_scale_rows(nc.scalar, w1_sc, w1_sc_ord)
+        load_table_words(nc.scalar, 1, "w1_sc_raw")
 
         nc.vector.tensor_copy(v_sc_raw[:], tab_sc[:].indirect(offs_sb[:]))
-        for q in range(QUADRANTS):
-            first = SC_ROW + 4 * PASSES * q
-            nc.scalar.dma_start(
-                out=v_sc[32 * q : 32 * q + 4, :].bitcast(I32).rearrange("r (a c) -> r a c", a=PASSES),
-                in_=v_sc_raw[first : first + 4 * PASSES, :].bitcast(I32),
-            )
+        move_scale_rows(nc.sync, v_sc, v_sc_raw)
+
+        vectors = keep.tile([P, 2, PASSES, SLOTS], F32, name="vectors", tag="w1_sc_ord", align_bytes=64)
+        gain_sb = vectors[:, 0]
+        step_sb = vectors[:, 1]
 
         v_w = {}
         list_cols = BANK // PER_COLUMN
@@ -103,30 +115,34 @@ def tile_list_creek_half_step_kernel(
 
         gather_words(0, 0, "v_w00")
         w1_c = keep.tile([P, PASSES * H * 2], U8, name="w1_c", align_bytes=64)
-        for a in range(PASSES):
-            nc.vector.tensor_copy(
-                out=w1_c[:, 2 * H * a : 2 * H * (a + 1)].bitcast(U16).rearrange("p (s t m) -> p s t m", t=SLOTS, m=P),
-                in_=w1_raw[a][:].bitcast(U16).rearrange("p (s m t) -> p s t m", t=SLOTS, m=P),
-            )
-        w1_sc = keep.tile([P, PASSES * H], U8, name="w1_sc", align_bytes=64)
         nc.vector.tensor_copy(
-            out=w1_sc[:].rearrange("p (s t m) -> p s t m", t=SLOTS, m=P),
-            in_=w1_sc_raw[:].bitcast(U8).rearrange("p (s m t) -> p s t m", t=SLOTS, m=P),
+            out=w1_c[:].bitcast(U16).rearrange("p (s t m) -> p s t m", t=SLOTS, m=P),
+            in_=w1_raw[:].bitcast(U16).rearrange("p (s m t) -> p s t m", t=SLOTS, m=P),
         )
-        gather_words(1, 0, "w1_sc_raw")
+        gather_words(1, 0, "v_w10")
         gather_words(1, 1, "v_w11")
-        gather_words(0, 1, "tab_w1")
+        gather_words(0, 1, "w1_sc_raw")
 
         units = [(a, b) for b in range(PASSES) for a in range(PASSES)]
-        w2_in = {}
-        for (a, b), tag in zip(units[:3], ("w1_raw0", "w1_raw1", "v_sc_raw")):
-            w2_in[a, b] = keep.tile([P, SLOTS, BANK], F32, name="w2_in%d%d" % (a, b), tag=tag, align_bytes=64)
-        for n, (a, b) in enumerate(units[:3]):
+        def load_w2(tile, a, b):
             rows = w2[BANK * a : BANK * (a + 1), BANK * b : BANK * (b + 1)]
-            nc.sync.dma_start(out=w2_in[a, b][:], in_=rows.rearrange("(p t) n -> p t n", t=SLOTS))
+            nc.sync.dma_start(out=tile, in_=rows.rearrange("(p t) n -> p t n", t=SLOTS))
 
-        w2_c = [keep.tile([P, H], U32, name="w2_c%d" % a, align_bytes=64) for a in range(PASSES)]
-        w2_sc = [keep.tile([P, H], U8, name="w2_sc%d" % a, align_bytes=64) for a in range(PASSES)]
+        w2_first = keep.tile([P, SLOTS, BANK], F32, name="w2_first", tag="w1_raw", align_bytes=64)
+        w2_rest = keep.tile([P, 3, SLOTS, BANK], F32, name="w2_rest", tag="tab_w0", align_bytes=64)
+        w2_in = {units[0]: w2_first[:]}
+        for n, unit in enumerate(units[1:]):
+            w2_in[unit] = w2_rest[:, n]
+        for a, b in units:
+            load_w2(w2_in[a, b], a, b)
+
+        operand = {}
+
+        def place(key, tile, n):
+            first = 5 * BANK * n
+            operand[key] = (tile[:, first : first + 4 * BANK], tile[:, first + 4 * BANK : first + 5 * BANK])
+
+        place(("w2", 0, 0), keep.tile([P, 5 * BANK], U8, name="w2_q00", align_bytes=64), 0)
         w2_bf = {}
 
         def cast_w2(copy, a, b, u, tag):
@@ -135,20 +151,16 @@ def tile_list_creek_half_step_kernel(
             part = slice(CAST_COLS * u, CAST_COLS * (u + 1))
             copy(
                 out=w2_bf[a, b][:].rearrange("p (s m t) -> p m t s", s=SLOTS, t=SLOTS)[:, part],
-                in_=w2_in[a, b][:].rearrange("p t (m s) -> p m t s", s=SLOTS)[:, part],
+                in_=w2_in[a, b].rearrange("p t (m s) -> p m t s", s=SLOTS)[:, part],
             )
 
         def quantise_w2(a, b):
             nc.vector.quantize_mx(
-                out=w2_c[a][:, BANK * b : BANK * (b + 1)].bitcast(FP8X4),
-                scales=w2_sc[a][:, BANK * b : BANK * (b + 1)],
-                in_=w2_bf[a, b][:],
+                out=operand["w2", a, b][0].bitcast(FP8X4), scales=operand["w2", a, b][1], in_=w2_bf[a, b][:]
             )
 
         h = [keep.tile([P, S], F32, name="h%d" % i) for i in range(TILES)]
-        picked = [keep.tile([P, SLOTS, M], F32, name="picked%d" % b) for b in range(PASSES)]
-        x_c = [keep.tile([P, M], U32, name="x_c%d" % b, align_bytes=64) for b in range(PASSES)]
-        x_sc = [keep.tile([P, M], U8, name="x_sc%d" % b, align_bytes=64) for b in range(PASSES)]
+        picked = [keep.tile([P, SLOTS, M], F32, name="picked%d" % b, align_bytes=64) for b in range(PASSES)]
 
         def first_product(i, c):
             acc = psum.tile([P, BANK], F32, name="acc", tag="bank")
@@ -169,35 +181,27 @@ def tile_list_creek_half_step_kernel(
             b, t = divmod(i, SLOTS)
             nc.vector.tensor_copy(picked[b][:, t, :], h[i][:].indirect(pos1_sb[:]))
 
-        x_bf = {}
+        x_bf = [keep.tile([P, M * SLOTS], BF16, name="x_bf%d" % b, align_bytes=64) for b in range(PASSES)]
 
         def make_x(b, c):
-            bounded = keep.tile([P, HALF * SLOTS], F32, name="bounded%d%d" % (b, c))
+            bounded = keep.tile([P, HALF * SLOTS], F32, name="bounded%d%d" % (b, c), align_bytes=64)
             nc.scalar.activation(
                 bounded[:].rearrange("p (g i t) -> p g t i", i=4, t=SLOTS),
                 picked[b][:, :, HALF * c : HALF * (c + 1)].rearrange("p t (g i) -> p g t i", i=4),
                 ACT.Tanh,
             )
-            x_bf[b, c] = keep.tile([P, HALF * SLOTS], BF16, name="x_bf%d%d" % (b, c), align_bytes=64)
-            engine = nc.gpsimd if GAIN_ON_GPSIMD[2 * b + c] else nc.vector
-            engine.tensor_tensor(
-                x_bf[b, c][:].rearrange("p (m t) -> p m t", t=SLOTS),
+            nc.gpsimd.tensor_tensor(
+                x_bf[b][:, HALF * SLOTS * c : HALF * SLOTS * (c + 1)].rearrange("p (m t) -> p m t", t=SLOTS),
                 bounded[:].rearrange("p (m t) -> p m t", t=SLOTS),
                 gain_sb[:, b, :].unsqueeze(1).to_broadcast([P, HALF, SLOTS]),
                 ALU.mult,
             )
 
-        def quantise_x(b, c):
-            cols = slice(HALF * c, HALF * (c + 1))
-            nc.vector.quantize_mx(out=x_c[b][:, cols].bitcast(FP8X4), scales=x_sc[b][:, cols], in_=x_bf[b, c][:])
+        def quantise_x(b):
+            nc.vector.quantize_mx(out=operand["x", b][0].bitcast(FP8X4), scales=operand["x", b][1], in_=x_bf[b][:])
 
-        nc.sync.dma_start(out=gain_sb[:], in_=gain.rearrange("(b p t) -> p b t", b=PASSES, t=SLOTS))
-        a, b = units[3]
-        rows = w2[BANK * a : BANK * (a + 1), BANK * b : BANK * (b + 1)]
-        w2_in[a, b] = keep.tile([P, SLOTS, BANK], F32, name="w2_in_last", tag="tab_w0", align_bytes=64)
-        nc.sync.dma_start(out=w2_in[a, b][:], in_=rows.rearrange("(p t) n -> p t n", t=SLOTS))
-        nc.sync.dma_start(pos2_sb[:], pos2)
-        nc.sync.dma_start(out=step_sb[:], in_=step.rearrange("(b p t) -> p b t", b=PASSES, t=SLOTS))
+        nc.sync.dma_start(out=gain_sb, in_=gain.rearrange("(b p t) -> p b t", b=PASSES, t=SLOTS))
+        nc.sync.dma_start(out=step_sb, in_=step.rearrange("(b p t) -> p b t", b=PASSES, t=SLOTS))
 
         for c in range(2):
             for i in range(SLOTS):
@@ -208,7 +212,7 @@ def tile_list_creek_half_step_kernel(
             pick_upstream(i)
         quantise_w2(0, 0)
         for i in range(SLOTS, TILES):
-            if i == TILES - 1:
+            if i == TILES - 2:
                 make_x(0, 0)
             for c in range(2):
                 first_product(i, c)
@@ -222,35 +226,36 @@ def tile_list_creek_half_step_kernel(
 
         down = {}
 
-        def pick_downstream(i, skip):
-            nc.vector.tensor_copy(skip, h[i][:].indirect(pos2_sb[:]))
-            down[i] = skip
+        def pick_downstream(first, count, tag):
+            tile = keep.tile([P, count, M], F32, name="down%d" % first, tag=tag, align_bytes=64)
+            for k in range(count):
+                nc.vector.tensor_copy(tile[:, k, :], h[first + k][:].indirect(pos2_sb[:]))
+                down[first + k] = tile[:, k, :]
 
-        early = keep.tile([P, SLOTS, M], F32, name="early", tag="picked0")
-        pick_downstream(0, early[:, 0, :])
-        pick_downstream(1, early[:, 1, :])
-        quantise_x(0, 0)
-        pick_downstream(2, early[:, 2, :])
-        quantise_x(0, 1)
-        pick_downstream(3, early[:, 3, :])
+        pick_downstream(0, 4, "picked0")
+        pick_downstream(4, 2, "bounded01")
+        late = keep.tile([P, 4 * 5 * BANK], U8, name="late", tag="bounded11", align_bytes=64)
+        for n, key in enumerate([("x", 0)] + [("w2", a, b) for a, b in units[1:]]):
+            place(key, late, n)
+        place(("x", 1), keep.tile([P, 5 * BANK], U8, name="x_q1", align_bytes=64), 0)
+        quantise_x(0)
         quantise_w2(1, 0)
-        quantise_x(1, 0)
-        pick_downstream(4, keep.tile([P, M], F32, name="down4", tag="x_bf01", align_bytes=64)[:])
-        quantise_x(1, 1)
-        pick_downstream(5, keep.tile([P, M], F32, name="down5", tag="x_bf11", align_bytes=64)[:])
+        quantise_x(1)
         quantise_w2(0, 1)
+        pick_downstream(6, 1, "x_bf1")
         quantise_w2(1, 1)
 
         y = [psum.tile([P, M], F32, name="y%d" % i, tag="bank") for i in range(TILES)]
         for b in range(PASSES):
             for a in range(PASSES):
-                for i in range(SLOTS * b, SLOTS * (b + 1)):
+                for t in range(SLOTS):
+                    codes, scales = operand["w2", a, b]
                     nc.tensor.matmul_mx(
-                        out=y[i][:],
-                        lhsT=w2_c[a][:, P * i : P * (i + 1)].bitcast(FP8X4),
-                        lhsT_scale=w2_sc[a][:, P * i : P * (i + 1)],
-                        rhs=x_c[a][:].bitcast(FP8X4),
-                        rhs_scale=x_sc[a][:],
+                        out=y[SLOTS * b + t][:],
+                        lhsT=codes[:, 4 * P * t : 4 * P * (t + 1)].bitcast(FP8X4),
+                        lhsT_scale=scales[:, P * t : P * (t + 1)],
+                        rhs=operand["x", a][0].bitcast(FP8X4),
+                        rhs_scale=operand["x", a][1],
                         start=(a == 0),
                         stop=(a == PASSES - 1),
                     )
@@ -265,25 +270,31 @@ def tile_list_creek_half_step_kernel(
             b, t = divmod(i, SLOTS)
             width = cols.stop - cols.start
             step_col = step_sb[:, b, t : t + 1]
-            res = keep.tile([P, width], F32, name="res%d" % n)
             if i in ON_GPSIMD:
-                scaled = ring.tile([P, width], F32, name="scaled")
+                res = keep.tile([P, width], F32, name="res%d" % n)
+                scaled = keep.tile([P, width], F32, name="scaled%d" % n)
                 nc.scalar.activation(scaled[:], rates[n][:], ACT.Copy, scale=step_col)
-                nc.gpsimd.tensor_tensor(res[:], scaled[:], down[i][:, cols], ALU.add)
+                nc.gpsimd.tensor_tensor(res[:, :], scaled[:], down[i][:, cols], ALU.add)
             else:
-                nc.vector.scalar_tensor_tensor(res[:], rates[n][:], step_col, down[i][:, cols], ALU.mult, ALU.add)
-            nc.sync.dma_start(out=out_rows[b, t][:, cols], in_=res[:])
+                res = held[:, M * i + cols.start - M * len(ON_GPSIMD) : M * i + cols.stop - M * len(ON_GPSIMD)]
+                nc.vector.scalar_tensor_tensor(res[:, :], rates[n][:], step_col, down[i][:, cols], ALU.mult, ALU.add)
+            nc.sync.dma_start(out=out_rows[b, t][:, cols], in_=res[:, :])
 
-        for n, (i, cols) in enumerate(pieces):
+        def add_and_bound(n):
+            i, cols = pieces[n]
             width = cols.stop - cols.start
-            moved = keep.tile([P, width], F32, name="moved%d" % n)
+            moved = keep.tile([P, width], F32, name="moved%d" % n, align_bytes=64)
             nc.vector.tensor_tensor(moved[:], y[i][:, cols], down[i][:, cols], ALU.add)
-            rate = ring.tile([P, width], F32, name="rate")
+            rate = keep.tile([P, width], F32, name="rate%d" % n)
             nc.scalar.activation(rate[:], moved[:], ACT.Tanh)
             rates.append(rate)
-            if n in (1, 3):
-                j = 6 + n // 2
-                pick_downstream(j, keep.tile([P, M], F32, name="down%d" % j, tag="moved%d" % (n - 1))[:])
-            if n > 0:
+
+        for n in range(len(pieces)):
+            add_and_bound(n)
+            if n == 2:
+                pick_downstream(7, 1, "moved1")
+            if n - 1 in ON_GPSIMD:
                 finish(n - 1)
-        finish(len(pieces) - 1)
+        held = keep.tile([P, M * (TILES - len(ON_GPSIMD))], F32, name="held", tag="scaled2")
+        for n in range(len(ON_GPSIMD), len(pieces)):
+            finish(n)

@@ -31,6 +31,7 @@ CAST_COLS = P // SLOTS
 
 
 ON_GPSIMD = (0, 1, 2)
+REP = 256
 
 
 def tile_list_creek_half_step_kernel(
@@ -56,8 +57,8 @@ def tile_list_creek_half_step_kernel(
 
         nc.vector.memset(w1_sc_raw[0:SC_ROW, :].bitcast(I32), 0)
         nc.vector.memset(tab_sc[0:SC_ROW, :].bitcast(I32), 0)
-        nc.vector.memset(w1_sc[:].bitcast(I32), 0)
-        nc.vector.memset(v_sc[:].bitcast(I32), 0)
+        nc.gpsimd.memset(w1_sc[:].bitcast(I32), 0)
+        nc.gpsimd.memset(v_sc[:].bitcast(I32), 0)
 
         def load_scale_rows(queue, tile, scales):
             queue.dma_start(out=tile[SC_ROW:P, :].bitcast(I32), in_=scales.bitcast(I32).rearrange("a q c -> q a c"))
@@ -114,22 +115,28 @@ def tile_list_creek_half_step_kernel(
             )
 
         gather_words(0, 0, "v_w00")
-        w1_c = keep.tile([P, PASSES * H * 2], U8, name="w1_c", align_bytes=64)
-        nc.vector.tensor_copy(
-            out=w1_c[:].bitcast(U16).rearrange("p (s t m) -> p s t m", t=SLOTS, m=P),
-            in_=w1_raw[:].bitcast(U16).rearrange("p (s m t) -> p s t m", t=SLOTS, m=P),
-        )
+        w1_c = [keep.tile([P, H * 2], U8, name="w1_c0", align_bytes=64)]
+
+        def order_w1(b, tile):
+            nc.vector.tensor_copy(
+                out=tile[:].bitcast(U16).rearrange("p (a t m) -> p a t m", t=SLOTS, m=P),
+                in_=w1_raw[:].bitcast(U16).rearrange("p (a b m t) -> p b a t m", a=PASSES, t=SLOTS, m=P)[:, b],
+            )
+
+        order_w1(0, w1_c[0])
+        gather_words(0, 1, "v_w01")
         gather_words(1, 0, "v_w10")
         gather_words(1, 1, "v_w11")
-        gather_words(0, 1, "w1_sc_raw")
+        w1_c.append(keep.tile([P, H * 2], U8, name="w1_c1", tag="w1_sc_raw", align_bytes=64))
+        order_w1(1, w1_c[1])
 
         units = [(a, b) for b in range(PASSES) for a in range(PASSES)]
         def load_w2(tile, a, b):
             rows = w2[BANK * a : BANK * (a + 1), BANK * b : BANK * (b + 1)]
             nc.sync.dma_start(out=tile, in_=rows.rearrange("(p t) n -> p t n", t=SLOTS))
 
-        w2_first = keep.tile([P, SLOTS, BANK], F32, name="w2_first", tag="w1_raw", align_bytes=64)
-        w2_rest = keep.tile([P, 3, SLOTS, BANK], F32, name="w2_rest", tag="tab_w0", align_bytes=64)
+        w2_first = keep.tile([P, SLOTS, BANK], F32, name="w2_first", tag="v_sc_raw", align_bytes=64)
+        w2_rest = keep.tile([P, 3, SLOTS, BANK], F32, name="w2_rest", tag="w1_raw", align_bytes=64)
         w2_in = {units[0]: w2_first[:]}
         for n, unit in enumerate(units[1:]):
             w2_in[unit] = w2_rest[:, n]
@@ -142,7 +149,6 @@ def tile_list_creek_half_step_kernel(
             first = 5 * BANK * n
             operand[key] = (tile[:, first : first + 4 * BANK], tile[:, first + 4 * BANK : first + 5 * BANK])
 
-        place(("w2", 0, 0), keep.tile([P, 5 * BANK], U8, name="w2_q00", align_bytes=64), 0)
         w2_bf = {}
 
         def cast_w2(copy, a, b, u, tag):
@@ -166,9 +172,10 @@ def tile_list_creek_half_step_kernel(
             acc = psum.tile([P, BANK], F32, name="acc", tag="bank")
             for a in range(PASSES):
                 col = H * a + P * i
+                word = BANK * a + P * (i % SLOTS)
                 nc.tensor.matmul_mx(
                     out=acc[:],
-                    lhsT=w1_c[:, 2 * col : 2 * (col + P)].bitcast(FP4X4),
+                    lhsT=w1_c[i // SLOTS][:, 2 * word : 2 * (word + P)].bitcast(FP4X4),
                     lhsT_scale=w1_sc[:, col : col + P],
                     rhs=v_w[a, c][:].bitcast(FP8X4),
                     rhs_scale=v_sc[:, S * a + BANK * c : S * a + BANK * (c + 1)],
@@ -191,9 +198,9 @@ def tile_list_creek_half_step_kernel(
                 ACT.Tanh,
             )
             nc.gpsimd.tensor_tensor(
-                x_bf[b][:, HALF * SLOTS * c : HALF * SLOTS * (c + 1)].rearrange("p (m t) -> p m t", t=SLOTS),
-                bounded[:].rearrange("p (m t) -> p m t", t=SLOTS),
-                gain_sb[:, b, :].unsqueeze(1).to_broadcast([P, HALF, SLOTS]),
+                x_bf[b][:, HALF * SLOTS * c : HALF * SLOTS * (c + 1)].rearrange("p (r e) -> p r e", e=REP),
+                bounded[:].rearrange("p (r e) -> p r e", e=REP),
+                gain_rep[:, b, :].unsqueeze(1).to_broadcast([P, HALF * SLOTS // REP, REP]),
                 ALU.mult,
             )
 
@@ -201,16 +208,18 @@ def tile_list_creek_half_step_kernel(
             nc.vector.quantize_mx(out=operand["x", b][0].bitcast(FP8X4), scales=operand["x", b][1], in_=x_bf[b][:])
 
         nc.sync.dma_start(out=gain_sb, in_=gain.rearrange("(b p t) -> p b t", b=PASSES, t=SLOTS))
+        gain_rep = keep.tile([P, PASSES, REP], F32, name="gain_rep")
+        nc.gpsimd.tensor_copy(
+            gain_rep[:].rearrange("p b (m t) -> p b m t", t=SLOTS),
+            gain_sb.unsqueeze(2).to_broadcast([P, PASSES, REP // SLOTS, SLOTS]),
+        )
         nc.sync.dma_start(out=step_sb, in_=step.rearrange("(b p t) -> p b t", b=PASSES, t=SLOTS))
 
-        for c in range(2):
-            for i in range(SLOTS):
+        for i in range(SLOTS):
+            for c in range(2):
                 first_product(i, c)
-        for u in range(SLOTS):
-            cast_w2(nc.vector.tensor_copy, 0, 0, u, "w2_bf00")
         for i in range(SLOTS):
             pick_upstream(i)
-        quantise_w2(0, 0)
         for i in range(SLOTS, TILES):
             if i == TILES - 2:
                 make_x(0, 0)
@@ -218,11 +227,12 @@ def tile_list_creek_half_step_kernel(
                 first_product(i, c)
             pick_upstream(i)
         make_x(0, 1)
-        for c in range(2):
-            make_x(1, c)
-        for a, b in units[1:]:
-            for u in range(SLOTS):
-                cast_w2(nc.scalar.copy, a, b, u, "w2_bf%d%d" % (a, b))
+        casts = [(a, b, u) for a, b in units for u in range(SLOTS)]
+        for n, (a, b, u) in enumerate(casts):
+            if n == 2:
+                for c in range(2):
+                    make_x(1, c)
+            cast_w2(nc.scalar.copy, a, b, u, "w2_bf%d%d" % (a, b))
 
         down = {}
 
@@ -234,10 +244,11 @@ def tile_list_creek_half_step_kernel(
 
         pick_downstream(0, 4, "picked0")
         pick_downstream(4, 2, "bounded01")
-        late = keep.tile([P, 4 * 5 * BANK], U8, name="late", tag="bounded11", align_bytes=64)
-        for n, key in enumerate([("x", 0)] + [("w2", a, b) for a, b in units[1:]]):
+        late = keep.tile([P, 5 * 5 * BANK], U8, name="late", tag="bounded11", align_bytes=64)
+        for n, key in enumerate([("x", 0)] + [("w2", a, b) for a, b in units]):
             place(key, late, n)
         place(("x", 1), keep.tile([P, 5 * BANK], U8, name="x_q1", align_bytes=64), 0)
+        quantise_w2(0, 0)
         quantise_x(0)
         quantise_w2(1, 0)
         quantise_x(1)

@@ -26,11 +26,9 @@ PER_COLUMN = 16
 HALF = M // 2
 SC_ROW = 96
 W1_WORDS = PASSES * H // 2
-W1_SCALES = PASSES * H // 4
 CAST_COLS = P // SLOTS
-
-
-ON_GPSIMD = (0, 1, 2)
+EARLY = 2
+ON_GPSIMD = 3
 REP = 256
 
 
@@ -41,27 +39,29 @@ def tile_list_creek_half_step_kernel(
     with ExitStack() as ctx:
         lists = ctx.enter_context(tc.tile_pool(name="lists", bufs=1))
         keep = ctx.enter_context(tc.tile_pool(name="keep", bufs=1))
-        ring = ctx.enter_context(tc.tile_pool(name="ring", bufs=3))
-        psum = ctx.enter_context(tc.psum_pool(name="psum", bufs=8))
+        psum = ctx.enter_context(tc.psum_pool(name="psum", bufs=1))
 
         offs_sb = lists.tile([P, S // PER_COLUMN], U16, name="offs_sb")
         pos1_sb = lists.tile([P, M // PER_COLUMN], U16, name="pos1_sb")
         pos2_sb = lists.tile([P, M // PER_COLUMN], U16, name="pos2_sb")
 
-        tab_sc = keep.tile([P, T], U8, name="tab_sc", align_bytes=64)
-        w1_sc_raw = keep.tile([P, H], U8, name="w1_sc_raw", align_bytes=64)
-        w1_sc_ord = keep.tile([P, H], U8, name="w1_sc_ord", align_bytes=64)
-        w1_sc = keep.tile([P, PASSES * H], U8, name="w1_sc", align_bytes=64)
-        v_sc_raw = keep.tile([P, S], U8, name="v_sc_raw", align_bytes=64)
-        v_sc = keep.tile([P, PASSES * S], U8, name="v_sc", align_bytes=64)
+        def tile(shape, dtype, name, after=None):
+            return keep.tile(shape, dtype, name=name, tag=after or name, align_bytes=64)
+
+        tab_sc = tile([P, T], U8, "tab_sc")
+        w1_sc_raw = tile([P, H], U8, "w1_sc_raw")
+        w1_sc_ord = tile([P, H], U8, "w1_sc_ord")
+        w1_sc = tile([P, PASSES * H], U8, "w1_sc")
+        v_sc_raw = tile([P, S], U8, "v_sc_raw")
+        v_sc = tile([P, PASSES * S], U8, "v_sc")
 
         nc.vector.memset(w1_sc_raw[0:SC_ROW, :].bitcast(I32), 0)
         nc.vector.memset(tab_sc[0:SC_ROW, :].bitcast(I32), 0)
-        nc.gpsimd.memset(w1_sc[:].bitcast(I32), 0)
-        nc.gpsimd.memset(v_sc[:].bitcast(I32), 0)
+        nc.vector.memset(w1_sc[:].bitcast(I32), 0)
+        nc.vector.memset(v_sc[:].bitcast(I32), 0)
 
-        def load_scale_rows(queue, tile, scales):
-            queue.dma_start(out=tile[SC_ROW:P, :].bitcast(I32), in_=scales.bitcast(I32).rearrange("a q c -> q a c"))
+        def load_scale_rows(queue, rows, scales):
+            queue.dma_start(out=rows[SC_ROW:P, :].bitcast(I32), in_=scales.bitcast(I32).rearrange("a q c -> q a c"))
 
         def move_scale_rows(queue, plane, rows):
             for q in range(QUADRANTS):
@@ -73,8 +73,8 @@ def tile_list_creek_half_step_kernel(
 
         tab_w = []
 
-        def load_table_words(queue, a, tag):
-            tab_w.append(keep.tile([P, T], U32, name="tab_w%d" % a, tag=tag, align_bytes=64))
+        def load_table_words(queue, a, after):
+            tab_w.append(tile([P, T], U32, "tab_w%d" % a, after))
             queue.dma_start(
                 out=tab_w[a][:].bitcast(I32), in_=tab_words[a].rearrange("p t i -> p (t i)").bitcast(I32)
             )
@@ -84,8 +84,8 @@ def tile_list_creek_half_step_kernel(
         load_scale_rows(nc.sync, tab_sc, tab_scales)
         nc.sync.dma_start(pos1_sb[:], pos1)
         nc.sync.dma_start(pos2_sb[:], pos2)
-        load_table_words(nc.sync, 0, "tab_w0")
-        w1_raw = keep.tile([P, W1_WORDS], I32, name="w1_raw", align_bytes=64)
+        load_table_words(nc.sync, 0, None)
+        w1_raw = tile([P, W1_WORDS], I32, "w1_raw")
         nc.sync.dma_start(
             out=w1_raw[:].rearrange("p (a c) -> p a c", a=PASSES),
             in_=w1_words.bitcast(I32).rearrange("a p c -> p a c"),
@@ -101,175 +101,162 @@ def tile_list_creek_half_step_kernel(
         nc.vector.tensor_copy(v_sc_raw[:], tab_sc[:].indirect(offs_sb[:]))
         move_scale_rows(nc.sync, v_sc, v_sc_raw)
 
-        vectors = keep.tile([P, 2, PASSES, SLOTS], F32, name="vectors", tag="w1_sc_ord", align_bytes=64)
-        gain_sb = vectors[:, 0]
-        step_sb = vectors[:, 1]
+        w1_c = []
+        for b in range(PASSES):
+            w1_c.append(tile([P, H * 2], U8, "w1_c%d" % b))
+            nc.scalar.copy(
+                out=w1_c[b][:].bitcast(U16).rearrange("p (a t m) -> p a m t", t=SLOTS, m=P),
+                in_=w1_raw[:].bitcast(U16).rearrange("p (a b m t) -> p b a m t", a=PASSES, t=SLOTS, m=P)[:, b],
+            )
 
         v_w = {}
         list_cols = BANK // PER_COLUMN
-
-        def gather_words(a, c, tag):
-            v_w[a, c] = keep.tile([P, BANK], U32, name="v_w%d%d" % (a, c), tag=tag, align_bytes=64)
-            nc.vector.tensor_copy(
-                v_w[a, c][:], tab_w[a][:].indirect(offs_sb[:, list_cols * c : list_cols * (c + 1)])
-            )
-
-        gather_words(0, 0, "v_w00")
-        w1_c = [keep.tile([P, H * 2], U8, name="w1_c0", align_bytes=64)]
-
-        def order_w1(b, tile):
-            nc.vector.tensor_copy(
-                out=tile[:].bitcast(U16).rearrange("p (a t m) -> p a t m", t=SLOTS, m=P),
-                in_=w1_raw[:].bitcast(U16).rearrange("p (a b m t) -> p b a t m", a=PASSES, t=SLOTS, m=P)[:, b],
-            )
-
-        order_w1(0, w1_c[0])
-        gather_words(0, 1, "v_w01")
-        gather_words(1, 0, "v_w10")
-        gather_words(1, 1, "v_w11")
-        w1_c.append(keep.tile([P, H * 2], U8, name="w1_c1", tag="w1_sc_raw", align_bytes=64))
-        order_w1(1, w1_c[1])
+        for a in range(PASSES):
+            for c in range(2):
+                v_w[a, c] = tile([P, BANK], U32, "v_w%d%d" % (a, c))
+                nc.vector.tensor_copy(
+                    v_w[a, c][:], tab_w[a][:].indirect(offs_sb[:, list_cols * c : list_cols * (c + 1)])
+                )
 
         units = [(a, b) for b in range(PASSES) for a in range(PASSES)]
-        def load_w2(tile, a, b):
+        w2_in = {}
+        for (a, b), after in zip(units, ["tab_sc", "tab_w0", "w1_raw", "w1_sc_raw"]):
+            w2_in[a, b] = tile([P, SLOTS, BANK], F32, "w2_in%d%d" % (a, b), after)
             rows = w2[BANK * a : BANK * (a + 1), BANK * b : BANK * (b + 1)]
-            nc.sync.dma_start(out=tile, in_=rows.rearrange("(p t) n -> p t n", t=SLOTS))
+            nc.sync.dma_start(out=w2_in[a, b][:], in_=rows.rearrange("(p t) n -> p t n", t=SLOTS))
 
-        w2_first = keep.tile([P, SLOTS, BANK], F32, name="w2_first", tag="v_sc_raw", align_bytes=64)
-        w2_rest = keep.tile([P, 3, SLOTS, BANK], F32, name="w2_rest", tag="w1_raw", align_bytes=64)
-        w2_in = {units[0]: w2_first[:]}
-        for n, unit in enumerate(units[1:]):
-            w2_in[unit] = w2_rest[:, n]
-        for a, b in units:
-            load_w2(w2_in[a, b], a, b)
+        vectors = tile([P, 2, PASSES, SLOTS], F32, "vectors", "w1_sc_ord")
+        gain_sb = vectors[:, 0]
+        step_sb = vectors[:, 1]
+        nc.sync.dma_start(out=gain_sb, in_=gain.rearrange("(b p t) -> p b t", b=PASSES, t=SLOTS))
+        nc.sync.dma_start(out=step_sb, in_=step.rearrange("(b p t) -> p b t", b=PASSES, t=SLOTS))
+        gain_rep = tile([P, PASSES, REP], F32, "gain_rep")
+        nc.gpsimd.tensor_copy(
+            gain_rep[:].rearrange("p b (m t) -> p b m t", t=SLOTS),
+            gain_sb.unsqueeze(2).to_broadcast([P, PASSES, REP // SLOTS, SLOTS]),
+        )
 
-        operand = {}
+        w2_bf = {(a, b): tile([P, SLOTS * BANK], BF16, "w2_bf%d%d" % (a, b)) for a, b in units}
 
-        def place(key, tile, n):
-            first = 5 * BANK * n
-            operand[key] = (tile[:, first : first + 4 * BANK], tile[:, first + 4 * BANK : first + 5 * BANK])
-
-        w2_bf = {}
-
-        def cast_w2(copy, a, b, u, tag):
-            if u == 0:
-                w2_bf[a, b] = keep.tile([P, SLOTS * BANK], BF16, name="w2_bf%d%d" % (a, b), tag=tag, align_bytes=64)
-            part = slice(CAST_COLS * u, CAST_COLS * (u + 1))
-            copy(
-                out=w2_bf[a, b][:].rearrange("p (s m t) -> p m t s", s=SLOTS, t=SLOTS)[:, part],
-                in_=w2_in[a, b].rearrange("p t (m s) -> p m t s", s=SLOTS)[:, part],
+        def cast_on_gpsimd(a, b):
+            nc.gpsimd.tensor_scalar(
+                w2_bf[a, b][:].rearrange("p (s m t) -> p m s t", s=SLOTS, t=SLOTS),
+                w2_in[a, b][:].rearrange("p t (m s) -> p m s t", s=SLOTS),
+                1.0,
+                0.0,
+                ALU.mult,
+                ALU.add,
             )
 
-        def quantise_w2(a, b):
-            nc.vector.quantize_mx(
-                out=operand["w2", a, b][0].bitcast(FP8X4), scales=operand["w2", a, b][1], in_=w2_bf[a, b][:]
-            )
-
-        h = [keep.tile([P, S], F32, name="h%d" % i) for i in range(TILES)]
-        picked = [keep.tile([P, SLOTS, M], F32, name="picked%d" % b, align_bytes=64) for b in range(PASSES)]
-
-        def first_product(i, c):
-            acc = psum.tile([P, BANK], F32, name="acc", tag="bank")
-            for a in range(PASSES):
-                col = H * a + P * i
-                word = BANK * a + P * (i % SLOTS)
-                nc.tensor.matmul_mx(
-                    out=acc[:],
-                    lhsT=w1_c[i // SLOTS][:, 2 * word : 2 * (word + P)].bitcast(FP4X4),
-                    lhsT_scale=w1_sc[:, col : col + P],
-                    rhs=v_w[a, c][:].bitcast(FP8X4),
-                    rhs_scale=v_sc[:, S * a + BANK * c : S * a + BANK * (c + 1)],
-                    start=(a == 0),
-                    stop=(a == PASSES - 1),
+        def cast_on_scalar(a, b):
+            for u in range(2):
+                part = slice(64 * u, 64 * (u + 1))
+                nc.scalar.copy(
+                    out=w2_bf[a, b][:].rearrange("p (s m t) -> p m t s", s=SLOTS, t=SLOTS)[:, part],
+                    in_=w2_in[a, b][:].rearrange("p t (m s) -> p m t s", s=SLOTS)[:, part],
                 )
-            nc.scalar.activation(h[i][:, BANK * c : BANK * (c + 1)], acc[:], ACT.Copy)
+
+        cast_on_gpsimd(0, 0)
+        cast_on_gpsimd(1, 0)
+
+        h = [tile([P, S], F32, "h%d" % i) for i in range(TILES)]
+        picked = [tile([P, SLOTS, M], F32, "picked%d" % b) for b in range(PASSES)]
+
+        def first_product(i):
+            order = range(PASSES) if i < EARLY else reversed(range(PASSES))
+            order = list(order)
+            for c in range(2):
+                acc = psum.tile([P, BANK], F32, name="acc", tag="bank%d" % ((2 * i + c) % TILES))
+                for a in order:
+                    col = H * a + P * i
+                    word = BANK * a + P * (i % SLOTS)
+                    nc.tensor.matmul_mx(
+                        out=acc[:],
+                        lhsT=w1_c[i // SLOTS][:, 2 * word : 2 * (word + P)].bitcast(FP4X4),
+                        lhsT_scale=w1_sc[:, col : col + P],
+                        rhs=v_w[a, c][:].bitcast(FP8X4),
+                        rhs_scale=v_sc[:, S * a + BANK * c : S * a + BANK * (c + 1)],
+                        start=(a == order[0]),
+                        stop=(a == order[-1]),
+                    )
+                nc.scalar.activation(h[i][:, BANK * c : BANK * (c + 1)], acc[:], ACT.Copy)
 
         def pick_upstream(i):
             b, t = divmod(i, SLOTS)
             nc.vector.tensor_copy(picked[b][:, t, :], h[i][:].indirect(pos1_sb[:]))
 
-        x_bf = [keep.tile([P, M * SLOTS], BF16, name="x_bf%d" % b, align_bytes=64) for b in range(PASSES)]
+        down = {}
 
-        def make_x(b, c):
-            bounded = keep.tile([P, HALF * SLOTS], F32, name="bounded%d%d" % (b, c), align_bytes=64)
+        def pick_downstream(i, after):
+            down[i] = tile([P, M], F32, "down%d" % i, after)
+            nc.vector.tensor_copy(down[i][:], h[i][:].indirect(pos2_sb[:]))
+
+        x_bf = [tile([P, M * SLOTS], BF16, "x_bf%d" % b) for b in range(PASSES)]
+
+        def make_x(b, first, width):
+            bounded = tile([P, width * SLOTS], F32, "bounded%d_%d" % (b, first))
             nc.scalar.activation(
                 bounded[:].rearrange("p (g i t) -> p g t i", i=4, t=SLOTS),
-                picked[b][:, :, HALF * c : HALF * (c + 1)].rearrange("p t (g i) -> p g t i", i=4),
+                picked[b][:, :, first : first + width].rearrange("p t (g i) -> p g t i", i=4),
                 ACT.Tanh,
             )
             nc.gpsimd.tensor_tensor(
-                x_bf[b][:, HALF * SLOTS * c : HALF * SLOTS * (c + 1)].rearrange("p (r e) -> p r e", e=REP),
+                x_bf[b][:, SLOTS * first : SLOTS * (first + width)].rearrange("p (r e) -> p r e", e=REP),
                 bounded[:].rearrange("p (r e) -> p r e", e=REP),
-                gain_rep[:, b, :].unsqueeze(1).to_broadcast([P, HALF * SLOTS // REP, REP]),
+                gain_rep[:, b, :].unsqueeze(1).to_broadcast([P, width * SLOTS // REP, REP]),
                 ALU.mult,
             )
 
-        def quantise_x(b):
-            nc.vector.quantize_mx(out=operand["x", b][0].bitcast(FP8X4), scales=operand["x", b][1], in_=x_bf[b][:])
-
-        nc.sync.dma_start(out=gain_sb, in_=gain.rearrange("(b p t) -> p b t", b=PASSES, t=SLOTS))
-        gain_rep = keep.tile([P, PASSES, REP], F32, name="gain_rep")
-        nc.gpsimd.tensor_copy(
-            gain_rep[:].rearrange("p b (m t) -> p b m t", t=SLOTS),
-            gain_sb.unsqueeze(2).to_broadcast([P, PASSES, REP // SLOTS, SLOTS]),
-        )
-        nc.sync.dma_start(out=step_sb, in_=step.rearrange("(b p t) -> p b t", b=PASSES, t=SLOTS))
-
         for i in range(SLOTS):
-            for c in range(2):
-                first_product(i, c)
-        for i in range(SLOTS):
+            first_product(i)
             pick_upstream(i)
-        for i in range(SLOTS, TILES):
-            if i == TILES - 2:
-                make_x(0, 0)
-            for c in range(2):
-                first_product(i, c)
+        pick_downstream(3, None)
+        first_product(4)
+        pick_upstream(4)
+        pick_downstream(4, None)
+        make_x(0, 0, HALF)
+        first_product(5)
+        pick_upstream(5)
+        make_x(0, HALF, HALF)
+        for i in (6, 7):
+            first_product(i)
             pick_upstream(i)
-        make_x(0, 1)
-        casts = [(a, b, u) for a, b in units for u in range(SLOTS)]
-        for n, (a, b, u) in enumerate(casts):
-            if n == 2:
-                for c in range(2):
-                    make_x(1, c)
-            cast_w2(nc.scalar.copy, a, b, u, "w2_bf%d%d" % (a, b))
+        make_x(1, 0, P)
+        make_x(1, P, P)
+        make_x(1, HALF, HALF)
+        cast_on_scalar(0, 1)
+        cast_on_scalar(1, 1)
+        pick_downstream(7, None)
+        rest = tile([P, 4, M], F32, "rest", "h7")
+        for k, i in enumerate((0, 1, 2, 5)):
+            down[i] = rest[:, k]
+            nc.vector.tensor_copy(down[i], h[i][:].indirect(pos2_sb[:]))
 
-        down = {}
+        operand = {}
+        late = tile([P, 6 * 5 * BANK], U8, "late", "bounded1_256")
+        keys = [("x", 0), ("w2", 0, 0), ("x", 1), ("w2", 1, 0), ("w2", 0, 1), ("w2", 1, 1)]
+        for n, key in enumerate(keys):
+            first = 5 * BANK * n
+            codes, scales = late[:, first : first + 4 * BANK], late[:, first + 4 * BANK : first + 5 * BANK]
+            operand[key] = (codes, scales)
+            source = x_bf[key[1]] if key[0] == "x" else w2_bf[key[1:]]
+            nc.vector.quantize_mx(out=codes.bitcast(FP8X4), scales=scales, in_=source[:])
 
-        def pick_downstream(first, count, tag):
-            tile = keep.tile([P, count, M], F32, name="down%d" % first, tag=tag, align_bytes=64)
-            for k in range(count):
-                nc.vector.tensor_copy(tile[:, k, :], h[first + k][:].indirect(pos2_sb[:]))
-                down[first + k] = tile[:, k, :]
-
-        pick_downstream(0, 4, "picked0")
-        pick_downstream(4, 2, "bounded01")
-        late = keep.tile([P, 5 * 5 * BANK], U8, name="late", tag="bounded11", align_bytes=64)
-        for n, key in enumerate([("x", 0)] + [("w2", a, b) for a, b in units]):
-            place(key, late, n)
-        place(("x", 1), keep.tile([P, 5 * BANK], U8, name="x_q1", align_bytes=64), 0)
-        quantise_w2(0, 0)
-        quantise_x(0)
-        quantise_w2(1, 0)
-        quantise_x(1)
-        quantise_w2(0, 1)
-        pick_downstream(6, 1, "x_bf1")
-        quantise_w2(1, 1)
-
-        y = [psum.tile([P, M], F32, name="y%d" % i, tag="bank") for i in range(TILES)]
-        for b in range(PASSES):
-            for a in range(PASSES):
-                for t in range(SLOTS):
-                    codes, scales = operand["w2", a, b]
-                    nc.tensor.matmul_mx(
-                        out=y[SLOTS * b + t][:],
-                        lhsT=codes[:, 4 * P * t : 4 * P * (t + 1)].bitcast(FP8X4),
-                        lhsT_scale=scales[:, P * t : P * (t + 1)],
-                        rhs=operand["x", a][0].bitcast(FP8X4),
-                        rhs_scale=operand["x", a][1],
-                        start=(a == 0),
-                        stop=(a == PASSES - 1),
-                    )
+        y = [psum.tile([P, M], F32, name="y%d" % i, tag="bank%d" % i) for i in range(TILES)]
+        for i in range(TILES):
+            b, t = divmod(i, SLOTS)
+            order = list(range(PASSES) if i < 2 else reversed(range(PASSES)))
+            for a in order:
+                codes, scales = operand["w2", a, b]
+                nc.tensor.matmul_mx(
+                    out=y[i][:],
+                    lhsT=codes[:, 4 * P * t : 4 * P * (t + 1)].bitcast(FP8X4),
+                    lhsT_scale=scales[:, P * t : P * (t + 1)],
+                    rhs=operand["x", a][0].bitcast(FP8X4),
+                    rhs_scale=operand["x", a][1],
+                    start=(a == order[0]),
+                    stop=(a == order[-1]),
+                )
 
         last = TILES - 1
         out_rows = out.rearrange("(b p t) m -> b t p m", b=PASSES, t=SLOTS)
@@ -281,31 +268,31 @@ def tile_list_creek_half_step_kernel(
             b, t = divmod(i, SLOTS)
             width = cols.stop - cols.start
             step_col = step_sb[:, b, t : t + 1]
-            if i in ON_GPSIMD:
-                res = keep.tile([P, width], F32, name="res%d" % n)
-                scaled = keep.tile([P, width], F32, name="scaled%d" % n)
+            if i < ON_GPSIMD:
+                res = tile([P, width], F32, "res%d" % n)
+                scaled = tile([P, width], F32, "scaled%d" % n)
                 nc.scalar.activation(scaled[:], rates[n][:], ACT.Copy, scale=step_col)
                 nc.gpsimd.tensor_tensor(res[:, :], scaled[:], down[i][:, cols], ALU.add)
             else:
-                res = held[:, M * i + cols.start - M * len(ON_GPSIMD) : M * i + cols.stop - M * len(ON_GPSIMD)]
+                res = held[:, M * (i - ON_GPSIMD) + cols.start : M * (i - ON_GPSIMD) + cols.stop]
                 nc.vector.scalar_tensor_tensor(res[:, :], rates[n][:], step_col, down[i][:, cols], ALU.mult, ALU.add)
             nc.sync.dma_start(out=out_rows[b, t][:, cols], in_=res[:, :])
 
         def add_and_bound(n):
             i, cols = pieces[n]
             width = cols.stop - cols.start
-            moved = keep.tile([P, width], F32, name="moved%d" % n, align_bytes=64)
+            moved = tile([P, width], F32, "moved%d" % n)
             nc.vector.tensor_tensor(moved[:], y[i][:, cols], down[i][:, cols], ALU.add)
-            rate = keep.tile([P, width], F32, name="rate%d" % n)
+            rate = tile([P, width], F32, "rate%d" % n)
             nc.scalar.activation(rate[:], moved[:], ACT.Tanh)
             rates.append(rate)
 
         for n in range(len(pieces)):
             add_and_bound(n)
-            if n == 2:
-                pick_downstream(7, 1, "moved1")
-            if n - 1 in ON_GPSIMD:
-                finish(n - 1)
-        held = keep.tile([P, M * (TILES - len(ON_GPSIMD))], F32, name="held", tag="scaled2")
-        for n in range(len(ON_GPSIMD), len(pieces)):
+            if n == 1:
+                pick_downstream(6, "moved0")
+            if n < ON_GPSIMD:
+                finish(n)
+        held = tile([P, M * (TILES - ON_GPSIMD)], F32, "held", "scaled%d" % (ON_GPSIMD - 1))
+        for n in range(ON_GPSIMD, len(pieces)):
             finish(n)

@@ -28,7 +28,7 @@ SC_ROW = 96
 W1_WORDS = PASSES * H // 2
 CAST_COLS = P // SLOTS
 EARLY = 2
-ON_GPSIMD = 3
+ON_GPSIMD = 4
 REP = 256
 
 
@@ -118,7 +118,7 @@ def tile_list_creek_half_step_kernel(
                     v_w[a, c][:], tab_w[a][:].indirect(offs_sb[:, list_cols * c : list_cols * (c + 1)])
                 )
 
-        units = [(a, b) for b in range(PASSES) for a in range(PASSES)]
+        units = [(a, b) for b in (1, 0) for a in range(PASSES)]
         w2_in = {}
         for (a, b), after in zip(units, ["tab_sc", "tab_w0", "w1_raw", "w1_sc_raw"]):
             w2_in[a, b] = tile([P, SLOTS, BANK], F32, "w2_in%d%d" % (a, b), after)
@@ -148,16 +148,8 @@ def tile_list_creek_half_step_kernel(
                 ALU.add,
             )
 
-        def cast_on_scalar(a, b):
-            for u in range(2):
-                part = slice(64 * u, 64 * (u + 1))
-                nc.scalar.copy(
-                    out=w2_bf[a, b][:].rearrange("p (s m t) -> p m t s", s=SLOTS, t=SLOTS)[:, part],
-                    in_=w2_in[a, b][:].rearrange("p t (m s) -> p m t s", s=SLOTS)[:, part],
-                )
-
-        cast_on_gpsimd(0, 0)
-        cast_on_gpsimd(1, 0)
+        for a, b in units[:3]:
+            cast_on_gpsimd(a, b)
 
         h = [tile([P, S], F32, "h%d" % i) for i in range(TILES)]
         picked = [tile([P, SLOTS, M], F32, "picked%d" % b) for b in range(PASSES)]
@@ -207,6 +199,15 @@ def tile_list_creek_half_step_kernel(
                 ALU.mult,
             )
 
+        both = tile([P, 2 * M * 2], BF16, "both")
+        pairs = [both[:, 2 * M * u : 2 * M * (u + 1)].rearrange("p (m e) -> p m e", e=2) for u in range(2)]
+
+        def scale_on_scalar(i):
+            b, t = divmod(i, SLOTS)
+            bounded = tile([P, M], F32, "bounded_t%d" % i)
+            nc.scalar.activation(bounded[:], picked[b][:, t, :], ACT.Tanh)
+            nc.scalar.activation(pairs[t // 2][:, :, t % 2], bounded[:], ACT.Copy, scale=gain_sb[:, b, t : t + 1])
+
         for i in range(SLOTS):
             first_product(i)
             pick_upstream(i)
@@ -216,25 +217,28 @@ def tile_list_creek_half_step_kernel(
         pick_downstream(4, None)
         make_x(0, 0, HALF)
         first_product(5)
-        pick_upstream(5)
         make_x(0, HALF, HALF)
-        for i in (6, 7):
-            first_product(i)
-            pick_upstream(i)
-        make_x(1, 0, P)
-        make_x(1, P, P)
-        make_x(1, HALF, HALF)
-        cast_on_scalar(0, 1)
-        cast_on_scalar(1, 1)
+        cast_on_gpsimd(*units[3])
+        pick_upstream(5)
+        pick_downstream(5, None)
+        first_product(6)
+        scale_on_scalar(4)
+        pick_upstream(6)
+        pick_downstream(6, None)
+        first_product(7)
+        scale_on_scalar(5)
+        pick_upstream(7)
+        scale_on_scalar(6)
+        scale_on_scalar(7)
         pick_downstream(7, None)
-        rest = tile([P, 4, M], F32, "rest", "h7")
-        for k, i in enumerate((0, 1, 2, 5)):
-            down[i] = rest[:, k]
-            nc.vector.tensor_copy(down[i], h[i][:].indirect(pos2_sb[:]))
+        nc.scalar.copy(
+            out=x_bf[1][:].bitcast(F32).rearrange("p (m u) -> p m u", u=2),
+            in_=both[:].bitcast(F32).rearrange("p (u m) -> p m u", u=2),
+        )
 
         operand = {}
-        late = tile([P, 6 * 5 * BANK], U8, "late", "bounded1_256")
-        keys = [("x", 0), ("w2", 0, 0), ("x", 1), ("w2", 1, 0), ("w2", 0, 1), ("w2", 1, 1)]
+        late = tile([P, 6 * 5 * BANK], U8, "late", "h7")
+        keys = [("w2", 0, 1), ("x", 0), ("w2", 1, 1), ("x", 1), ("w2", 0, 0), ("w2", 1, 0)]
         for n, key in enumerate(keys):
             first = 5 * BANK * n
             codes, scales = late[:, first : first + 4 * BANK], late[:, first + 4 * BANK : first + 5 * BANK]
@@ -242,10 +246,12 @@ def tile_list_creek_half_step_kernel(
             source = x_bf[key[1]] if key[0] == "x" else w2_bf[key[1:]]
             nc.vector.quantize_mx(out=codes.bitcast(FP8X4), scales=scales, in_=source[:])
 
-        y = [psum.tile([P, M], F32, name="y%d" % i, tag="bank%d" % i) for i in range(TILES)]
-        for i in range(TILES):
+        turn = [4, 5, 6, 7, 3, 0, 1, 2]
+        y = {}
+        for n, i in enumerate(turn):
             b, t = divmod(i, SLOTS)
-            order = list(range(PASSES) if i < 2 else reversed(range(PASSES)))
+            y[i] = psum.tile([P, M], F32, name="y%d" % i, tag="bank%d" % n)
+            order = list(range(PASSES) if n < SLOTS else reversed(range(PASSES)))
             for a in order:
                 codes, scales = operand["w2", a, b]
                 nc.tensor.matmul_mx(
@@ -258,9 +264,8 @@ def tile_list_creek_half_step_kernel(
                     stop=(a == order[-1]),
                 )
 
-        last = TILES - 1
         out_rows = out.rearrange("(b p t) m -> b t p m", b=PASSES, t=SLOTS)
-        pieces = [(i, slice(0, M)) for i in range(last)] + [(last, slice(0, HALF)), (last, slice(HALF, M))]
+        pieces = [(i, slice(0, M)) for i in turn[:-1]] + [(turn[-1], slice(0, HALF)), (turn[-1], slice(HALF, M))]
         rates = []
 
         def finish(n):
@@ -268,13 +273,14 @@ def tile_list_creek_half_step_kernel(
             b, t = divmod(i, SLOTS)
             width = cols.stop - cols.start
             step_col = step_sb[:, b, t : t + 1]
-            if i < ON_GPSIMD:
+            if n < ON_GPSIMD:
                 res = tile([P, width], F32, "res%d" % n)
                 scaled = tile([P, width], F32, "scaled%d" % n)
                 nc.scalar.activation(scaled[:], rates[n][:], ACT.Copy, scale=step_col)
                 nc.gpsimd.tensor_tensor(res[:, :], scaled[:], down[i][:, cols], ALU.add)
             else:
-                res = held[:, M * (i - ON_GPSIMD) + cols.start : M * (i - ON_GPSIMD) + cols.stop]
+                first = M * (min(n, TILES - 1) - ON_GPSIMD)
+                res = held[:, first + cols.start : first + cols.stop]
                 nc.vector.scalar_tensor_tensor(res[:, :], rates[n][:], step_col, down[i][:, cols], ALU.mult, ALU.add)
             nc.sync.dma_start(out=out_rows[b, t][:, cols], in_=res[:, :])
 
@@ -289,8 +295,8 @@ def tile_list_creek_half_step_kernel(
 
         for n in range(len(pieces)):
             add_and_bound(n)
-            if n == 1:
-                pick_downstream(6, "moved0")
+            if 1 <= n <= 3:
+                pick_downstream(n - 1, "moved%d" % (n - 1))
             if n < ON_GPSIMD:
                 finish(n)
         held = tile([P, M * (TILES - ON_GPSIMD)], F32, "held", "scaled%d" % (ON_GPSIMD - 1))

@@ -28,7 +28,7 @@ SC_ROW = 96
 W1_WORDS = PASSES * H // 2
 CAST_COLS = P // SLOTS
 EARLY = 2
-ON_GPSIMD = 4
+ON_GPSIMD = 5
 REP = 256
 
 
@@ -237,21 +237,26 @@ def tile_list_creek_half_step_kernel(
         )
 
         operand = {}
-        late = tile([P, 6 * 5 * BANK], U8, "late", "h7")
-        keys = [("w2", 0, 1), ("x", 0), ("w2", 1, 1), ("x", 1), ("w2", 0, 0), ("w2", 1, 0)]
-        for n, key in enumerate(keys):
-            first = 5 * BANK * n
-            codes, scales = late[:, first : first + 4 * BANK], late[:, first + 4 * BANK : first + 5 * BANK]
+
+        def quantise(key, place):
+            codes, scales = place[:, : 4 * BANK], place[:, 4 * BANK :]
             operand[key] = (codes, scales)
             source = x_bf[key[1]] if key[0] == "x" else w2_bf[key[1:]]
             nc.vector.quantize_mx(out=codes.bitcast(FP8X4), scales=scales, in_=source[:])
 
+        late = tile([P, 5 * 5 * BANK], U8, "late", "h7")
+        keys = [("w2", 0, 1), ("x", 0), ("w2", 1, 1), ("x", 1), ("w2", 0, 0)]
+        for n, key in enumerate(keys):
+            quantise(key, late[:, 5 * BANK * n : 5 * BANK * (n + 1)])
+
         turn = [4, 5, 6, 7, 3, 0, 1, 2]
         y = {}
-        for n, i in enumerate(turn):
+
+        def second_product(n):
+            i = turn[n]
             b, t = divmod(i, SLOTS)
             y[i] = psum.tile([P, M], F32, name="y%d" % i, tag="bank%d" % n)
-            order = list(range(PASSES) if n < SLOTS else reversed(range(PASSES)))
+            order = list(range(PASSES) if n < 2 else reversed(range(PASSES)))
             for a in order:
                 codes, scales = operand["w2", a, b]
                 nc.tensor.matmul_mx(
@@ -263,6 +268,9 @@ def tile_list_creek_half_step_kernel(
                     start=(a == order[0]),
                     stop=(a == order[-1]),
                 )
+
+        for n in range(SLOTS):
+            second_product(n)
 
         out_rows = out.rearrange("(b p t) m -> b t p m", b=PASSES, t=SLOTS)
         pieces = [(i, slice(0, M)) for i in turn[:-1]] + [(turn[-1], slice(0, HALF)), (turn[-1], slice(HALF, M))]
@@ -295,8 +303,12 @@ def tile_list_creek_half_step_kernel(
 
         for n in range(len(pieces)):
             add_and_bound(n)
-            if 1 <= n <= 3:
-                pick_downstream(n - 1, "moved%d" % (n - 1))
+            if n == 1:
+                quantise(("w2", 1, 0), tile([P, 5 * BANK], U8, "w2_q_last", "moved0")[:])
+                for later in range(SLOTS, TILES):
+                    second_product(later)
+            if 3 <= n <= 5:
+                pick_downstream(n - 3, "moved%d" % (n - 2))
             if n < ON_GPSIMD:
                 finish(n)
         held = tile([P, M * (TILES - ON_GPSIMD)], F32, "held", "scaled%d" % (ON_GPSIMD - 1))

@@ -136,7 +136,7 @@ def tile_list_creek_half_step_kernel(
             gain_sb.unsqueeze(2).to_broadcast([P, PASSES, REP // SLOTS, SLOTS]),
         )
 
-        w2_bf = {(a, b): tile([P, SLOTS * BANK], BF16, "w2_bf%d%d" % (a, b)) for a, b in units}
+        w2_bf = {(a, b): tile([P, SLOTS * BANK], BF16, "w2_bf%d%d" % (a, b)) for a, b in units[:3]}
 
         def cast_on_gpsimd(a, b):
             nc.gpsimd.tensor_scalar(
@@ -218,7 +218,6 @@ def tile_list_creek_half_step_kernel(
         make_x(0, 0, HALF)
         first_product(5)
         make_x(0, HALF, HALF)
-        cast_on_gpsimd(*units[3])
         pick_upstream(5)
         pick_downstream(5, None)
         first_product(6)
@@ -234,6 +233,11 @@ def tile_list_creek_half_step_kernel(
         nc.scalar.copy(
             out=x_bf[1][:].bitcast(F32).rearrange("p (m u) -> p m u", u=2),
             in_=both[:].bitcast(F32).rearrange("p (u m) -> p m u", u=2),
+        )
+        w2_bf[units[3]] = tile([P, SLOTS * BANK], BF16, "w2_bf_last", "both")
+        nc.scalar.copy(
+            out=w2_bf[units[3]][:].rearrange("p (s m t) -> p m t s", s=SLOTS, t=SLOTS),
+            in_=w2_in[units[3]][:].rearrange("p t (m s) -> p m t s", s=SLOTS),
         )
 
         operand = {}

@@ -25,9 +25,6 @@ QUADRANTS = 4
 PER_COLUMN = 16
 HALF = M // 2
 SC_ROW = 96
-W1_WORDS = PASSES * H // 2
-CAST_COLS = P // SLOTS
-EARLY = 2
 ON_GPSIMD = 5
 REP = 256
 
@@ -49,65 +46,80 @@ def tile_list_creek_half_step_kernel(
             return keep.tile(shape, dtype, name=name, tag=after or name, align_bytes=64)
 
         tab_sc = tile([P, T], U8, "tab_sc")
-        w1_sc_raw = tile([P, H], U8, "w1_sc_raw")
-        w1_sc_ord = tile([P, H], U8, "w1_sc_ord")
-        w1_sc = tile([P, PASSES * H], U8, "w1_sc")
+        w1_sc_raw = tile([P, PASSES * H], U8, "w1_sc_raw")
         v_sc_raw = tile([P, S], U8, "v_sc_raw")
         v_sc = tile([P, PASSES * S], U8, "v_sc")
+        gain_in = tile([P, PASSES, SLOTS], F32, "gain_in")
 
-        nc.vector.memset(w1_sc_raw[0:SC_ROW, :].bitcast(I32), 0)
+        nc.vector.memset(w1_sc_raw[:].bitcast(I32), 0)
         nc.vector.memset(tab_sc[0:SC_ROW, :].bitcast(I32), 0)
-        nc.vector.memset(w1_sc[:].bitcast(I32), 0)
         nc.vector.memset(v_sc[:].bitcast(I32), 0)
-
-        def load_scale_rows(queue, rows, scales):
-            queue.dma_start(out=rows[SC_ROW:P, :].bitcast(I32), in_=scales.bitcast(I32).rearrange("a q c -> q a c"))
-
-        def move_scale_rows(queue, plane, rows):
-            for q in range(QUADRANTS):
-                first = SC_ROW + 4 * PASSES * q
-                queue.dma_start(
-                    out=plane[32 * q : 32 * q + 4, :].bitcast(I32).rearrange("r (a c) -> r a c", a=PASSES),
-                    in_=rows[first : first + 4 * PASSES, :].bitcast(I32),
-                )
 
         tab_w = []
 
-        def load_table_words(queue, a, after):
+        def load_table_words(a, after):
             tab_w.append(tile([P, T], U32, "tab_w%d" % a, after))
-            queue.dma_start(
+            nc.sync.dma_start(
                 out=tab_w[a][:].bitcast(I32), in_=tab_words[a].rearrange("p t i -> p (t i)").bitcast(I32)
             )
 
-        load_scale_rows(nc.scalar, w1_sc_raw, w1_scales)
+        w1_raw = []
+
+        def load_w1_words(queue, b, after):
+            w1_raw.append(tile([P, PASSES * BANK // 2], I32, "w1_raw%d" % b, after))
+            queue.dma_start(
+                out=w1_raw[b][:].rearrange("p (a c) -> p a c", a=PASSES),
+                in_=w1_words.bitcast(I32).rearrange("a p (b c) -> b p a c", b=PASSES)[b],
+            )
+
         nc.sync.dma_start(offs_sb[:], offs)
-        load_scale_rows(nc.sync, tab_sc, tab_scales)
+        nc.sync.dma_start(
+            out=tab_sc[SC_ROW:P, :].bitcast(I32), in_=tab_scales.bitcast(I32).rearrange("a q c -> q a c")
+        )
+        nc.sync.dma_start(out=gain_in[:], in_=gain.rearrange("(b p t) -> p b t", b=PASSES, t=SLOTS))
+        for q in range(QUADRANTS):
+            nc.sync.dma_start(
+                out=w1_sc_raw[32 * q : 32 * q + 4, :].bitcast(I32).rearrange("r (a c) -> r a c", a=PASSES),
+                in_=w1_scales.bitcast(I32)[:, 4 * q : 4 * q + 4, :].rearrange("a r c -> r a c"),
+            )
+        load_table_words(0, None)
+        load_w1_words(nc.sync, 0, None)
+        load_table_words(1, None)
         nc.sync.dma_start(pos1_sb[:], pos1)
         nc.sync.dma_start(pos2_sb[:], pos2)
-        load_table_words(nc.sync, 0, None)
-        w1_raw = tile([P, W1_WORDS], I32, "w1_raw")
-        nc.sync.dma_start(
-            out=w1_raw[:].rearrange("p (a c) -> p a c", a=PASSES),
-            in_=w1_words.bitcast(I32).rearrange("a p c -> p a c"),
-        )
 
-        nc.vector.tensor_copy(
-            out=w1_sc_ord[:].rearrange("p (b t m) -> p b t m", t=SLOTS, m=P),
-            in_=w1_sc_raw[:].rearrange("p (b m t) -> p b t m", t=SLOTS, m=P),
+        gain_rep = tile([P, PASSES, REP], F32, "gain_rep")
+        nc.scalar.activation(
+            gain_rep[:].rearrange("p b (m t) -> p b m t", t=SLOTS),
+            gain_in[:].unsqueeze(2).to_broadcast([P, PASSES, REP // SLOTS, SLOTS]),
+            ACT.Copy,
         )
-        move_scale_rows(nc.scalar, w1_sc, w1_sc_ord)
-        load_table_words(nc.scalar, 1, "w1_sc_raw")
 
         nc.vector.tensor_copy(v_sc_raw[:], tab_sc[:].indirect(offs_sb[:]))
-        move_scale_rows(nc.sync, v_sc, v_sc_raw)
+        for q in range(QUADRANTS):
+            first = SC_ROW + 4 * PASSES * q
+            nc.scalar.dma_start(
+                out=v_sc[32 * q : 32 * q + 4, :].bitcast(I32).rearrange("r (a c) -> r a c", a=PASSES),
+                in_=v_sc_raw[first : first + 4 * PASSES, :].bitcast(I32),
+            )
+        load_w1_words(nc.scalar, 1, "tab_sc")
 
-        w1_c = []
-        for b in range(PASSES):
+        w1_c, w1_sc = [], []
+
+        def order_w1(b):
+            w1_sc.append(tile([P, PASSES * BANK], U8, "w1_sc%d" % b))
+            nc.gpsimd.tensor_copy(
+                out=w1_sc[b][:].rearrange("p (a t m) -> p a t m", t=SLOTS, m=P),
+                in_=w1_sc_raw[:].rearrange("p (a b m t) -> p b a t m", a=PASSES, t=SLOTS, m=P)[:, b],
+            )
             w1_c.append(tile([P, H * 2], U8, "w1_c%d" % b))
             nc.scalar.copy(
                 out=w1_c[b][:].bitcast(U16).rearrange("p (a t m) -> p a m t", t=SLOTS, m=P),
-                in_=w1_raw[:].bitcast(U16).rearrange("p (a b m t) -> p b a m t", a=PASSES, t=SLOTS, m=P)[:, b],
+                in_=w1_raw[b][:].bitcast(U16).rearrange("p (a m t) -> p a m t", t=SLOTS, m=P),
             )
+
+        order_w1(0)
+        order_w1(1)
 
         v_w = {}
         list_cols = BANK // PER_COLUMN
@@ -120,25 +132,17 @@ def tile_list_creek_half_step_kernel(
 
         units = [(a, b) for b in (1, 0) for a in range(PASSES)]
         w2_in = {}
-        for (a, b), after in zip(units, ["tab_sc", "tab_w0", "w1_raw", "w1_sc_raw"]):
+        for (a, b), after in zip(units, ["w1_raw0", "tab_w0", "w1_sc_raw", "tab_sc"]):
             w2_in[a, b] = tile([P, SLOTS, BANK], F32, "w2_in%d%d" % (a, b), after)
             rows = w2[BANK * a : BANK * (a + 1), BANK * b : BANK * (b + 1)]
             nc.sync.dma_start(out=w2_in[a, b][:], in_=rows.rearrange("(p t) n -> p t n", t=SLOTS))
 
-        vectors = tile([P, 2, PASSES, SLOTS], F32, "vectors", "w1_sc_ord")
-        gain_sb = vectors[:, 0]
-        step_sb = vectors[:, 1]
-        nc.sync.dma_start(out=gain_sb, in_=gain.rearrange("(b p t) -> p b t", b=PASSES, t=SLOTS))
-        nc.sync.dma_start(out=step_sb, in_=step.rearrange("(b p t) -> p b t", b=PASSES, t=SLOTS))
-        gain_rep = tile([P, PASSES, REP], F32, "gain_rep")
-        nc.gpsimd.tensor_copy(
-            gain_rep[:].rearrange("p b (m t) -> p b m t", t=SLOTS),
-            gain_sb.unsqueeze(2).to_broadcast([P, PASSES, REP // SLOTS, SLOTS]),
-        )
+        step_sb = tile([P, PASSES, SLOTS], F32, "step_sb", "v_sc_raw")
+        nc.sync.dma_start(out=step_sb[:], in_=step.rearrange("(b p t) -> p b t", b=PASSES, t=SLOTS))
 
         w2_bf = {(a, b): tile([P, SLOTS * BANK], BF16, "w2_bf%d%d" % (a, b)) for a, b in units[:3]}
 
-        def cast_on_gpsimd(a, b):
+        for a, b in units[:3]:
             nc.gpsimd.tensor_scalar(
                 w2_bf[a, b][:].rearrange("p (s m t) -> p m s t", s=SLOTS, t=SLOTS),
                 w2_in[a, b][:].rearrange("p t (m s) -> p m s t", s=SLOTS),
@@ -148,30 +152,29 @@ def tile_list_creek_half_step_kernel(
                 ALU.add,
             )
 
-        for a, b in units[:3]:
-            cast_on_gpsimd(a, b)
-
         h = [tile([P, S], F32, "h%d" % i) for i in range(TILES)]
         picked = [tile([P, SLOTS, M], F32, "picked%d" % b) for b in range(PASSES)]
 
         def first_product(i):
-            order = range(PASSES) if i < EARLY else reversed(range(PASSES))
-            order = list(order)
+            b, t = divmod(i, SLOTS)
+            order = list(range(PASSES) if i < 2 else reversed(range(PASSES)))
             for c in range(2):
                 acc = psum.tile([P, BANK], F32, name="acc", tag="bank%d" % ((2 * i + c) % TILES))
                 for a in order:
-                    col = H * a + P * i
-                    word = BANK * a + P * (i % SLOTS)
+                    col = BANK * a + P * t
                     nc.tensor.matmul_mx(
                         out=acc[:],
-                        lhsT=w1_c[i // SLOTS][:, 2 * word : 2 * (word + P)].bitcast(FP4X4),
-                        lhsT_scale=w1_sc[:, col : col + P],
+                        lhsT=w1_c[b][:, 2 * col : 2 * (col + P)].bitcast(FP4X4),
+                        lhsT_scale=w1_sc[b][:, col : col + P],
                         rhs=v_w[a, c][:].bitcast(FP8X4),
                         rhs_scale=v_sc[:, S * a + BANK * c : S * a + BANK * (c + 1)],
                         start=(a == order[0]),
                         stop=(a == order[-1]),
                     )
-                nc.scalar.activation(h[i][:, BANK * c : BANK * (c + 1)], acc[:], ACT.Copy)
+                if (i, c) == (0, 1):
+                    nc.vector.tensor_copy(h[i][:, BANK * c : BANK * (c + 1)], acc[:])
+                else:
+                    nc.scalar.activation(h[i][:, BANK * c : BANK * (c + 1)], acc[:], ACT.Copy)
 
         def pick_upstream(i):
             b, t = divmod(i, SLOTS)
@@ -199,14 +202,22 @@ def tile_list_creek_half_step_kernel(
                 ALU.mult,
             )
 
-        both = tile([P, 2 * M * 2], BF16, "both")
-        pairs = [both[:, 2 * M * u : 2 * M * (u + 1)].rearrange("p (m e) -> p m e", e=2) for u in range(2)]
+        gained = tile([P, SLOTS, M], F32, "gained")
 
-        def scale_on_scalar(i):
+        def scale_on_scalar(i, cols):
             b, t = divmod(i, SLOTS)
-            bounded = tile([P, M], F32, "bounded_t%d" % i)
-            nc.scalar.activation(bounded[:], picked[b][:, t, :], ACT.Tanh)
-            nc.scalar.activation(pairs[t // 2][:, :, t % 2], bounded[:], ACT.Copy, scale=gain_sb[:, b, t : t + 1])
+            bounded = tile([P, cols.stop - cols.start], F32, "bounded_t%d_%d" % (i, cols.start))
+            nc.scalar.activation(bounded[:], picked[b][:, t, cols], ACT.Tanh)
+            nc.scalar.activation(gained[:, t, cols], bounded[:], ACT.Copy, scale=gain_rep[:, b, t : t + 1])
+
+        def woven(cols):
+            part = x_bf[1][:, SLOTS * cols.start : SLOTS * cols.stop]
+            return (
+                part.rearrange("p (m t) -> p m t", t=SLOTS),
+                gained[:, :, cols].rearrange("p t m -> p m t"),
+            )
+
+        whole, low, high = slice(0, M), slice(0, HALF), slice(HALF, M)
 
         for i in range(SLOTS):
             first_product(i)
@@ -221,20 +232,19 @@ def tile_list_creek_half_step_kernel(
         pick_upstream(5)
         pick_downstream(5, None)
         first_product(6)
-        scale_on_scalar(4)
+        scale_on_scalar(4, whole)
         pick_upstream(6)
-        pick_downstream(6, None)
         first_product(7)
-        scale_on_scalar(5)
+        scale_on_scalar(5, whole)
         pick_upstream(7)
-        scale_on_scalar(6)
-        scale_on_scalar(7)
+        scale_on_scalar(6, whole)
+        scale_on_scalar(7, low)
+        nc.gpsimd.tensor_scalar(*woven(low), 1.0, 0.0, ALU.mult, ALU.add)
+        scale_on_scalar(7, high)
         pick_downstream(7, None)
-        nc.scalar.copy(
-            out=x_bf[1][:].bitcast(F32).rearrange("p (m u) -> p m u", u=2),
-            in_=both[:].bitcast(F32).rearrange("p (u m) -> p m u", u=2),
-        )
-        w2_bf[units[3]] = tile([P, SLOTS * BANK], BF16, "w2_bf_last", "both")
+        pick_downstream(6, "bounded_t5_0")
+        nc.scalar.copy(*woven(high))
+        w2_bf[units[3]] = tile([P, SLOTS * BANK], BF16, "w2_bf_last", "gained")
         nc.scalar.copy(
             out=w2_bf[units[3]][:].rearrange("p (s m t) -> p m t s", s=SLOTS, t=SLOTS),
             in_=w2_in[units[3]][:].rearrange("p t (m s) -> p m t s", s=SLOTS),
@@ -248,7 +258,7 @@ def tile_list_creek_half_step_kernel(
             source = x_bf[key[1]] if key[0] == "x" else w2_bf[key[1:]]
             nc.vector.quantize_mx(out=codes.bitcast(FP8X4), scales=scales, in_=source[:])
 
-        late = tile([P, 5 * 5 * BANK], U8, "late", "h7")
+        late = tile([P, 5 * 5 * BANK], U8, "late", "h6")
         keys = [("w2", 0, 1), ("x", 0), ("w2", 1, 1), ("x", 1), ("w2", 0, 0)]
         for n, key in enumerate(keys):
             quantise(key, late[:, 5 * BANK * n : 5 * BANK * (n + 1)])
@@ -286,7 +296,7 @@ def tile_list_creek_half_step_kernel(
             width = cols.stop - cols.start
             step_col = step_sb[:, b, t : t + 1]
             if n < ON_GPSIMD:
-                res = tile([P, width], F32, "res%d" % n)
+                res = tile([P, width], F32, "res%d" % n, "gained" if n == 0 else None)
                 scaled = tile([P, width], F32, "scaled%d" % n)
                 nc.scalar.activation(scaled[:], rates[n][:], ACT.Copy, scale=step_col)
                 nc.gpsimd.tensor_tensor(res[:, :], scaled[:], down[i][:, cols], ALU.add)
@@ -307,8 +317,8 @@ def tile_list_creek_half_step_kernel(
 
         for n in range(len(pieces)):
             add_and_bound(n)
-            if n == 1:
-                quantise(("w2", 1, 0), tile([P, 5 * BANK], U8, "w2_q_last", "moved0")[:])
+            if n == 0:
+                quantise(("w2", 1, 0), tile([P, 5 * BANK], U8, "w2_q_last")[:])
                 for later in range(SLOTS, TILES):
                     second_product(later)
             if 3 <= n <= 5:

@@ -202,22 +202,14 @@ def tile_list_creek_half_step_kernel(
                 ALU.mult,
             )
 
-        gained = tile([P, SLOTS, M], F32, "gained")
+        both = tile([P, 2 * M * 2], BF16, "both")
+        pairs = [both[:, 2 * M * u : 2 * M * (u + 1)].rearrange("p (m e) -> p m e", e=2) for u in range(2)]
 
-        def scale_on_scalar(i, cols):
+        def scale_on_scalar(i):
             b, t = divmod(i, SLOTS)
-            bounded = tile([P, cols.stop - cols.start], F32, "bounded_t%d_%d" % (i, cols.start))
-            nc.scalar.activation(bounded[:], picked[b][:, t, cols], ACT.Tanh)
-            nc.scalar.activation(gained[:, t, cols], bounded[:], ACT.Copy, scale=gain_rep[:, b, t : t + 1])
-
-        def woven(cols):
-            part = x_bf[1][:, SLOTS * cols.start : SLOTS * cols.stop]
-            return (
-                part.rearrange("p (m t) -> p m t", t=SLOTS),
-                gained[:, :, cols].rearrange("p t m -> p m t"),
-            )
-
-        whole, low, high = slice(0, M), slice(0, HALF), slice(HALF, M)
+            bounded = tile([P, M], F32, "bounded_t%d" % i)
+            nc.scalar.activation(bounded[:], picked[b][:, t, :], ACT.Tanh)
+            nc.scalar.activation(pairs[t // 2][:, :, t % 2], bounded[:], ACT.Copy, scale=gain_rep[:, b, t : t + 1])
 
         for i in range(SLOTS):
             first_product(i)
@@ -232,19 +224,20 @@ def tile_list_creek_half_step_kernel(
         pick_upstream(5)
         pick_downstream(5, None)
         first_product(6)
-        scale_on_scalar(4, whole)
+        scale_on_scalar(4)
         pick_upstream(6)
         first_product(7)
-        scale_on_scalar(5, whole)
+        scale_on_scalar(5)
         pick_upstream(7)
-        scale_on_scalar(6, whole)
-        scale_on_scalar(7, low)
-        nc.gpsimd.tensor_scalar(*woven(low), 1.0, 0.0, ALU.mult, ALU.add)
-        scale_on_scalar(7, high)
+        scale_on_scalar(6)
+        scale_on_scalar(7)
         pick_downstream(7, None)
-        pick_downstream(6, "bounded_t5_0")
-        nc.scalar.copy(*woven(high))
-        w2_bf[units[3]] = tile([P, SLOTS * BANK], BF16, "w2_bf_last", "gained")
+        pick_downstream(6, "bounded_t5")
+        nc.scalar.copy(
+            out=x_bf[1][:].bitcast(F32).rearrange("p (m u) -> p m u", u=2),
+            in_=both[:].bitcast(F32).rearrange("p (u m) -> p m u", u=2),
+        )
+        w2_bf[units[3]] = tile([P, SLOTS * BANK], BF16, "w2_bf_last", "both")
         nc.scalar.copy(
             out=w2_bf[units[3]][:].rearrange("p (s m t) -> p m t s", s=SLOTS, t=SLOTS),
             in_=w2_in[units[3]][:].rearrange("p t (m s) -> p m t s", s=SLOTS),
@@ -296,7 +289,7 @@ def tile_list_creek_half_step_kernel(
             width = cols.stop - cols.start
             step_col = step_sb[:, b, t : t + 1]
             if n < ON_GPSIMD:
-                res = tile([P, width], F32, "res%d" % n, "gained" if n == 0 else None)
+                res = tile([P, width], F32, "res%d" % n)
                 scaled = tile([P, width], F32, "scaled%d" % n)
                 nc.scalar.activation(scaled[:], rates[n][:], ACT.Copy, scale=step_col)
                 nc.gpsimd.tensor_tensor(res[:, :], scaled[:], down[i][:, cols], ALU.add)

@@ -106,20 +106,32 @@ def tile_list_creek_half_step_kernel(
 
         w1_c, w1_sc = [], []
 
-        def order_w1(b):
-            w1_sc.append(tile([P, PASSES * BANK], U8, "w1_sc%d" % b))
+        def order_w1_scales(b, first, count):
+            plane = tile([P, PASSES * count * P], U8, "w1_sc%d%d" % (b, first))
             nc.gpsimd.tensor_copy(
-                out=w1_sc[b][:].rearrange("p (a t m) -> p a t m", t=SLOTS, m=P),
-                in_=w1_sc_raw[:].rearrange("p (a b m t) -> p b a t m", a=PASSES, t=SLOTS, m=P)[:, b],
+                out=plane[:].rearrange("p (a t m) -> p a t m", t=count, m=P),
+                in_=w1_sc_raw[:].rearrange("p (a b m t) -> p b a t m", a=PASSES, t=SLOTS, m=P)[
+                    :, b, :, first : first + count
+                ],
             )
-            w1_c.append(tile([P, H * 2], U8, "w1_c%d" % b))
-            nc.scalar.copy(
-                out=w1_c[b][:].bitcast(U16).rearrange("p (a t m) -> p a m t", t=SLOTS, m=P),
-                in_=w1_raw[b][:].bitcast(U16).rearrange("p (a m t) -> p a m t", t=SLOTS, m=P),
-            )
+            for t in range(count):
+                w1_sc.append([plane[:, P * (count * a + t) : P * (count * a + t + 1)] for a in range(PASSES)])
 
-        order_w1(0)
-        order_w1(1)
+        def order_w1_words(copy, b, first, count, after):
+            words = tile([P, PASSES * count * P * 2], U8, "w1_c%d%d" % (b, first), after)
+            copy(
+                out=words[:].bitcast(U16).rearrange("p (a t m) -> p a m t", t=count, m=P),
+                in_=w1_raw[b][:].bitcast(U16).rearrange("p (a m t) -> p a m t", t=SLOTS, m=P)[
+                    :, :, :, first : first + count
+                ],
+            )
+            for t in range(count):
+                w1_c.append([words[:, 2 * P * (count * a + t) : 2 * P * (count * a + t + 1)] for a in range(PASSES)])
+
+        order_w1_scales(0, 0, SLOTS)
+        order_w1_scales(1, 0, 2)
+        order_w1_scales(1, 2, 2)
+        order_w1_words(nc.scalar.copy, 0, 0, SLOTS, None)
 
         v_w = {}
         list_cols = BANK // PER_COLUMN
@@ -130,14 +142,16 @@ def tile_list_creek_half_step_kernel(
                     v_w[a, c][:], tab_w[a][:].indirect(offs_sb[:, list_cols * c : list_cols * (c + 1)])
                 )
 
+        order_w1_words(nc.vector.tensor_copy, 1, 0, SLOTS, "tab_w1")
+
         units = [(a, b) for b in (1, 0) for a in range(PASSES)]
         w2_in = {}
-        for (a, b), after in zip(units, ["w1_raw0", "tab_w0", "w1_sc_raw", "tab_sc"]):
+        for (a, b), after in zip(units, ["w1_raw0", "v_sc_raw", "w1_sc_raw", "tab_sc"]):
             w2_in[a, b] = tile([P, SLOTS, BANK], F32, "w2_in%d%d" % (a, b), after)
             rows = w2[BANK * a : BANK * (a + 1), BANK * b : BANK * (b + 1)]
             nc.sync.dma_start(out=w2_in[a, b][:], in_=rows.rearrange("(p t) n -> p t n", t=SLOTS))
 
-        step_sb = tile([P, PASSES, SLOTS], F32, "step_sb", "v_sc_raw")
+        step_sb = tile([P, PASSES, SLOTS], F32, "step_sb", "gain_in")
         nc.sync.dma_start(out=step_sb[:], in_=step.rearrange("(b p t) -> p b t", b=PASSES, t=SLOTS))
 
         w2_bf = {(a, b): tile([P, SLOTS * BANK], BF16, "w2_bf%d%d" % (a, b)) for a, b in units[:3]}
@@ -153,19 +167,17 @@ def tile_list_creek_half_step_kernel(
             )
 
         h = [tile([P, S], F32, "h%d" % i) for i in range(TILES)]
-        picked = [tile([P, SLOTS, M], F32, "picked%d" % b) for b in range(PASSES)]
+        picked = [tile([P, SLOTS, M], F32, "picked%d" % b, after) for b, after in enumerate([None, None])]
 
         def first_product(i):
-            b, t = divmod(i, SLOTS)
             order = list(range(PASSES) if i < 2 else reversed(range(PASSES)))
             for c in range(2):
                 acc = psum.tile([P, BANK], F32, name="acc", tag="bank%d" % ((2 * i + c) % TILES))
                 for a in order:
-                    col = BANK * a + P * t
                     nc.tensor.matmul_mx(
                         out=acc[:],
-                        lhsT=w1_c[b][:, 2 * col : 2 * (col + P)].bitcast(FP4X4),
-                        lhsT_scale=w1_sc[b][:, col : col + P],
+                        lhsT=w1_c[i][a].bitcast(FP4X4),
+                        lhsT_scale=w1_sc[i][a],
                         rhs=v_w[a, c][:].bitcast(FP8X4),
                         rhs_scale=v_sc[:, S * a + BANK * c : S * a + BANK * (c + 1)],
                         start=(a == order[0]),
@@ -188,8 +200,8 @@ def tile_list_creek_half_step_kernel(
 
         x_bf = [tile([P, M * SLOTS], BF16, "x_bf%d" % b) for b in range(PASSES)]
 
-        def make_x(b, first, width):
-            bounded = tile([P, width * SLOTS], F32, "bounded%d_%d" % (b, first))
+        def make_x(b, first, width, after):
+            bounded = tile([P, width * SLOTS], F32, "bounded%d_%d" % (b, first), after)
             nc.scalar.activation(
                 bounded[:].rearrange("p (g i t) -> p g t i", i=4, t=SLOTS),
                 picked[b][:, :, first : first + width].rearrange("p t (g i) -> p g t i", i=4),
@@ -205,34 +217,25 @@ def tile_list_creek_half_step_kernel(
         both = tile([P, 2 * M * 2], BF16, "both")
         pairs = [both[:, 2 * M * u : 2 * M * (u + 1)].rearrange("p (m e) -> p m e", e=2) for u in range(2)]
 
-        def scale_on_scalar(i):
+        def scale_on_scalar(i, after):
             b, t = divmod(i, SLOTS)
-            bounded = tile([P, M], F32, "bounded_t%d" % i)
+            bounded = tile([P, M], F32, "bounded_t%d" % i, after)
             nc.scalar.activation(bounded[:], picked[b][:, t, :], ACT.Tanh)
             nc.scalar.activation(pairs[t // 2][:, :, t % 2], bounded[:], ACT.Copy, scale=gain_rep[:, b, t : t + 1])
 
-        for i in range(SLOTS):
+        for i in range(TILES):
             first_product(i)
             pick_upstream(i)
-        pick_downstream(3, None)
-        first_product(4)
-        pick_upstream(4)
-        pick_downstream(4, None)
-        make_x(0, 0, HALF)
-        first_product(5)
-        make_x(0, HALF, HALF)
-        pick_upstream(5)
-        pick_downstream(5, None)
-        first_product(6)
-        scale_on_scalar(4)
-        pick_upstream(6)
-        first_product(7)
-        scale_on_scalar(5)
-        pick_upstream(7)
-        scale_on_scalar(6)
-        scale_on_scalar(7)
-        pick_downstream(7, None)
-        pick_downstream(6, "bounded_t5")
+            if i >= SLOTS:
+                pick_downstream(i, None)
+            if i == 5:
+                make_x(0, 0, HALF, "w1_sc10")
+        make_x(0, HALF, HALF, "v_w01")
+        scale_on_scalar(4, "v_w11")
+        scale_on_scalar(5, "v_sc")
+        scale_on_scalar(6, "v_w00")
+        scale_on_scalar(7, None)
+        pick_downstream(3, "w1_sc10")
         nc.scalar.copy(
             out=x_bf[1][:].bitcast(F32).rearrange("p (m u) -> p m u", u=2),
             in_=both[:].bitcast(F32).rearrange("p (u m) -> p m u", u=2),
@@ -251,7 +254,7 @@ def tile_list_creek_half_step_kernel(
             source = x_bf[key[1]] if key[0] == "x" else w2_bf[key[1:]]
             nc.vector.quantize_mx(out=codes.bitcast(FP8X4), scales=scales, in_=source[:])
 
-        late = tile([P, 5 * 5 * BANK], U8, "late", "h6")
+        late = tile([P, 5 * 5 * BANK], U8, "late", "h3")
         keys = [("w2", 0, 1), ("x", 0), ("w2", 1, 1), ("x", 1), ("w2", 0, 0)]
         for n, key in enumerate(keys):
             quantise(key, late[:, 5 * BANK * n : 5 * BANK * (n + 1)])
@@ -314,8 +317,9 @@ def tile_list_creek_half_step_kernel(
                 quantise(("w2", 1, 0), tile([P, 5 * BANK], U8, "w2_q_last")[:])
                 for later in range(SLOTS, TILES):
                     second_product(later)
-            if 3 <= n <= 5:
-                pick_downstream(n - 3, "moved%d" % (n - 2))
+            if n == ON_GPSIMD - 1:
+                for i in range(3):
+                    pick_downstream(i, "moved%d" % (i + 1))
             if n < ON_GPSIMD:
                 finish(n)
         held = tile([P, M * (TILES - ON_GPSIMD)], F32, "held", "scaled%d" % (ON_GPSIMD - 1))

@@ -25,7 +25,7 @@ QUADRANTS = 4
 PER_COLUMN = 16
 HALF = M // 2
 SC_ROW = 96
-ON_GPSIMD = 5
+ON_GPSIMD = 6
 REP = 256
 
 
@@ -145,21 +145,25 @@ def tile_list_creek_half_step_kernel(
         order_w1_words(nc.vector.tensor_copy, 1, 0, SLOTS, "tab_w1")
 
         units = [(a, b) for b in (1, 0) for a in range(PASSES)]
+        pieces_w2 = [units[0] + (0, HALF), units[0] + (HALF, HALF)] + [unit + (0, BANK) for unit in units[1:]]
         w2_in = {}
-        for (a, b), after in zip(units, ["w1_raw0", "v_sc_raw", "w1_sc_raw", "tab_sc"]):
-            w2_in[a, b] = tile([P, SLOTS, BANK], F32, "w2_in%d%d" % (a, b), after)
-            rows = w2[BANK * a : BANK * (a + 1), BANK * b : BANK * (b + 1)]
-            nc.sync.dma_start(out=w2_in[a, b][:], in_=rows.rearrange("(p t) n -> p t n", t=SLOTS))
+        for piece, after in zip(pieces_w2, ["w1_raw0", "w1_sc_raw", "tab_w0", "v_sc_raw", "tab_sc"]):
+            a, b, first, width = piece
+            w2_in[piece] = tile([P, SLOTS, width], F32, "w2_in%d%d_%d" % (a, b, first), after)
+            rows = w2[BANK * a : BANK * (a + 1), BANK * b + first : BANK * b + first + width]
+            nc.sync.dma_start(out=w2_in[piece][:], in_=rows.rearrange("(p t) n -> p t n", t=SLOTS))
 
         step_sb = tile([P, PASSES, SLOTS], F32, "step_sb", "gain_in")
         nc.sync.dma_start(out=step_sb[:], in_=step.rearrange("(b p t) -> p b t", b=PASSES, t=SLOTS))
 
         w2_bf = {(a, b): tile([P, SLOTS * BANK], BF16, "w2_bf%d%d" % (a, b)) for a, b in units[:3]}
 
-        for a, b in units[:3]:
+        for a, b, first, width in pieces_w2[:-1]:
             nc.gpsimd.tensor_scalar(
-                w2_bf[a, b][:].rearrange("p (s m t) -> p m s t", s=SLOTS, t=SLOTS),
-                w2_in[a, b][:].rearrange("p t (m s) -> p m s t", s=SLOTS),
+                w2_bf[a, b][:].rearrange("p (s m t) -> p m s t", s=SLOTS, t=SLOTS)[
+                    :, first // SLOTS : (first + width) // SLOTS
+                ],
+                w2_in[a, b, first, width][:].rearrange("p t (m s) -> p m s t", s=SLOTS),
                 1.0,
                 0.0,
                 ALU.mult,
@@ -243,7 +247,7 @@ def tile_list_creek_half_step_kernel(
         w2_bf[units[3]] = tile([P, SLOTS * BANK], BF16, "w2_bf_last", "both")
         nc.scalar.copy(
             out=w2_bf[units[3]][:].rearrange("p (s m t) -> p m t s", s=SLOTS, t=SLOTS),
-            in_=w2_in[units[3]][:].rearrange("p t (m s) -> p m t s", s=SLOTS),
+            in_=w2_in[pieces_w2[-1]][:].rearrange("p t (m s) -> p m t s", s=SLOTS),
         )
 
         operand = {}
@@ -283,7 +287,12 @@ def tile_list_creek_half_step_kernel(
             second_product(n)
 
         out_rows = out.rearrange("(b p t) m -> b t p m", b=PASSES, t=SLOTS)
-        pieces = [(i, slice(0, M)) for i in turn[:-1]] + [(turn[-1], slice(0, HALF)), (turn[-1], slice(HALF, M))]
+        halves = [slice(0, HALF), slice(HALF, M)]
+        pieces = (
+            [(turn[0], cols) for cols in halves]
+            + [(i, slice(0, M)) for i in turn[1:-1]]
+            + [(turn[-1], cols) for cols in halves]
+        )
         rates = []
 
         def finish(n):
@@ -297,7 +306,7 @@ def tile_list_creek_half_step_kernel(
                 nc.scalar.activation(scaled[:], rates[n][:], ACT.Copy, scale=step_col)
                 nc.gpsimd.tensor_tensor(res[:, :], scaled[:], down[i][:, cols], ALU.add)
             else:
-                first = M * (min(n, TILES - 1) - ON_GPSIMD)
+                first = M * (min(n, TILES) - ON_GPSIMD)
                 res = held[:, first + cols.start : first + cols.stop]
                 nc.vector.scalar_tensor_tensor(res[:, :], rates[n][:], step_col, down[i][:, cols], ALU.mult, ALU.add)
             nc.sync.dma_start(out=out_rows[b, t][:, cols], in_=res[:, :])
@@ -313,15 +322,15 @@ def tile_list_creek_half_step_kernel(
 
         for n in range(len(pieces)):
             add_and_bound(n)
-            if n == 0:
+            if n == 1:
                 quantise(("w2", 1, 0), tile([P, 5 * BANK], U8, "w2_q_last")[:])
                 for later in range(SLOTS, TILES):
                     second_product(later)
             if n == ON_GPSIMD - 1:
                 for i in range(3):
-                    pick_downstream(i, "moved%d" % (i + 1))
+                    pick_downstream(i, "moved%d" % (i + 2))
             if n < ON_GPSIMD:
                 finish(n)
-        held = tile([P, M * (TILES - ON_GPSIMD)], F32, "held", "scaled%d" % (ON_GPSIMD - 1))
+        held = tile([P, M * (TILES + 1 - ON_GPSIMD)], F32, "held", "scaled%d" % (ON_GPSIMD - 1))
         for n in range(ON_GPSIMD, len(pieces)):
             finish(n)

@@ -102,6 +102,7 @@ def tile_list_creek_half_step_kernel(
                 out=v_sc[32 * q : 32 * q + 4, :].bitcast(I32).rearrange("r (a c) -> r a c", a=PASSES),
                 in_=v_sc_raw[first : first + 4 * PASSES, :].bitcast(I32),
             )
+
         load_w1_words(nc.scalar, 1, "tab_sc")
 
         w1_c, w1_sc = [], []
@@ -147,7 +148,7 @@ def tile_list_creek_half_step_kernel(
         units = [(a, b) for b in (1, 0) for a in range(PASSES)]
         pieces_w2 = [units[0] + (0, HALF), units[0] + (HALF, HALF)] + [unit + (0, BANK) for unit in units[1:]]
         w2_in = {}
-        for piece, after in zip(pieces_w2, ["w1_raw0", "w1_sc_raw", "tab_w0", "v_sc_raw", "tab_sc"]):
+        for piece, after in zip(pieces_w2, ["tab_w0", "w1_raw0", "w1_sc_raw", "v_sc_raw", "tab_sc"]):
             a, b, first, width = piece
             w2_in[piece] = tile([P, SLOTS, width], F32, "w2_in%d%d_%d" % (a, b, first), after)
             rows = w2[BANK * a : BANK * (a + 1), BANK * b + first : BANK * b + first + width]
@@ -169,6 +170,17 @@ def tile_list_creek_half_step_kernel(
                 ALU.mult,
                 ALU.add,
             )
+
+        last_bf = [tile([P, 2 * BANK], BF16, "last_bf0")]
+        last_in = w2_in[pieces_w2[-1]][:]
+        nc.gpsimd.tensor_scalar(
+            last_bf[0][:].rearrange("p (s m t) -> p m s t", s=2, t=SLOTS),
+            last_in.rearrange("p t (m s) -> p m s t", s=SLOTS)[:, :, 0:2],
+            1.0,
+            0.0,
+            ALU.mult,
+            ALU.add,
+        )
 
         h = [tile([P, S], F32, "h%d" % i) for i in range(TILES)]
         picked = [tile([P, SLOTS, M], F32, "picked%d" % b, after) for b, after in enumerate([None, None])]
@@ -221,11 +233,17 @@ def tile_list_creek_half_step_kernel(
         both = tile([P, 2 * M * 2], BF16, "both")
         pairs = [both[:, 2 * M * u : 2 * M * (u + 1)].rearrange("p (m e) -> p m e", e=2) for u in range(2)]
 
-        def scale_on_scalar(i, after):
+        bounded_rows = {}
+
+        def bound_rows(i, after):
+            bounded_rows[i] = tile([P, M], F32, "bounded_t%d" % i, after)
+            nc.scalar.activation(bounded_rows[i][:], picked[1][:, i - SLOTS, :], ACT.Tanh)
+
+        def scale_rows(i):
             b, t = divmod(i, SLOTS)
-            bounded = tile([P, M], F32, "bounded_t%d" % i, after)
-            nc.scalar.activation(bounded[:], picked[b][:, t, :], ACT.Tanh)
-            nc.scalar.activation(pairs[t // 2][:, :, t % 2], bounded[:], ACT.Copy, scale=gain_rep[:, b, t : t + 1])
+            nc.scalar.activation(
+                pairs[t // 2][:, :, t % 2], bounded_rows[i][:], ACT.Copy, scale=gain_rep[:, b, t : t + 1]
+            )
 
         for i in range(TILES):
             first_product(i)
@@ -235,19 +253,20 @@ def tile_list_creek_half_step_kernel(
             if i == 5:
                 make_x(0, 0, HALF, "w1_sc10")
         make_x(0, HALF, HALF, "v_w01")
-        scale_on_scalar(4, "v_w11")
-        scale_on_scalar(5, "v_sc")
-        scale_on_scalar(6, "v_w00")
-        scale_on_scalar(7, None)
+        for i, after in zip(range(SLOTS, TILES), ["v_w11", "v_sc", "v_w00", None]):
+            bound_rows(i, after)
+            if i > SLOTS:
+                scale_rows(i - 1)
+        scale_rows(TILES - 1)
         pick_downstream(3, "w1_sc10")
         nc.scalar.copy(
             out=x_bf[1][:].bitcast(F32).rearrange("p (m u) -> p m u", u=2),
             in_=both[:].bitcast(F32).rearrange("p (u m) -> p m u", u=2),
         )
-        w2_bf[units[3]] = tile([P, SLOTS * BANK], BF16, "w2_bf_last", "both")
+        last_bf.append(tile([P, 2 * BANK], BF16, "last_bf1", "both"))
         nc.scalar.copy(
-            out=w2_bf[units[3]][:].rearrange("p (s m t) -> p m t s", s=SLOTS, t=SLOTS),
-            in_=w2_in[pieces_w2[-1]][:].rearrange("p t (m s) -> p m t s", s=SLOTS),
+            out=last_bf[1][:].rearrange("p (s m t) -> p m t s", s=2, t=SLOTS),
+            in_=last_in.rearrange("p t (m s) -> p m t s", s=SLOTS)[:, :, :, 2:4],
         )
 
         operand = {}
@@ -258,10 +277,21 @@ def tile_list_creek_half_step_kernel(
             source = x_bf[key[1]] if key[0] == "x" else w2_bf[key[1:]]
             nc.vector.quantize_mx(out=codes.bitcast(FP8X4), scales=scales, in_=source[:])
 
-        late = tile([P, 5 * 5 * BANK], U8, "late", "h3")
+        late = tile([P, 6 * 5 * BANK], U8, "late", "v_w01")
         keys = [("w2", 0, 1), ("x", 0), ("w2", 1, 1), ("x", 1), ("w2", 0, 0)]
         for n, key in enumerate(keys):
             quantise(key, late[:, 5 * BANK * n : 5 * BANK * (n + 1)])
+        last_codes, last_scales = late[:, 25 * BANK : 29 * BANK], late[:, 29 * BANK :]
+        operand["w2", 1, 0] = (last_codes, last_scales)
+
+        def quantise_last(u):
+            nc.vector.quantize_mx(
+                out=last_codes[:, 4 * HALF * u : 4 * HALF * (u + 1)].bitcast(FP8X4),
+                scales=last_scales[:, HALF * u : HALF * (u + 1)],
+                in_=last_bf[u][:],
+            )
+
+        quantise_last(0)
 
         turn = [4, 5, 6, 7, 3, 0, 1, 2]
         y = {}
@@ -301,10 +331,8 @@ def tile_list_creek_half_step_kernel(
             width = cols.stop - cols.start
             step_col = step_sb[:, b, t : t + 1]
             if n < ON_GPSIMD:
-                res = tile([P, width], F32, "res%d" % n)
-                scaled = tile([P, width], F32, "scaled%d" % n)
-                nc.scalar.activation(scaled[:], rates[n][:], ACT.Copy, scale=step_col)
-                nc.gpsimd.tensor_tensor(res[:, :], scaled[:], down[i][:, cols], ALU.add)
+                res = behind[:, 3, cols] if n < 2 else tile([P, width], F32, "res%d" % n)
+                nc.gpsimd.tensor_tensor(res[:, :], rates[n][:], down[i][:, cols], ALU.add)
             else:
                 first = M * (min(n, TILES) - ON_GPSIMD)
                 res = held[:, first + cols.start : first + cols.stop]
@@ -314,21 +342,32 @@ def tile_list_creek_half_step_kernel(
         def add_and_bound(n):
             i, cols = pieces[n]
             width = cols.stop - cols.start
-            moved = tile([P, width], F32, "moved%d" % n)
-            nc.vector.tensor_tensor(moved[:], y[i][:, cols], down[i][:, cols], ALU.add)
+            if 2 <= n < 5:
+                moved = behind[:, n - 2, :]
+            else:
+                moved = tile([P, width], F32, "moved%d" % n)[:]
+            nc.vector.tensor_tensor(moved, y[i][:, cols], down[i][:, cols], ALU.add)
             rate = tile([P, width], F32, "rate%d" % n)
-            nc.scalar.activation(rate[:], moved[:], ACT.Tanh)
+            nc.scalar.activation(rate[:], moved, ACT.Tanh)
+            if n < ON_GPSIMD:
+                b, t = divmod(i, SLOTS)
+                scaled = tile([P, width], F32, "scaled%d" % n)
+                nc.scalar.activation(scaled[:], rate[:], ACT.Copy, scale=step_sb[:, b, t : t + 1])
+                rate = scaled
             rates.append(rate)
 
-        for n in range(len(pieces)):
+        for n in range(2):
             add_and_bound(n)
-            if n == 1:
-                quantise(("w2", 1, 0), tile([P, 5 * BANK], U8, "w2_q_last")[:])
-                for later in range(SLOTS, TILES):
-                    second_product(later)
+        quantise_last(1)
+        behind = tile([P, 4, M], F32, "behind", "both")
+        for later in range(SLOTS, TILES):
+            second_product(later)
+        for n in range(len(pieces)):
+            if n >= 2:
+                add_and_bound(n)
             if n == ON_GPSIMD - 1:
                 for i in range(3):
-                    pick_downstream(i, "moved%d" % (i + 2))
+                    pick_downstream(i, "rate%d" % (i + 1))
             if n < ON_GPSIMD:
                 finish(n)
         held = tile([P, M * (TILES + 1 - ON_GPSIMD)], F32, "held", "scaled%d" % (ON_GPSIMD - 1))

@@ -103,7 +103,17 @@ def tile_list_creek_half_step_kernel(
                 in_=v_sc_raw[first : first + 4 * PASSES, :].bitcast(I32),
             )
 
-        load_w1_words(nc.scalar, 1, "tab_sc")
+        units = [(a, b) for b in (1, 0) for a in range(PASSES)]
+        pieces_w2 = [units[0] + (0, HALF), units[0] + (HALF, HALF)] + [unit + (0, BANK) for unit in units[1:]]
+        w2_in = {}
+
+        def load_w2(queue, piece, after):
+            a, b, first, width = piece
+            w2_in[piece] = tile([P, SLOTS, width], F32, "w2_in%d%d_%d" % (a, b, first), after)
+            rows = w2[BANK * a : BANK * (a + 1), BANK * b + first : BANK * b + first + width]
+            queue.dma_start(out=w2_in[piece][:], in_=rows.rearrange("(p t) n -> p t n", t=SLOTS))
+
+        load_w2(nc.scalar, pieces_w2[0], "tab_sc")
 
         w1_c, w1_sc = [], []
 
@@ -129,10 +139,23 @@ def tile_list_creek_half_step_kernel(
             for t in range(count):
                 w1_c.append([words[:, 2 * P * (count * a + t) : 2 * P * (count * a + t + 1)] for a in range(PASSES)])
 
+        def order_w1_pairs(b, first, count):
+            words = tile([P, PASSES * count * P * 2], U8, "w1_c%d%d" % (b, first))
+            for a in range(PASSES):
+                nc.gpsimd.tensor_copy(
+                    out=words[:].rearrange("p (a t m e) -> p a t m e", t=count, m=P, e=2)[:, a],
+                    in_=w1_raw[b][:].bitcast(U8).rearrange("p (a m t e) -> p a t m e", t=SLOTS, m=P, e=2)[
+                        :, a, first : first + count
+                    ],
+                )
+            for t in range(count):
+                w1_c.append([words[:, 2 * P * (count * a + t) : 2 * P * (count * a + t + 1)] for a in range(PASSES)])
+
         order_w1_scales(0, 0, SLOTS)
         order_w1_scales(1, 0, 2)
         order_w1_scales(1, 2, 2)
         order_w1_words(nc.scalar.copy, 0, 0, SLOTS, None)
+        load_w1_words(nc.sync, 1, "w1_raw0")
 
         v_w = {}
         list_cols = BANK // PER_COLUMN
@@ -143,18 +166,13 @@ def tile_list_creek_half_step_kernel(
                     v_w[a, c][:], tab_w[a][:].indirect(offs_sb[:, list_cols * c : list_cols * (c + 1)])
                 )
 
-        order_w1_words(nc.vector.tensor_copy, 1, 0, SLOTS, "tab_w1")
+        order_w1_words(nc.vector.tensor_copy, 1, 0, 2, "tab_w1")
+        order_w1_pairs(1, 2, 2)
 
-        units = [(a, b) for b in (1, 0) for a in range(PASSES)]
-        pieces_w2 = [units[0] + (0, HALF), units[0] + (HALF, HALF)] + [unit + (0, BANK) for unit in units[1:]]
-        w2_in = {}
-        for piece, after in zip(pieces_w2, ["tab_w0", "w1_raw0", "w1_sc_raw", "v_sc_raw", "tab_sc"]):
-            a, b, first, width = piece
-            w2_in[piece] = tile([P, SLOTS, width], F32, "w2_in%d%d_%d" % (a, b, first), after)
-            rows = w2[BANK * a : BANK * (a + 1), BANK * b + first : BANK * b + first + width]
-            nc.sync.dma_start(out=w2_in[piece][:], in_=rows.rearrange("(p t) n -> p t n", t=SLOTS))
+        for piece, after in zip(pieces_w2[1:], ["tab_w0", "v_sc_raw", "w1_sc_raw", "tab_sc"]):
+            load_w2(nc.sync, piece, after)
 
-        step_sb = tile([P, PASSES, SLOTS], F32, "step_sb", "gain_in")
+        step_sb = tile([P, PASSES, SLOTS], F32, "step_sb", "w1_sc_raw")
         nc.sync.dma_start(out=step_sb[:], in_=step.rearrange("(b p t) -> p b t", b=PASSES, t=SLOTS))
 
         w2_bf = {(a, b): tile([P, SLOTS * BANK], BF16, "w2_bf%d%d" % (a, b)) for a, b in units[:3]}

@@ -51,7 +51,7 @@ def tile_list_creek_half_step_kernel(
         v_sc = tile([P, PASSES * S], U8, "v_sc")
         gain_in = tile([P, PASSES, SLOTS], F32, "gain_in")
 
-        nc.vector.memset(w1_sc_raw[:].bitcast(I32), 0)
+        nc.gpsimd.memset(w1_sc_raw[:].bitcast(I32), 0)
         nc.vector.memset(tab_sc[0:SC_ROW, :].bitcast(I32), 0)
         nc.vector.memset(v_sc[:].bitcast(I32), 0)
 
@@ -76,16 +76,29 @@ def tile_list_creek_half_step_kernel(
         nc.sync.dma_start(
             out=tab_sc[SC_ROW:P, :].bitcast(I32), in_=tab_scales.bitcast(I32).rearrange("a q c -> q a c")
         )
-        nc.sync.dma_start(out=gain_in[:], in_=gain.rearrange("(b p t) -> p b t", b=PASSES, t=SLOTS))
+        nc.scalar.dma_start(out=gain_in[:], in_=gain.rearrange("(b p t) -> p b t", b=PASSES, t=SLOTS))
         for q in range(QUADRANTS):
-            nc.sync.dma_start(
+            nc.scalar.dma_start(
                 out=w1_sc_raw[32 * q : 32 * q + 4, :].bitcast(I32).rearrange("r (a c) -> r a c", a=PASSES),
                 in_=w1_scales.bitcast(I32)[:, 4 * q : 4 * q + 4, :].rearrange("a r c -> r a c"),
             )
         load_table_words(0, None)
         load_w1_words(nc.sync, 0, None)
-        load_table_words(1, None)
         nc.sync.dma_start(pos1_sb[:], pos1)
+        load_table_words(1, None)
+        load_w1_words(nc.sync, 1, None)
+
+        units = [(a, b) for b in (1, 0) for a in range(PASSES)]
+        pieces_w2 = [units[0] + (0, HALF), units[0] + (HALF, HALF)] + [unit + (0, BANK) for unit in units[1:]]
+        w2_in = {}
+
+        def load_w2(queue, piece, after):
+            a, b, first, width = piece
+            w2_in[piece] = tile([P, SLOTS, width], F32, "w2_in%d%d_%d" % (a, b, first), after)
+            rows = w2[BANK * a : BANK * (a + 1), BANK * b + first : BANK * b + first + width]
+            queue.dma_start(out=w2_in[piece][:], in_=rows.rearrange("(p t) n -> p t n", t=SLOTS))
+
+        load_w2(nc.sync, pieces_w2[0], "w2_first")
         nc.sync.dma_start(pos2_sb[:], pos2)
 
         gain_rep = tile([P, PASSES, REP], F32, "gain_rep")
@@ -102,18 +115,6 @@ def tile_list_creek_half_step_kernel(
                 out=v_sc[32 * q : 32 * q + 4, :].bitcast(I32).rearrange("r (a c) -> r a c", a=PASSES),
                 in_=v_sc_raw[first : first + 4 * PASSES, :].bitcast(I32),
             )
-
-        units = [(a, b) for b in (1, 0) for a in range(PASSES)]
-        pieces_w2 = [units[0] + (0, HALF), units[0] + (HALF, HALF)] + [unit + (0, BANK) for unit in units[1:]]
-        w2_in = {}
-
-        def load_w2(queue, piece, after):
-            a, b, first, width = piece
-            w2_in[piece] = tile([P, SLOTS, width], F32, "w2_in%d%d_%d" % (a, b, first), after)
-            rows = w2[BANK * a : BANK * (a + 1), BANK * b + first : BANK * b + first + width]
-            queue.dma_start(out=w2_in[piece][:], in_=rows.rearrange("(p t) n -> p t n", t=SLOTS))
-
-        load_w2(nc.scalar, pieces_w2[0], "tab_sc")
 
         w1_c, w1_sc = [], []
 
@@ -139,23 +140,11 @@ def tile_list_creek_half_step_kernel(
             for t in range(count):
                 w1_c.append([words[:, 2 * P * (count * a + t) : 2 * P * (count * a + t + 1)] for a in range(PASSES)])
 
-        def order_w1_pairs(b, first, count):
-            words = tile([P, PASSES * count * P * 2], U8, "w1_c%d%d" % (b, first))
-            for a in range(PASSES):
-                nc.gpsimd.tensor_copy(
-                    out=words[:].rearrange("p (a t m e) -> p a t m e", t=count, m=P, e=2)[:, a],
-                    in_=w1_raw[b][:].bitcast(U8).rearrange("p (a m t e) -> p a t m e", t=SLOTS, m=P, e=2)[
-                        :, a, first : first + count
-                    ],
-                )
-            for t in range(count):
-                w1_c.append([words[:, 2 * P * (count * a + t) : 2 * P * (count * a + t + 1)] for a in range(PASSES)])
-
         order_w1_scales(0, 0, SLOTS)
         order_w1_scales(1, 0, 2)
         order_w1_scales(1, 2, 2)
         order_w1_words(nc.scalar.copy, 0, 0, SLOTS, None)
-        load_w1_words(nc.sync, 1, "w1_raw0")
+        order_w1_words(nc.scalar.copy, 1, 0, SLOTS, None)
 
         v_w = {}
         list_cols = BANK // PER_COLUMN
@@ -166,10 +155,8 @@ def tile_list_creek_half_step_kernel(
                     v_w[a, c][:], tab_w[a][:].indirect(offs_sb[:, list_cols * c : list_cols * (c + 1)])
                 )
 
-        order_w1_words(nc.vector.tensor_copy, 1, 0, 2, "tab_w1")
-        order_w1_pairs(1, 2, 2)
 
-        for piece, after in zip(pieces_w2[1:], ["tab_w0", "v_sc_raw", "w1_sc_raw", "tab_sc"]):
+        for piece, after in zip(pieces_w2[1:], ["tab_w0", "v_sc_raw", "w1_sc_raw", "w2_first"]):
             load_w2(nc.sync, piece, after)
 
         step_sb = tile([P, PASSES, SLOTS], F32, "step_sb", "w1_sc_raw")

@@ -89,7 +89,11 @@ def tile_list_creek_half_step_kernel(
         load_w1_words(nc.sync, 1, None)
 
         units = [(a, b) for b in (1, 0) for a in range(PASSES)]
-        pieces_w2 = [units[0] + (0, HALF), units[0] + (HALF, HALF)] + [unit + (0, BANK) for unit in units[1:]]
+        pieces_w2 = (
+            [units[0] + (0, P), units[0] + (P, P), units[0] + (HALF, HALF)]
+            + [units[1] + (0, HALF), units[1] + (HALF, HALF)]
+            + [unit + (0, BANK) for unit in units[2:]]
+        )
         w2_in = {}
 
         def load_w2(queue, piece, after):
@@ -98,8 +102,9 @@ def tile_list_creek_half_step_kernel(
             rows = w2[BANK * a : BANK * (a + 1), BANK * b + first : BANK * b + first + width]
             queue.dma_start(out=w2_in[piece][:], in_=rows.rearrange("(p t) n -> p t n", t=SLOTS))
 
-        load_w2(nc.sync, pieces_w2[0], "w2_first")
+        load_w2(nc.sync, pieces_w2[0], None)
         nc.sync.dma_start(pos2_sb[:], pos2)
+
 
         gain_rep = tile([P, PASSES, REP], F32, "gain_rep")
         nc.scalar.activation(
@@ -151,12 +156,28 @@ def tile_list_creek_half_step_kernel(
         for a in range(PASSES):
             for c in range(2):
                 v_w[a, c] = tile([P, BANK], U32, "v_w%d%d" % (a, c))
-                nc.vector.tensor_copy(
-                    v_w[a, c][:], tab_w[a][:].indirect(offs_sb[:, list_cols * c : list_cols * (c + 1)])
-                )
+                parts = 2 if (a, c) == (1, 1) else 1
+                for u in range(parts):
+                    first = list_cols * c + u * list_cols // parts
+                    nc.vector.tensor_copy(
+                        v_w[a, c][:, u * BANK // parts : (u + 1) * BANK // parts],
+                        tab_w[a][:].indirect(offs_sb[:, first : first + list_cols // parts]),
+                    )
 
 
-        for piece, after in zip(pieces_w2[1:], ["tab_w0", "v_sc_raw", "w1_sc_raw", "w2_first"]):
+        warm = psum.tile([P, BANK], F32, name="warm", tag="bank6")
+        for c in (0, 1, 1):
+            nc.tensor.matmul_mx(
+                out=warm[:],
+                lhsT=w1_raw[0][:].bitcast(U8)[:, : 2 * P].bitcast(FP4X4),
+                lhsT_scale=w1_sc_raw[:, :P],
+                rhs=v_w[0, c][:].bitcast(FP8X4),
+                rhs_scale=v_sc_raw[:, BANK * c : BANK * (c + 1)],
+                start=True,
+                stop=True,
+            )
+
+        for piece, after in zip(pieces_w2[1:], ["tab_w0", "w1_raw0", "w1_raw1", "v_sc_raw", "tab_w1", "tab_w0"]):
             load_w2(nc.sync, piece, after)
 
         step_sb = tile([P, PASSES, SLOTS], F32, "step_sb", "w1_sc_raw")
@@ -190,24 +211,32 @@ def tile_list_creek_half_step_kernel(
         h = [tile([P, S], F32, "h%d" % i) for i in range(TILES)]
         picked = [tile([P, SLOTS, M], F32, "picked%d" % b, after) for b, after in enumerate([None, None])]
 
+        def columns_of_h(i, first, width, bank, order, empty):
+            acc = psum.tile([P, width], F32, name="acc", tag="bank%d" % bank)
+            c, inside = divmod(first, BANK)
+            for a in order:
+                nc.tensor.matmul_mx(
+                    out=acc[:],
+                    lhsT=w1_c[i][a].bitcast(FP4X4),
+                    lhsT_scale=w1_sc[i][a],
+                    rhs=v_w[a, c][:, inside : inside + width].bitcast(FP8X4),
+                    rhs_scale=v_sc[:, S * a + first : S * a + first + width],
+                    start=(a == order[0]),
+                    stop=(a == order[-1]),
+                )
+            empty(h[i][:, first : first + width], acc[:])
+
+        def empty_on_scalar(dest, acc):
+            nc.scalar.activation(dest, acc, ACT.Copy)
+
         def first_product(i):
-            order = list(range(PASSES) if i < 2 else reversed(range(PASSES)))
-            for c in range(2):
-                acc = psum.tile([P, BANK], F32, name="acc", tag="bank%d" % ((2 * i + c) % TILES))
-                for a in order:
-                    nc.tensor.matmul_mx(
-                        out=acc[:],
-                        lhsT=w1_c[i][a].bitcast(FP4X4),
-                        lhsT_scale=w1_sc[i][a],
-                        rhs=v_w[a, c][:].bitcast(FP8X4),
-                        rhs_scale=v_sc[:, S * a + BANK * c : S * a + BANK * (c + 1)],
-                        start=(a == order[0]),
-                        stop=(a == order[-1]),
-                    )
-                if (i, c) == (0, 1):
-                    nc.vector.tensor_copy(h[i][:, BANK * c : BANK * (c + 1)], acc[:])
-                else:
-                    nc.scalar.activation(h[i][:, BANK * c : BANK * (c + 1)], acc[:], ACT.Copy)
+            if i == 0:
+                columns_of_h(i, 0, BANK, 0, [0, 1], empty_on_scalar)
+                columns_of_h(i, BANK, HALF, 1, [0, 1], empty_on_scalar)
+                columns_of_h(i, BANK + HALF, HALF, TILES - 1, [0, 1], nc.vector.tensor_copy)
+            else:
+                for c in range(2):
+                    columns_of_h(i, BANK * c, BANK, (2 * i + c) % TILES, [1, 0], empty_on_scalar)
 
         def pick_upstream(i):
             b, t = divmod(i, SLOTS)
@@ -253,16 +282,19 @@ def tile_list_creek_half_step_kernel(
         for i in range(TILES):
             first_product(i)
             pick_upstream(i)
-            if i >= SLOTS:
+            if i >= SLOTS and i != 6:
                 pick_downstream(i, None)
             if i == 5:
                 make_x(0, 0, HALF, "w1_sc10")
         make_x(0, HALF, HALF, "v_w01")
-        for i, after in zip(range(SLOTS, TILES), ["v_w11", "v_sc", "v_w00", None]):
+        for i, after in zip(range(SLOTS, TILES - 1), ["v_w11", "v_sc", "v_w00"]):
             bound_rows(i, after)
             if i > SLOTS:
                 scale_rows(i - 1)
+        scale_rows(TILES - 2)
+        bound_rows(TILES - 1, None)
         scale_rows(TILES - 1)
+        pick_downstream(6, "v_w11")
         pick_downstream(3, "w1_sc10")
         nc.scalar.copy(
             out=x_bf[1][:].bitcast(F32).rearrange("p (m u) -> p m u", u=2),

@@ -231,7 +231,7 @@ def tile_list_creek_half_step_kernel(
 
         def first_product(i):
             if i == 0:
-                columns_of_h(i, 0, BANK, 0, [0, 1], empty_on_scalar)
+                columns_of_h(i, 0, BANK, 0, [0, 1], nc.vector.tensor_copy)
                 columns_of_h(i, BANK, HALF, 1, [0, 1], empty_on_scalar)
                 columns_of_h(i, BANK + HALF, HALF, TILES - 1, [0, 1], nc.vector.tensor_copy)
             else:

@@ -169,8 +169,8 @@ def tile_list_creek_half_step_kernel(
         for c in (0, 1, 1):
             nc.tensor.matmul_mx(
                 out=warm[:],
-                lhsT=w1_raw[0][:].bitcast(U8)[:, : 2 * P].bitcast(FP4X4),
-                lhsT_scale=w1_sc_raw[:, :P],
+                lhsT=w1_c[0][0].bitcast(FP4X4),
+                lhsT_scale=w1_sc[0][0],
                 rhs=v_w[0, c][:].bitcast(FP8X4),
                 rhs_scale=v_sc_raw[:, BANK * c : BANK * (c + 1)],
                 start=True,
@@ -227,7 +227,7 @@ def tile_list_creek_half_step_kernel(
             empty(h[i][:, first : first + width], acc[:])
 
         def empty_on_scalar(dest, acc):
-            nc.scalar.activation(dest, acc, ACT.Copy)
+            nc.scalar.copy(dest, acc)
 
         def first_product(i):
             if i == 0:

@@ -165,18 +165,6 @@ def tile_list_creek_half_step_kernel(
                     )
 
 
-        warm = psum.tile([P, BANK], F32, name="warm", tag="bank6")
-        for c in (0, 1, 1):
-            nc.tensor.matmul_mx(
-                out=warm[:],
-                lhsT=w1_c[0][0].bitcast(FP4X4),
-                lhsT_scale=w1_sc[0][0],
-                rhs=v_w[0, c][:].bitcast(FP8X4),
-                rhs_scale=v_sc_raw[:, BANK * c : BANK * (c + 1)],
-                start=True,
-                stop=True,
-            )
-
         for piece, after in zip(pieces_w2[1:], ["tab_w0", "w1_raw0", "w1_raw1", "v_sc_raw", "tab_w1", "tab_w0"]):
             load_w2(nc.sync, piece, after)
 

from contextlib import ExitStack

import concourse.mybir as mybir

F32 = mybir.dt.float32
BF16 = mybir.dt.bfloat16
I32 = mybir.dt.int32
U32 = mybir.dt.uint32
U16 = mybir.dt.uint16
U8 = mybir.dt.uint8
FP8X4 = mybir.dt.float8_e4m3fn_x4
FP4X4 = mybir.dt.float4_e2m1fn_x4
ACT = mybir.ActivationFunctionType
ALU = mybir.AluOpType

K, H, T, S, M = 1024, 1024, 2048, 1024, 512
FLOPS = 2 * K * H * S + 2 * H * H * M

P = 128
SLOTS = 4
PASSES = 2
TILES = PASSES * SLOTS
BANK = 512
QUADRANTS = 4
PER_COLUMN = 16
HALF = M // 2
SC_ROW = 96
ON_GPSIMD = 6
REP = 256


def tile_list_creek_half_step_kernel(
    tc, tab_words, tab_scales, offs, pos1, pos2, w1_words, w1_scales, gain, w2, step, out
):
    nc = tc.nc
    with ExitStack() as ctx:
        lists = ctx.enter_context(tc.tile_pool(name="lists", bufs=1))
        keep = ctx.enter_context(tc.tile_pool(name="keep", bufs=1))
        psum = ctx.enter_context(tc.psum_pool(name="psum", bufs=1))

        offs_sb = lists.tile([P, S // PER_COLUMN], U16, name="offs_sb")
        pos1_sb = lists.tile([P, M // PER_COLUMN], U16, name="pos1_sb")
        pos2_sb = lists.tile([P, M // PER_COLUMN], U16, name="pos2_sb")

        def tile(shape, dtype, name, after=None):
            return keep.tile(shape, dtype, name=name, tag=after or name, align_bytes=64)

        tab_sc = tile([P, T], U8, "tab_sc")
        w1_sc_raw = tile([P, PASSES * H], U8, "w1_sc_raw")
        v_sc_raw = tile([P, S], U8, "v_sc_raw")
        v_sc = tile([P, PASSES * S], U8, "v_sc")
        gain_in = tile([P, PASSES, SLOTS], F32, "gain_in")

        nc.gpsimd.memset(w1_sc_raw[:].bitcast(I32), 0)
        nc.vector.memset(tab_sc[0:SC_ROW, :].bitcast(I32), 0)
        nc.vector.memset(v_sc[:].bitcast(I32), 0)

        tab_w = []

        def load_table_words(a, after):
            tab_w.append(tile([P, T], U32, "tab_w%d" % a, after))
            nc.sync.dma_start(
                out=tab_w[a][:].bitcast(I32), in_=tab_words[a].rearrange("p t i -> p (t i)").bitcast(I32)
            )

        w1_raw = []

        def load_w1_words(queue, b, after):
            w1_raw.append(tile([P, PASSES * BANK // 2], I32, "w1_raw%d" % b, after))
            queue.dma_start(
                out=w1_raw[b][:].rearrange("p (a c) -> p a c", a=PASSES),
                in_=w1_words.bitcast(I32).rearrange("a p (b c) -> b p a c", b=PASSES)[b],
            )

        nc.sync.dma_start(offs_sb[:], offs)
        nc.sync.dma_start(
            out=tab_sc[SC_ROW:P, :].bitcast(I32), in_=tab_scales.bitcast(I32).rearrange("a q c -> q a c")
        )
        nc.scalar.dma_start(out=gain_in[:], in_=gain.rearrange("(b p t) -> p b t", b=PASSES, t=SLOTS))
        for q in range(QUADRANTS):
            nc.scalar.dma_start(
                out=w1_sc_raw[32 * q : 32 * q + 4, :].bitcast(I32).rearrange("r (a c) -> r a c", a=PASSES),
                in_=w1_scales.bitcast(I32)[:, 4 * q : 4 * q + 4, :].rearrange("a r c -> r a c"),
            )
        load_table_words(0, None)
        load_w1_words(nc.sync, 0, None)
        nc.sync.dma_start(pos1_sb[:], pos1)
        load_table_words(1, None)
        load_w1_words(nc.sync, 1, None)

        units = [(a, b) for b in (1, 0) for a in range(PASSES)]
        pieces_w2 = (
            [units[0] + (0, P), units[0] + (P, P), units[0] + (HALF, HALF)]
            + [units[1] + (0, HALF), units[1] + (HALF, HALF)]
            + [unit + (0, BANK) for unit in units[2:]]
        )
        w2_in = {}

        def load_w2(queue, piece, after):
            a, b, first, width = piece
            w2_in[piece] = tile([P, SLOTS, width], F32, "w2_in%d%d_%d" % (a, b, first), after)
            rows = w2[BANK * a : BANK * (a + 1), BANK * b + first : BANK * b + first + width]
            queue.dma_start(out=w2_in[piece][:], in_=rows.rearrange("(p t) n -> p t n", t=SLOTS))

        load_w2(nc.sync, pieces_w2[0], None)
        nc.sync.dma_start(pos2_sb[:], pos2)


        gain_rep = tile([P, PASSES, REP], F32, "gain_rep")
        nc.scalar.activation(
            gain_rep[:].rearrange("p b (m t) -> p b m t", t=SLOTS),
            gain_in[:].unsqueeze(2).to_broadcast([P, PASSES, REP // SLOTS, SLOTS]),
            ACT.Copy,
        )

        nc.vector.tensor_copy(v_sc_raw[:], tab_sc[:].indirect(offs_sb[:]))
        for q in range(QUADRANTS):
            first = SC_ROW + 4 * PASSES * q
            nc.scalar.dma_start(
                out=v_sc[32 * q : 32 * q + 4, :].bitcast(I32).rearrange("r (a c) -> r a c", a=PASSES),
                in_=v_sc_raw[first : first + 4 * PASSES, :].bitcast(I32),
            )

        w1_c, w1_sc = [], []

        def order_w1_scales(b, first, count):
            plane = tile([P, PASSES * count * P], U8, "w1_sc%d%d" % (b, first))
            nc.gpsimd.tensor_copy(
                out=plane[:].rearrange("p (a t m) -> p a t m", t=count, m=P),
                in_=w1_sc_raw[:].rearrange("p (a b m t) -> p b a t m", a=PASSES, t=SLOTS, m=P)[
                    :, b, :, first : first + count
                ],
            )
            for t in range(count):
                w1_sc.append([plane[:, P * (count * a + t) : P * (count * a + t + 1)] for a in range(PASSES)])

        def order_w1_words(copy, b, first, count, after):
            words = tile([P, PASSES * count * P * 2], U8, "w1_c%d%d" % (b, first), after)
            copy(
                out=words[:].bitcast(U16).rearrange("p (a t m) -> p a m t", t=count, m=P),
                in_=w1_raw[b][:].bitcast(U16).rearrange("p (a m t) -> p a m t", t=SLOTS, m=P)[
                    :, :, :, first : first + count
                ],
            )
            for t in range(count):
                w1_c.append([words[:, 2 * P * (count * a + t) : 2 * P * (count * a + t + 1)] for a in range(PASSES)])

        order_w1_scales(0, 0, SLOTS)
        order_w1_scales(1, 0, 2)
        order_w1_scales(1, 2, 2)
        order_w1_words(nc.scalar.copy, 0, 0, SLOTS, None)
        order_w1_words(nc.scalar.copy, 1, 0, SLOTS, None)

        v_w = {}
        list_cols = BANK // PER_COLUMN
        for a in range(PASSES):
            for c in range(2):
                v_w[a, c] = tile([P, BANK], U32, "v_w%d%d" % (a, c))
                parts = 2 if (a, c) == (1, 1) else 1
                for u in range(parts):
                    first = list_cols * c + u * list_cols // parts
                    nc.vector.tensor_copy(
                        v_w[a, c][:, u * BANK // parts : (u + 1) * BANK // parts],
                        tab_w[a][:].indirect(offs_sb[:, first : first + list_cols // parts]),
                    )


        for piece, after in zip(pieces_w2[1:], ["tab_w0", "w1_raw0", "w1_raw1", "v_sc_raw", "tab_w1", "tab_w0"]):
            load_w2(nc.sync, piece, after)

        step_sb = tile([P, PASSES, SLOTS], F32, "step_sb", "w1_sc_raw")
        nc.sync.dma_start(out=step_sb[:], in_=step.rearrange("(b p t) -> p b t", b=PASSES, t=SLOTS))

        w2_bf = {(a, b): tile([P, SLOTS * BANK], BF16, "w2_bf%d%d" % (a, b)) for a, b in units[:3]}

        for a, b, first, width in pieces_w2[:-1]:
            nc.gpsimd.tensor_scalar(
                w2_bf[a, b][:].rearrange("p (s m t) -> p m s t", s=SLOTS, t=SLOTS)[
                    :, first // SLOTS : (first + width) // SLOTS
                ],
                w2_in[a, b, first, width][:].rearrange("p t (m s) -> p m s t", s=SLOTS),
                1.0,
                0.0,
                ALU.mult,
                ALU.add,
            )

        last_bf = [tile([P, 2 * BANK], BF16, "last_bf0")]
        last_in = w2_in[pieces_w2[-1]][:]
        nc.gpsimd.tensor_scalar(
            last_bf[0][:].rearrange("p (s m t) -> p m s t", s=2, t=SLOTS),
            last_in.rearrange("p t (m s) -> p m s t", s=SLOTS)[:, :, 0:2],
            1.0,
            0.0,
            ALU.mult,
            ALU.add,
        )

        h = [tile([P, S], F32, "h%d" % i) for i in range(TILES)]
        picked = [tile([P, SLOTS, M], F32, "picked%d" % b, after) for b, after in enumerate([None, None])]

        def columns_of_h(i, first, width, bank, order, empty):
            acc = psum.tile([P, width], F32, name="acc", tag="bank%d" % bank)
            c, inside = divmod(first, BANK)
            for a in order:
                nc.tensor.matmul_mx(
                    out=acc[:],
                    lhsT=w1_c[i][a].bitcast(FP4X4),
                    lhsT_scale=w1_sc[i][a],
                    rhs=v_w[a, c][:, inside : inside + width].bitcast(FP8X4),
                    rhs_scale=v_sc[:, S * a + first : S * a + first + width],
                    start=(a == order[0]),
                    stop=(a == order[-1]),
                )
            empty(h[i][:, first : first + width], acc[:])

        def empty_on_scalar(dest, acc):
            nc.scalar.copy(dest, acc)

        def first_product(i):
            if i == 0:
                columns_of_h(i, 0, BANK, 0, [0, 1], nc.vector.tensor_copy)
                columns_of_h(i, BANK, HALF, 1, [0, 1], empty_on_scalar)
                columns_of_h(i, BANK + HALF, HALF, TILES - 1, [0, 1], nc.vector.tensor_copy)
            else:
                for c in range(2):
                    columns_of_h(i, BANK * c, BANK, (2 * i + c) % TILES, [1, 0], empty_on_scalar)

        def pick_upstream(i):
            b, t = divmod(i, SLOTS)
            nc.vector.tensor_copy(picked[b][:, t, :], h[i][:].indirect(pos1_sb[:]))

        down = {}

        def pick_downstream(i, after):
            down[i] = tile([P, M], F32, "down%d" % i, after)
            nc.vector.tensor_copy(down[i][:], h[i][:].indirect(pos2_sb[:]))

        x_bf = [tile([P, M * SLOTS], BF16, "x_bf%d" % b) for b in range(PASSES)]

        def make_x(b, first, width, after):
            bounded = tile([P, width * SLOTS], F32, "bounded%d_%d" % (b, first), after)
            nc.scalar.activation(
                bounded[:].rearrange("p (g i t) -> p g t i", i=4, t=SLOTS),
                picked[b][:, :, first : first + width].rearrange("p t (g i) -> p g t i", i=4),
                ACT.Tanh,
            )
            nc.gpsimd.tensor_tensor(
                x_bf[b][:, SLOTS * first : SLOTS * (first + width)].rearrange("p (r e) -> p r e", e=REP),
                bounded[:].rearrange("p (r e) -> p r e", e=REP),
                gain_rep[:, b, :].unsqueeze(1).to_broadcast([P, width * SLOTS // REP, REP]),
                ALU.mult,
            )

        both = tile([P, 2 * M * 2], BF16, "both")
        pairs = [both[:, 2 * M * u : 2 * M * (u + 1)].rearrange("p (m e) -> p m e", e=2) for u in range(2)]

        bounded_rows = {}

        def bound_rows(i, after):
            bounded_rows[i] = tile([P, M], F32, "bounded_t%d" % i, after)
            nc.scalar.activation(bounded_rows[i][:], picked[1][:, i - SLOTS, :], ACT.Tanh)

        def scale_rows(i):
            b, t = divmod(i, SLOTS)
            nc.scalar.activation(
                pairs[t // 2][:, :, t % 2], bounded_rows[i][:], ACT.Copy, scale=gain_rep[:, b, t : t + 1]
            )

        for i in range(TILES):
            first_product(i)
            pick_upstream(i)
            if i >= SLOTS and i != 6:
                pick_downstream(i, None)
            if i == 5:
                make_x(0, 0, HALF, "w1_sc10")
        make_x(0, HALF, HALF, "v_w01")
        for i, after in zip(range(SLOTS, TILES - 1), ["v_w11", "v_sc", "v_w00"]):
            bound_rows(i, after)
            if i > SLOTS:
                scale_rows(i - 1)
        scale_rows(TILES - 2)
        bound_rows(TILES - 1, None)
        scale_rows(TILES - 1)
        pick_downstream(6, "v_w11")
        pick_downstream(3, "w1_sc10")
        nc.scalar.copy(
            out=x_bf[1][:].bitcast(F32).rearrange("p (m u) -> p m u", u=2),
            in_=both[:].bitcast(F32).rearrange("p (u m) -> p m u", u=2),
        )
        last_bf.append(tile([P, 2 * BANK], BF16, "last_bf1", "both"))
        nc.scalar.copy(
            out=last_bf[1][:].rearrange("p (s m t) -> p m t s", s=2, t=SLOTS),
            in_=last_in.rearrange("p t (m s) -> p m t s", s=SLOTS)[:, :, :, 2:4],
        )

        operand = {}

        def quantise(key, place):
            codes, scales = place[:, : 4 * BANK], place[:, 4 * BANK :]
            operand[key] = (codes, scales)
            source = x_bf[key[1]] if key[0] == "x" else w2_bf[key[1:]]
            nc.vector.quantize_mx(out=codes.bitcast(FP8X4), scales=scales, in_=source[:])

        late = tile([P, 6 * 5 * BANK], U8, "late", "v_w01")
        keys = [("w2", 0, 1), ("x", 0), ("w2", 1, 1), ("x", 1), ("w2", 0, 0)]
        for n, key in enumerate(keys):
            quantise(key, late[:, 5 * BANK * n : 5 * BANK * (n + 1)])
        last_codes, last_scales = late[:, 25 * BANK : 29 * BANK], late[:, 29 * BANK :]
        operand["w2", 1, 0] = (last_codes, last_scales)

        def quantise_last(u):
            nc.vector.quantize_mx(
                out=last_codes[:, 4 * HALF * u : 4 * HALF * (u + 1)].bitcast(FP8X4),
                scales=last_scales[:, HALF * u : HALF * (u + 1)],
                in_=last_bf[u][:],
            )

        quantise_last(0)

        turn = [4, 5, 6, 7, 3, 0, 1, 2]
        y = {}

        def second_product(n):
            i = turn[n]
            b, t = divmod(i, SLOTS)
            y[i] = psum.tile([P, M], F32, name="y%d" % i, tag="bank%d" % n)
            order = list(range(PASSES) if n < 2 else reversed(range(PASSES)))
            for a in order:
                codes, scales = operand["w2", a, b]
                nc.tensor.matmul_mx(
                    out=y[i][:],
                    lhsT=codes[:, 4 * P * t : 4 * P * (t + 1)].bitcast(FP8X4),
                    lhsT_scale=scales[:, P * t : P * (t + 1)],
                    rhs=operand["x", a][0].bitcast(FP8X4),
                    rhs_scale=operand["x", a][1],
                    start=(a == order[0]),
                    stop=(a == order[-1]),
                )

        for n in range(SLOTS):
            second_product(n)

        out_rows = out.rearrange("(b p t) m -> b t p m", b=PASSES, t=SLOTS)
        halves = [slice(0, HALF), slice(HALF, M)]
        pieces = (
            [(turn[0], cols) for cols in halves]
            + [(i, slice(0, M)) for i in turn[1:-1]]
            + [(turn[-1], cols) for cols in halves]
        )
        rates = []

        def finish(n):
            i, cols = pieces[n]
            b, t = divmod(i, SLOTS)
            width = cols.stop - cols.start
            step_col = step_sb[:, b, t : t + 1]
            if n < ON_GPSIMD:
                res = behind[:, 3, cols] if n < 2 else tile([P, width], F32, "res%d" % n)
                nc.gpsimd.tensor_tensor(res[:, :], rates[n][:], down[i][:, cols], ALU.add)
            else:
                first = M * (min(n, TILES) - ON_GPSIMD)
                res = held[:, first + cols.start : first + cols.stop]
                nc.vector.scalar_tensor_tensor(res[:, :], rates[n][:], step_col, down[i][:, cols], ALU.mult, ALU.add)
            nc.sync.dma_start(out=out_rows[b, t][:, cols], in_=res[:, :])

        def add_and_bound(n):
            i, cols = pieces[n]
            width = cols.stop - cols.start
            if 2 <= n < 5:
                moved = behind[:, n - 2, :]
            else:
                moved = tile([P, width], F32, "moved%d" % n)[:]
            nc.vector.tensor_tensor(moved, y[i][:, cols], down[i][:, cols], ALU.add)
            rate = tile([P, width], F32, "rate%d" % n)
            nc.scalar.activation(rate[:], moved, ACT.Tanh)
            if n < ON_GPSIMD:
                b, t = divmod(i, SLOTS)
                scaled = tile([P, width], F32, "scaled%d" % n)
                nc.scalar.activation(scaled[:], rate[:], ACT.Copy, scale=step_sb[:, b, t : t + 1])
                rate = scaled
            rates.append(rate)

        for n in range(2):
            add_and_bound(n)
        quantise_last(1)
        behind = tile([P, 4, M], F32, "behind", "both")
        for later in range(SLOTS, TILES):
            second_product(later)
        for n in range(len(pieces)):
            if n >= 2:
                add_and_bound(n)
            if n == ON_GPSIMD - 1:
                for i in range(3):
                    pick_downstream(i, "rate%d" % (i + 1))
            if n < ON_GPSIMD:
                finish(n)
        held = tile([P, M * (TILES + 1 - ON_GPSIMD)], F32, "held", "scaled%d" % (ON_GPSIMD - 1))
        for n in range(ON_GPSIMD, len(pieces)):
            finish(n)
